import numpy as np, ml_dtypes
CORES = [23,119,17,113]
N = 4
BF = ml_dtypes.bfloat16
L, W, E, D, RO, EPS = 256, 4096, 4096, 512, 4, 6
def pack(S, EF, OT, Q, K, P, G, M):
    bf = lambda a: np.ascontiguousarray(a.reshape(N, 128, -1)).astype(np.float32).astype(BF)
    li = lambda a: np.ascontiguousarray(a.transpose(0, 1, 3, 2, 4)).reshape(N, 128, 3 * L).astype(np.int32)
    return {"st0": bf(S), "ef": bf(EF), "ot": bf(OT), "qn": li(Q), "qk": li(K), "tu": np.ascontiguousarray(P.reshape(N, 8, 3 * L)).astype(np.int32), "gl": bf(G), "rm": bf(M)}
def with15(v, last):
    return np.concatenate([v, np.broadcast_to(last, v.shape[:2] + (1, v.shape[3]))], axis=2).astype(np.int64)
def base(rng):
    cen = rng.integers(8, 56, (N, 8, 15, 1))
    def near(n):
        return np.clip(np.rint(cen + rng.standard_normal((N, 8, 15, n), dtype=np.float32) * rng.choice(np.array([1.5, 3.0, 6.0, 16.0]), (N, 8, 1, n))), 0, 63)
    S = with15(near(W), rng.random((N, 8, 1, W)) < rng.choice(np.array([0.1, 0.3, 0.5, 0.85]), (N, 8, 1, 1))); S[:, :, 15, W - 1] = 1
    EF = with15(np.rint((2 * rng.random((N, 8, 15, E)) - 1) * rng.integers(1, 9, (N, 8, 1, E))), 0)
    OT = rng.integers(0, 256, (N, 8, 16, D)); Q = rng.integers(0, W, (N, 8, 3, 16, L)); K = rng.integers(0, 946, (N, 8, 3, 16, L))
    kind = rng.integers(0, 3, (N, 8, 1, 1, L)); K = np.where(kind == 1, np.maximum(K, 300), np.where(kind == 2, K - K % 64, K))
    P = rng.integers(-3, 4, (N, 8, 3, L)); G = with15(near(L), 0); M = with15(rng.random((N, 8, 15, 1)) < 0.5, 0)
    for q in range(N):
        for g in range(8):
            Q[q, g, :, :, 5::16] = rng.choice(np.flatnonzero(S[q, g, 15]), (3, 16, L // 16))
    return S, EF, OT, Q, K, P, G, M
def setup_inputs(rng):
    return pack(*base(rng))
def setup_inputs_spread(rng):
    def un(hi, shape, eshape):
        return np.minimum(((hi + 1) * rng.random(shape) ** np.exp2(rng.integers(-2, 4, eshape))).astype(np.int64), hi)
    S = with15(un(63, (N, 8, 15, W), (N, 8, 1, W)), rng.random((N, 8, 1, W)) < rng.random((N, 8, 1, 1)))
    EF = with15(un(8, (N, 8, 15, E), (N, 8, 1, E)) * (2 * rng.integers(0, 2, (N, 8, 15, E)) - 1), 0)
    OT = un(255, (N, 8, 16, D), (N, 8, 1, D)); Q = un(W - 1, (N, 8, 3, 16, L), (N, 8, 3, 1, L)); K = un(945, (N, 8, 3, 16, L), (N, 8, 3, 1, L))
    P = rng.integers(-6, 7, (N, 8, 3, L)); G = with15(un(63, (N, 8, 15, L), (N, 8, 1, L)), 0)
    M = with15(rng.random((N, 8, 15, 1)) < rng.random((N, 8, 1, 1)), 0)
    return pack(S, EF, OT, Q, K, P, G, M)
def setup_inputs_ends(rng):
    def bits(n):
        r = rng.integers(0, 4, (N, 8, 1, n))
        return np.where(r == 0, 0, np.where(r == 1, 1, rng.integers(0, 2, (N, 8, 15, n))))
    S = with15(63 * bits(W), rng.integers(0, 2, (N, 8, 1, W))); EF = with15(16 * bits(E) - 8, 0); G = with15(63 * bits(L), 0)
    OT = 255 * rng.integers(0, 2, (N, 8, 16, D)); K = 945 * rng.integers(0, 2, (N, 8, 3, 16, L)); P = 12 * rng.integers(0, 2, (N, 8, 3, L)) - 6
    Q = np.where(rng.random((N, 8, 3, 16, L)) < 0.8, (W - 1) * rng.integers(0, 2, (N, 8, 3, 16, L)), rng.integers(0, W, (N, 8, 3, 16, L)))
    M = with15(rng.integers(0, 2, (N, 8, 15, 1)), 0)
    q, g = N - 1, 7
    S[q, g, :15, W - 1] = 63; S[q, g, :15, 0] = 0; S[q, g, 15, W - 1] = 0; S[q, g, 15, 0] = 0; EF[q, g, :15, E - 1] = 8; EF[q, g, :15, 0] = -8
    Q[q, g, :, :, L - 4:] = 0; Q[q, g, :, 15, L - 1] = W - 1; Q[q, g, :, 14, L - 2] = W - 1
    K[q, g, :, :, L - 2:] = 945; K[q, g, :, 15, L - 1] = 0; K[q, g, :, 14:, L - 2] = 0; K[q, g, :, :, L - 3] = 0; K[q, g, :, :, L - 4] = 945
    G[q, g, :15, L - 1] = 0; G[q, g, :15, L - 2] = 63; G[q, g, :15, L - 3] = 0; G[q, g, :15, L - 4] = 63
    P[q, g, :, L - 4:] = -6; P[q, g, 0, L - 2] = 6
    M[q, g, :15, 0] = 1; OT[q, g, :, 15120 % D] = 255
    return pack(S, EF, OT, Q, K, P, G, M)
def setup_inputs_corners(rng):
    S, EF, OT, Q, K, P, G, M = base(rng); i = np.arange(L); n8 = L // 8
    EF[:, 1::2] = np.take_along_axis(EF[:, 1::2], rng.integers(0, 4, (N, 4, 1, E)), 3)
    for q in range(N):
        for g in range(8):
            mode = (q + g) % 4; B = Q[q, g]; C = K[q, g]; c = (0, W - 1, L, int(rng.integers(0, W)))[int(rng.integers(0, 4))]
            S[q, g, 15] = 0 if mode == 0 else 1 if mode < 3 else (rng.random(W) < 0.5)
            B[:, :, 0::8] = rng.integers(0, W, (3, 1, n8)); B[:, :, 1::8] = L * rng.integers(0, 2 * RO, (3, 16, n8)) + i[1::8]
            B[:, :, 2::8] = (W - 1) * rng.integers(0, 2, (3, 16, n8)); B[:, :, 6::8] = L * rng.integers(0, 2 * RO, (3, 16, n8)) + i[6::8] + 1
            C[:, :, 3::8] = C[:, :1, 3::8].copy(); C[:, :, 4::8] = 945 * rng.integers(0, 2, (3, 16, n8)); C[:, :15, 5::8] = 945
            if mode == 2:
                S[q, g, 15, c] = 0; sl = rng.choice(np.array([0, 7, 15]), (3, L)); o = i[rng.random(L) < 0.5]
                for l in range(3): B[l, sl[l, o], o] = c
            m = (g // 2 + q) % 4
            if m < 3: M[q, g, :15, 0] = 0 if m != 1 else 1
            if m == 2: M[q, g, int(rng.integers(0, 15)), 0] = 1
            P[q, g, :, 0::4] = P[q, g, :1, 0::4].copy(); P[q, g, :, 1::4] = 12 * rng.integers(0, 2, (3, L // 4)) - 6; P[q, g, 2, 2::4] = P[q, g, 1, 2::4]
            G[q, g, :15, 3::8] = S[q, g][:15, B[0, 0, 3::8]]
    return pack(S, EF, OT, Q, K, P, G, M)
def setup_inputs_crowd(rng):
    S, EF, OT, Q, K, P, G, M = base(rng); i = np.arange(L); first = int(rng.integers(0, 8)); flip = int(rng.integers(0, 2))
    o = [int(g) for g in rng.permutation(8) if g not in (first, 7 - first)]
    for m, g in enumerate((first, o[0], 7 - first, o[1], o[2], o[3])):
        if m > 3: c = int(rng.integers(L, W - 2))
        elif m // 2 == flip: c = int(rng.integers(L, RO * L - 2))
        else: c = int(rng.integers(2 * RO * L, W - 2))
        z = L - 1 if m == 1 else int(rng.integers(0, L))
        S[:, g, 15, c:c + 3] = 0; P[:, g, 0] = -6; P[:, g, 1:] = 6
        if m < 4:
            EF[:, g, :15] = rng.integers(1, 9, (N, 15, E)); G[:, g, :15] = 63
            if m < 2: Q[:, g, 0] = c
            else:
                sl = rng.integers(0, 16, L); K[:, g, 0] = 945; K[:, g, 0, sl, i] = 0; Q[:, g, 0, sl, i] = c
            if m % 2 == 1:
                Q[:, g, 0, :, z] = c + 1; G[:, g, :15, z] = 0
        else:
            Q[:, g, 0] = c + rng.integers(0, 3, (N, 16, L))
            if m == 5:
                EF[:, g, :15] = rng.integers(1, 9, (N, 15, E)); G[:, g, :15] = 0; P[:, g, 0, ::2] = 6
    return pack(S, EF, OT, Q, K, P, G, M)
def check_inputs(d):
    bad = []
    for k, lo, hi in (("st0", 0, 63), ("ef", -8, 8), ("ot", 0, 255), ("qn", 0, W - 1), ("qk", 0, 945), ("tu", -6, 6), ("gl", 0, 63), ("rm", 0, 1)):
        v = np.asarray(d[k]).astype(np.float64)
        if not (np.min(v) >= lo and np.max(v) <= hi): bad.append("range of " + k)
        elif np.any(v != np.rint(v)): bad.append("whole numbers in " + k)
    for k in ("st0", "ef", "gl", "rm"):
        v = np.asarray(d[k]).astype(np.float64).reshape(N, 8, 16, -1)[:, :, 15]
        if not (np.min(v) >= 0 and np.max(v) <= (1 if k == "st0" else 0)): bad.append("last row of the groups in " + k)
    return bad
def ints(a):
    return a.astype(np.float32).astype(np.int32)
def reference(st0, ef, ot, qn, qk, tu, gl, rm):
    S = ints(st0).reshape(N, 8, 16, W); EF = ints(ef).reshape(N, 8, 16, E)[:, :, :15]; OT = ints(ot).reshape(N, 8, 16, D); M = ints(rm).reshape(N, 8, 16, 1, 1)[:, :, :15]
    Q = np.ascontiguousarray(ints(qn).reshape(N, 8, 16, 3, L).transpose(0, 1, 3, 2, 4)); K = np.ascontiguousarray(ints(qk).reshape(N, 8, 16, 3, L).transpose(0, 1, 3, 2, 4))
    P = ints(tu).reshape(N, 8, 3, L); G = ints(gl).reshape(N, 8, 16, 1, L)[:, :, :15]; A = np.zeros((N, 8, 1, 1), np.int64)
    cf = (2 * np.arange(15) + 1)[:, None]; kk = np.arange(16)[:, None]; lane = np.arange(L)
    def hs(y, g):
        dd = np.abs(y - g)
        return np.stack([np.add.reduce(dd, axis=2), 16 * np.add.reduce((dd > EPS).astype(np.int32), axis=2), np.add.reduce(dd * M, axis=2)], axis=2)
    for t in range(RO):
        if t > 0:
            Q, K, P, G = (np.roll(a, 1, axis=0) for a in (Q, K, P, G))
        j = np.argmin(P, axis=2); jj = j[:, :, None, None, :]
        q = np.take_along_axis(Q, jj, 2)[:, :, 0]; key = np.take_along_axis(K, jj, 2)[:, :, 0]
        s = np.take_along_axis(S, q.reshape(N, 8, 1, 16 * L), 3).reshape(N, 8, 16, 16, L)
        key = np.where(s[:, :, 15] == 1, 1023, key)
        k0 = np.argmin(key, axis=2)
        x = np.take_along_axis(s, k0[:, :, None, None, :], 3)[:, :, :15, 0]; xn = np.take_along_axis(q, k0[:, :, None], 2)[:, :, 0]
        u = np.add.reduce(cf * x, axis=2); v = np.add.reduce(np.maximum.reduce(s[:, :, :15], axis=3), axis=2)
        o = np.take_along_axis(OT, ((u + v) & (D - 1))[:, :, None, :], 3)
        n = (((o * u[:, :, None]) >> 5) + o + 37 * kk + A) & (E - 1)
        e = np.take_along_axis(EF, n.reshape(N, 8, 1, 16 * L), 3).reshape(N, 8, 15, 16, L)
        y = np.clip(x[:, :, :, None] + e, 0, 63)
        h = hs(y, G); hx = hs(x[:, :, :, None], G)[:, :, :, 0]
        ha = np.take_along_axis(h, jj, 2)[:, :, 0]; hb = np.take_along_axis(h, (jj + 1) % 3, 2)[:, :, 0]
        a = np.argmin(ha, axis=2); b = np.argmin(hb, axis=2)
        ya = np.take_along_axis(y, a[:, :, None, None, :], 3)[:, :, :, 0]; yb = np.take_along_axis(y, b[:, :, None, None, :], 3)[:, :, :, 0]
        np.put_along_axis(S[:, :, 15], xn, 1, 2)
        S[:, :, :15, t * L:(t + 1) * L] = ya; S[:, :, 15, t * L:(t + 1) * L] = 0
        S[:, :, :15, (RO + t) * L:(RO + t + 1) * L] = np.roll(yb, 1, axis=0); S[:, :, 15, (RO + t) * L:(RO + t + 1) * L] = 0
        np.put_along_axis(K, jj, key[:, :, None], 2)
        w = np.argmax(K, axis=3)[:, :, :, None]
        np.put_along_axis(Q, w, t * L + lane, 3); np.put_along_axis(K, w, hx[:, :, :, None], 3)
        go = (np.min(ha, axis=2) < np.take_along_axis(hx, j[:, :, None], 2)[:, :, 0]).astype(np.int32)
        np.put_along_axis(P, j[:, :, None], np.take_along_axis(P, j[:, :, None], 2) + 1 - 3 * go[:, :, None], 2)
        A = (np.add.reduce(go, axis=2) & 63)[:, :, None, None]
    yq = np.ascontiguousarray((4096 * K + Q).transpose(0, 1, 3, 2, 4)).reshape(N, 128, 3 * L)
    return {"ys": np.ascontiguousarray(S[..., :2 * RO * L]).reshape(N, 128, 2 * RO * L).astype(np.float32).astype(BF), "ym": np.ascontiguousarray(S[:, :, 15, 2 * RO * L:]).astype(np.float32).astype(BF),
            "yq": yq.astype(np.float32), "yp": P.reshape(N, 8, 3 * L).astype(np.float32)}

@@ -1,0 +1,800 @@
+from concourse.bass import DstId, RemoteDMATransfer
+from concourse.mybir import AluOpType, AxisListType, ActivationFunctionType
+
+N, RO = 4, 4
+ALU = AluOpType
+AF = ActivationFunctionType
+F32, BF, I32, U16 = "float32", "bfloat16", "int32", "uint16"
+VW = 896
+PB, PM, EB, ED = 768, 816, 864, 880
+RC = 1.5 * 2.0 ** 35
+BIG = 2.0 ** 23
+
+SB = {
+    "S": (4128, BF), "EF": (4736, BF), "OT": (512, BF), "qni": (768, I32), "qki": (768, I32), "tui": (768, I32),
+    "tub": (768, BF), "gli": (256, BF), "rmb": (8, BF), "rmf": (4, F32),
+    "s": (4096, BF), "sm": (4096, BF), "e": (4096, BF), "y": (4096, BF), "xs": (4096, BF), "xb": (4096, BF),
+    "D2": (VW, F32), "D": (768, F32), "KR": (768, F32), "KT": (768, F32), "KM": (1024, F32), "VO": (768, F32),
+    "Ve": (256, F32), "E": (256, F32), "Ne": (256, F32), "Z": (256, F32), "ZT": (256, F32), "ZM": (256, F32),
+    "q16": (256, U16), "n16": (256, U16), "pn": (256, I32), "pn2": (256, I32), "ub": (256, F32),
+    "x": (256, BF), "xm": (256, BF), "xT": (256, BF), "HS": (768, BF), "MN": (256, F32),
+    "XT": (512, F32), "EQ": (512, BF), "EM": (512, BF), "RM": (768, F32),
+    "elf": (16, F32), "elt": (16, F32), "elu": (16, U16), "jv": (16, F32), "m1": (48, F32),
+    "Pc": (48, F32), "Pt": (48, F32), "mn": (16, F32), "mni": (16, I32), "mnj": (16, I32),
+    "k0i": (16, I32), "k0j": (16, I32), "k0b": (16, BF), "lx": (16, U16), "lk": (16, U16),
+    "opi": (16, I32), "opj": (16, I32), "lo": (16, U16), "wi": (64, I32), "wj": (64, I32), "wb": (64, BF), "w1": (48, F32), "w2": (48, F32), "lw": (48, U16),
+    "TT": (96, F32), "T2": (32, F32), "ri": (32, I32), "rj": (32, I32), "la": (16, U16), "lb": (16, U16),
+    "hx3": (48, F32), "hx2": (16, F32), "hx1": (16, F32), "o1": (16, F32), "o2": (16, F32), "o3": (16, F32), "lm": (16, U16),
+    "gs": (4, F32), "gsb": (8, BF), "Ai": (4, I32), "Aj": (4, I32), "ncol": (4, F32), "Pb": (48, BF), "yo": (768, F32),
+    "pi": (4, I32), "ci": (32, I32), "cf": (32, F32), "J160": (160, BF), "Jg": (128, BF), "J32": (128, BF), "Jc": (256, BF),
+    "Jb": (128, F32), "Jl": (48, F32), "KI2": (128, BF), "c16": (8, BF), "iL": (16, F32), "PC": (48, F32),
+    "NIf": (128, F32), "l8a": (8, U16), "l8b": (8, U16), "LT": (128, BF), "RT": (384, BF), "WD": (16, BF), "penT": (96, F32), "goT": (16, F32),
+    "gmj": (256, F32), "gmb": (256, F32), "gmg": (256, F32), "gma": (256, F32), "df": (4096, BF), "tf": (4096, BF),
+    "l8": (8, U16), "Ma": (128, F32), "Rb": (8, F32), "gm": (256, F32), "L3": (128, BF), "R3": (128, BF), "R3a": (128, BF), "CR": (128, BF), "C128": (128, BF),
+    "W": (160, BF), "W0": (160, BF), "W1": (160, BF), "W0f": (160, F32), "W1f": (160, F32), "Inz": (128, BF),
+    "Fone": (160, BF), "Fcf": (160, BF), "F4": (160, BF), "F8": (160, BF), "Frm": (160, BF), "Fmk": (160, BF), "G8": (160, BF),
+    "B4": (128, BF), "Bcf": (128, BF), "B1": (128, BF), "H0": (128, F32), "H1": (128, F32), "Tri": (256, BF), "Tm": (16, F32),
+    "R": (2048, BF), "k16": (1024, BF), "d32": (512, BF), "dmin": (128, BF), "dmax": (256, BF), "dres": (384, BF),
+}
+SCRATCH, PLACE, _fill = {}, {}, {}
+for _k, (_w, _d) in SB.items():
+    if _w <= 160 and _k not in ("rmb", "gs"):
+        PLACE[_k] = ("pool_" + _d, _fill.get(_d, 0), _w)
+        _fill[_d] = _fill.get(_d, 0) + (_w + 15) // 16 * 16
+    else:
+        SCRATCH[_k] = ("sbuf", [128, _w], _d)
+for _d, _w in _fill.items():
+    SCRATCH["pool_" + _d] = ("sbuf", [128, _w], _d)
+SCRATCH["pen"] = ("sbuf", [128, 4, 16], F32)
+SCRATCH["d"] = ("sbuf", [128, 16, 16, 16], BF)
+SCRATCH["tt"] = ("sbuf", [128, 16, 16, 16], BF)
+for _t in range(RO):
+    SCRATCH["V%d" % _t] = ("sbuf", [128, VW], F32)
+    SCRATCH["GT%d" % _t] = ("sbuf", [128, 256], BF)
+    SCRATCH["SY%d" % _t] = ("sbuf", [128, 272], BF)
+    SCRATCH["LY%d" % _t] = ("sbuf", [128, 272], BF)
+for _b in range(8):
+    SCRATCH["ps%d" % _b] = ("psum", [128, 512], F32)
+DMAS = ["dS0", "dS1", "dE0", "dE1", "dE2", "dOT", "dqn", "dqk", "dtu", "dgl", "drm", "oq0", "oq1", "op", "os0", "os1", "os2", "om"]
+SEMAPHORES = (["cV", "cA", "cP", "cG"] + DMAS + ["lg", "ag1", "ag2", "ag3"]
+              + ["%s%d" % (k, t) for k in ("lv", "av") for t in range(1, RO)]
+              + ["%s%d_%d" % (k, t, c) for k in ("ly", "ay") for t in range(RO) for c in range(2)])
+
+CY, PCY, GC, SC = 1.0, 0.5, 1.5, 3.5
+XLAT, SLAT = 120.0, 70.0
+OPT = {"s": "AAVAAAAA", "eq": "A" * 16, "e": "AAAAAAAA", "ly": "V", "ve": "AA", "x": "AA", "ya": "AA", "t": "VVAA", "kr": "AAA", "en": "AV", "h": "T", "d": "VVV", "gj": "VV", "qat": 4, "mat": 7, "yb": "AA",
+       "tries": 2500, "seed": 0, "noise": 8000.0, "window": 15000.0}
+
+
+def build(g, core, T, topo):
+    rank = T.rank_of(core)
+    ops = []
+    hist = {}
+    steps = {}
+    seen = {}
+    now = [-1]
+    Q = {"V": g.vector, "A": g.scalar, "P": g.tensor, "G": g, "S": g.sync}
+
+    def ap(name, lo=0, hi=None, step=1, p=None):
+        if name in PLACE:
+            name, at, w = PLACE[name]
+            lo, hi = at + lo, at + (w if hi is None else hi)
+        t = T[name]
+        if hi is None:
+            hi = t.shape[1]
+        r = t[:, lo:hi:step] if p is None else t[p[0]:p[1], lo:hi:step]
+        steps[(name, lo, hi, len(range(lo, hi, step)))] = step
+        return (name, lo, hi, r, len(range(lo, hi, step)), SCRATCH[name][2])
+
+    def ap4(name, b0, b1, a=None):
+        t = T[name]
+        r = t[:, b0:b1, :, :] if a is None else t[:, b0:b1, a, :]
+        return (name, 256 * b0, 256 * b1, r, (b1 - b0) * (256 if a is None else 16), BF)
+
+    def pen(l0, c=None, n=3):
+        t = T["pen"]
+        r = t[:, l0:l0 + n, :] if c is None else t[:, l0:l0 + n, 8 * c:8 * c + 8]
+        return ("pen", 16 * l0, 16 * (l0 + n), r, n * (16 if c is None else 8), F32)
+
+    def ind(win, off):
+        return (win[0], win[1], win[2], win[3].indirect(off[3]), 16 * off[4], win[5], off)
+
+    def val(s):
+        return s[3] if isinstance(s, tuple) else s
+
+    def stp(a):
+        return steps.get((a[0], a[1], a[2], a[4]), 1) if len(a) == 6 else 1
+
+    def add(eng, fns, cost, reads, writes, kind="c", sem=None, cnt=0, lat=0.0, after=(), goes_on=False):
+        i = len(ops)
+        rd, wr = [], []
+        for lst, a in [(rd, a) for a in reads] + [(wr, a) for a in writes]:
+            if isinstance(a, tuple):
+                lst.append(a)
+                if len(a) > 6:
+                    rd.append(a[6])
+        deps = {j: False for j in after}
+        ops.append({"eng": eng, "fns": fns, "cost": cost, "deps": deps, "kind": kind, "sem": sem, "cnt": cnt, "lat": lat,
+                    "tag": wr[0][:2] if wr else ("", 0)})
+        nm = wr[0][0] if wr else ""
+        nm = (eng, kind, nm[:2] if nm[:2] in ("SY", "LY", "ps") else "V" if nm[:1] == "V" and nm[1:].isdigit() else nm)
+        seen[(now[0], nm)] = seen.get((now[0], nm), 0) + 1
+        ops[i]["cls"] = (now[0], nm, seen[(now[0], nm)])
+        for isw, a in [(False, a) for a in rd] + [(True, a) for a in wr]:
+            psum = a[0].startswith("ps")
+            st = stp(a)
+            for (lo, hi, j, w, s2) in hist.get(a[0], []):
+                o = ops[j]
+                same = o["eng"] == eng and o["kind"] == "c" and kind == "c"
+                over = lo < a[2] and a[1] < hi and not (st == s2 and st > 1 and (lo - a[1]) % st)
+                if psum:
+                    need = (not same) or (over and (w or isw) and not goes_on)
+                    deps[j] = deps.get(j, False) or need
+                elif over and (w or isw):
+                    deps[j] = True
+        for isw, a in [(False, a) for a in rd] + [(True, a) for a in wr]:
+            h = hist.setdefault(a[0], [])
+            if a[0].startswith("ps"):
+                if any(ops[r[2]]["eng"] != eng for r in h):
+                    h[:] = [r for r in h if r[2] == i]
+            elif isw and stp(a) == 1:
+                h[:] = [r for r in h if not (a[1] <= r[0] and r[1] <= a[2])]
+            h.append((a[1], a[2], i, isw, stp(a)))
+        deps.pop(i, None)
+        return i
+
+    def vcost(out, ins, two=False):
+        n = out[4]
+        if len(out) > 6:
+            return 50 + n * SC * CY
+        if len(ins[0]) > 6:
+            return 50 + n * GC * CY
+        if two:
+            f = 1.0 if any(a[0].startswith("ps") for a in ins) else 2.0
+        else:
+            f = 0.5 if all(a[5] in (BF, U16) for a in [out] + ins) else 1.0
+        return max(64, n * f) * CY
+
+    def ts(out, in0, s1, op0, s2=None, op1=None):
+        if op1 is None:
+            f = lambda: g.vector.tensor_scalar(out[3], in0[3], val(s1), None, op0)
+        else:
+            f = lambda: g.vector.tensor_scalar(out[3], in0[3], val(s1), val(s2), op0, op1)
+        return add("V", [f], vcost(out, [in0]), [in0, s1, s2], [out])
+
+    def tt(out, a, b, op):
+        return add("V", [lambda: g.vector.tensor_tensor(out[3], a[3], b[3], op)], vcost(out, [a, b], True), [a, b], [out])
+
+    def cp(out, a, eng="V"):
+        if eng == "A":
+            return act(out, a, AF.Identity)
+        return add("V", [lambda: g.vector.tensor_copy(out[3], a[3])], vcost(out, [a]), [a], [out])
+
+    def ms(out, c):
+        return add("V", [lambda: g.vector.memset(out[3], c)], vcost(out, [out]), [], [out])
+
+    def scan(out, d0, d1, op0, op1):
+        return add("V", [lambda: g.vector.tensor_tensor_scan(out[3], d0[3], d1[3], 0.0, op0, op1)], vcost(out, [d0, d1]), [d0, d1], [out])
+
+    def tr(out, a):
+        return add("V", [lambda: g.vector.transpose(out[3], a[3])], vcost(out, [a]), [a], [out])
+
+    def act(out, a, fn, bias=0.0, scale=1.0):
+        c = 65 + out[4] * GC * CY if len(a) > 6 else max(64, out[4]) * CY
+        return add("A", [lambda: g.scalar.activation(out[3], a[3], fn, bias=val(bias), scale=val(scale))], c, [a, bias, scale], [out])
+
+    def mm(items, last=True):
+        fns, cost, rd, wr = [], 0.0, [], []
+        for k, (o, l, r, st) in enumerate(items):
+            nxt = items[k + 1][3] if k + 1 < len(items) else last
+            fns.append(lambda o=o, l=l, r=r, st=st, sp=nxt: g.tensor.matmul(o[3], l[3], r[3], st, sp))
+            cost += max(min(64, l[4]), r[4]) * (4 if r[5] == F32 else 1) * PCY
+            rd += [l, r]
+            wr.append(o)
+        return add("P", fns, cost, rd, wr, goes_on=not items[0][3])
+
+    def grp(o, pairs, first=True):
+        return [(o, l, r, first and k == 0) for k, (l, r) in enumerate(pairs)]
+
+    def iota(out, pat, base, cm):
+        if out[5] == I32:
+            f = lambda: g.iota(out[3], pat, base, cm)
+        else:
+            f = lambda: g.iota(out[3], pat, base, cm, allow_small_or_imprecise_dtypes=True)
+        return add("G", [f], 130 + 2 * out[4] * CY, [], [out])
+
+    def dma(eng, sem, out, in_, reads, writes, lat, after=(), **kw):
+        return add(eng, [lambda: Q[eng].dma_start(out, in_, **kw)], 60.0, reads, writes, "d", sem, 16, lat, after)
+
+    def send(srcs, dsts, lsem, lat):
+        trs = []
+        for k, (dist, land, asem) in enumerate(dsts):
+            dst = T.cores[(rank + dist) % N]
+            en = topo.engines(core, dst)
+            per = len(en) if len(dsts) == 1 else 2
+            m = sum(1 << e for e in en[k * per:(k + 1) * per])
+            rid, pid = topo.addr(dst)[0], topo.addr(dst)[1]
+            kw = {"src": srcs[0][3]} if len(srcs) == 1 else {"srcs": [a[3] for a in srcs], "alu_op": 1}
+            trs.append((RemoteDMATransfer(dst_ids=[DstId(rid=rid, pnc=pid)], dma_engine_mask=m, remote_sem=T.sem[asem], dst=land[3], **kw), per))
+        i = add("G", [lambda: g.remote_dma_fused([a for a, b in trs], local_sem=T.sem[lsem])], 600.0, srcs, [], "s", lsem, sum(b for a, b in trs), lat)
+        for (dist, land, asem), (a, per) in zip(dsts, trs):
+            add(None, [], 0.0, [], [land], "r", asem, per, 0.0, [i])
+
+    ps = lambda b, lo=0, hi=512, step=1, p=None: ap("ps%d" % b, lo, hi, step, p)
+    col = lambda k: ap("cf", k, k + 1)
+    sl = lambda name, s: ap(name, 16 - s, 144 - s)
+
+    dma("S", "dtu", T["tui"][0:8, :], T.tu[:], [], [ap("tui")], 2200)
+    dma("A", "dqk", T["qki"][:], T.qk[:], [], [ap("qki")], 2500)
+    dma("S", "dqn", T["qni"][:], T.qn[:], [], [ap("qni")], 2500)
+    dma("A", "dS0", T["S"][:, 0:2048], T.st0[:, 0:2048], [], [ap("S", 0, 2048)], 5500)
+    dma("S", "dS1", T["S"][:, 2048:4096], T.st0[:, 2048:4096], [], [ap("S", 2048, 4096)], 5500)
+    dma("S", "dgl", T["gli"][:], T.gl[:], [], [ap("gli")], 5500)
+    dma("A", "drm", T["rmb"][:, 0:1], T.rm[:], [], [ap("rmb")], 5500)
+    dma("S", "dOT", T["OT"][:], T.ot[:], [], [ap("OT")], 6000)
+    dma("S", "dE0", T["EF"][:, 0:2048], T.ef[:, 0:2048], [], [ap("EF", 0, 2048)], 9000)
+    dma("S", "dE1", T["EF"][:, 2048:4096], T.ef[:, 2048:4096], [], [ap("EF", 2048, 4096)], 9000)
+    dma("S", "dE2", T["EF"][:, 4096:4736], T.ef[:, 0:640], [], [ap("EF", 4096, 4736)], 9500)
+
+    P_, K_, G16, P32, A32, NZ, CFC, NZ4, MK, HH0, HH1, R15, K16, K37, DC, P16, RM4, E0, N0, E1, N1, E1X, E2, E3X, M65, E2X = range(26)
+    iota(ap("pi", 0, 1), [[0, 1]], 0, 1)
+    iota(ap("J160"), [[1, 160]], -16, 0)
+    iota(ap("Jl"), [[256, 3], [16, 16]], 0, 0)
+    iota(ap("Jb"), [[256, 8], [0, 16]], 0, 0)
+    iota(ap("Jg"), [[16, 8], [0, 16]], 0, 0)
+    iota(ap("KI2"), [[0, 8], [1, 16]], 0, 0)
+    iota(ap("J32"), [[32, 4], [0, 32]], 0, 0)
+    iota(ap("Jc"), [[0, 8], [1, 32]], 0, 0)
+    cp(col(P_), ap("pi", 0, 1))
+    ts(ap("ci", 0, 1), ap("pi", 0, 1), 15, ALU.bitwise_and)
+    ts(ap("ci", 4, 5), ap("pi", 0, 1), 31, ALU.bitwise_and)
+    cp(col(K_), ap("ci", 0, 1))
+    cp(col(P32), ap("ci", 4, 5))
+    ts(col(G16), col(P_), col(K_), ALU.subtract)
+    ts(col(A32), col(P_), col(P32), ALU.subtract)
+    ts(col(NZ), col(K_), 15.0, ALU.is_lt)
+    ts(col(CFC), col(K_), 2.0, ALU.mult, 1.0, ALU.add)
+    ts(col(CFC), col(CFC), col(NZ), ALU.mult)
+    ts(col(NZ4), col(K_), 15.0, ALU.is_lt, 4096.0, ALU.mult)
+    ts(col(MK), col(K_), 15.0, ALU.is_equal, 2.0 ** 22, ALU.mult)
+    ts(col(HH0), col(P32), 16.0, ALU.is_lt)
+    ts(col(HH1), col(P32), 16.0, ALU.is_ge)
+    ts(col(R15), col(K_), 15.0, ALU.is_equal)
+    ts(col(K16), col(K_), 16.0, ALU.mult)
+    ts(col(K37), col(K_), 37.0, ALU.mult)
+    ts(col(DC), col(P32), 2048.5, ALU.add)
+    ts(col(P16), col(P_), 16.0, ALU.mult)
+    ts(col(E0), col(P_), 0.0, ALU.is_equal)
+    ts(col(N0), col(P_), 0.0, ALU.not_equal)
+    ts(col(E1), col(P_), 1.0, ALU.is_equal)
+    ts(col(N1), col(P_), 1.0, ALU.not_equal)
+    ts(col(E1X), col(P_), 1.0, ALU.is_equal, 16.0, ALU.mult)
+    ts(col(E2), col(P_), 2.0, ALU.is_equal)
+    cp(ap("rmf", 0, 1), ap("rmb", 0, 1))
+    ts(col(RM4), ap("rmf", 0, 1), 4096.0, ALU.mult)
+    J = ap("J160")
+    ts(ap("G8"), J, col(P16), ALU.is_equal)
+    for nm, c in (("Fmk", MK), ("Fone", NZ), ("Fcf", CFC), ("F4", NZ4), ("Frm", RM4)):
+        ts(ap(nm), J, col(G16), ALU.is_equal, col(c), ALU.mult)
+    ts(ap("W"), J, col(P_), ALU.is_equal)
+    for sfx in ("", "f"):
+        ts(ap("W0" + sfx), J, col(P_), ALU.is_equal, col(HH0), ALU.mult)
+        ts(ap("W1" + sfx), J, col(P_), ALU.is_equal, col(HH1), ALU.mult)
+    ts(ap("Inz"), ap("J160", 16, 144), col(P_), ALU.is_equal, col(NZ), ALU.mult)
+    ts(ap("B4"), ap("Jg"), col(G16), ALU.is_equal, col(NZ4), ALU.mult)
+    ts(ap("Bcf"), ap("Jg"), col(G16), ALU.is_equal, col(CFC), ALU.mult)
+    ts(ap("B1"), ap("Jg"), col(G16), ALU.is_equal)
+    ts(ap("H0"), ap("J32"), col(A32), ALU.is_equal, col(HH0), ALU.mult)
+    ts(ap("H1"), ap("J32"), col(A32), ALU.is_equal, col(HH1), ALU.mult)
+    ts(ap("Tri"), ap("Jc"), col(P32), ALU.is_ge, 16384.0, ALU.mult)
+    ts(ap("Tm"), ap("J160", 16, 32), col(K_), ALU.is_equal)
+    ts(ap("R3a"), ap("KI2"), col(E0), ALU.mult, col(E1), ALU.add)
+    if OPT["h"] != "T":
+        ts(col(E3X), col(P_), 3.0, ALU.is_equal, 120.0 * 4096, ALU.mult)
+        ts(ap("L3"), ap("KI2"), col(E1X), ALU.mult, col(N1), ALU.add)
+        ts(ap("R3"), ap("Jb"), col(E2), ALU.mult, col(E3X), ALU.add)
+        tt(ap("R3"), ap("R3"), ap("R3a"), ALU.add)
+    if "A" in OPT["t"]:
+        ts(ap("F8"), ap("F4"), 8.0, ALU.mult)
+        ms(col(M65), -6.5)
+    if "A" in OPT["d"]:
+        ts(ap("NIf"), ap("J160", 16, 144), col(P_), ALU.is_equal, -1.0, ALU.mult)
+    ts(ap("CR"), ap("J160", 16, 144), 0.5, ALU.add, 1.0 / 128, ALU.mult)
+    ts(ap("CR"), ap("CR"), col(E0), ALU.mult, col(N0), ALU.add)
+    ms(ap("C128"), 128.0)
+    ts(ap("c16"), ap("Jb", 0, 128, 16), col(K16), ALU.add)
+    ts(ap("iL"), ap("Jl", 0, 16), col(K_), ALU.add)
+    ts(ap("PC"), ap("Jl"), col(K_), ALU.add, 16384.0, ALU.add)
+    I_ = sl("W", 0)
+    for k in range(16):
+        cp(ap("R", k, 2048, 16), I_)
+    for nm, per, v0, v in (("k16", 16, 0.0, 1.0), ("d32", 32, 2 * BIG, 0.0), ("dmin", 16, 2 * BIG, -256.0), ("dmax", 16, -2 * BIG, 256.0), ("dres", 16, 2 * BIG, 0.0)):
+        ms(ap(nm), v)
+        ms(ap(nm, 0, None, per), v0)
+    ms(ap("D2", 768, VW), 0.0)
+    bank = [0]
+    for c in range(2):
+        if "V" in OPT["e"][4 * c:4 * c + 4]:
+            ms(ap("xs", 2048 * c, 2048 * c + 2048), 0.0)
+    cp(ap("ncol", 0, 1), col(K37))
+
+    def swap(bank, lo, n, src, f32, extra=None):
+        it = []
+        for c in range(2):
+            pr = [(sl("W%d%s" % (c, "f" if f32 else ""), 16 * (h - c)), src(h)) for h in range(2)]
+            if extra is not None:
+                pr.append((I_, extra(c)))
+            it += grp(ps(bank, lo + c, lo + 2 * n, 2), pr)
+        mm(it)
+
+    def turn(src, tmp, out, lst="l8"):
+        tt(tmp, ind(src, ap(lst)), ap("Ma"), ALU.mult)
+        mm(grp(out, [(tmp, ap("Rb"))]))
+
+    ts(ap("l8"), ap("Jb", 0, 128, 16), 1.0 / 256, ALU.mult)
+    if OPT["h"] == "T":
+        ts(ap("l8a"), ap("Jb", 0, 128, 16), 1.0 / 128, ALU.mult)
+        ts(ap("l8b"), ap("Jb", 0, 128, 16), 1.0 / 128, ALU.mult, 1.0, ALU.add)
+        ts(ap("LT"), ap("J160", 16, 144), col(E1X), ALU.mult, col(N1), ALU.add)
+        cp(ap("RT", 0, 128), ap("R3a"))
+        cp(ap("RT", 128, 256), ap("R3a"))
+        ts(col(E2X), col(E2), 120.0 * 4096, ALU.mult)
+        ts(ap("RT", 256, 384), ap("R3a"), col(E2X), ALU.add)
+        cp(ap("WD", 0, 8), ap("F4", 16, 144, 16))
+        cp(ap("WD", 8, 16), ap("Frm", 16, 144, 16))
+    ts(ap("Ma"), ap("KI2"), col(K_), ALU.is_equal)
+    ts(ap("Rb"), ap("Jg", 0, 128, 16), col(G16), ALU.is_equal)
+
+    for k in range(2):
+        ts(ps(2 + k, 0, 384), ap("qki", 384 * k, 384 * k + 384), 4096.0, ALU.mult, 2048.5, ALU.add)
+        tt(ap("V0", 384 * k, 384 * k + 384), ps(2 + k, 0, 384), ap("qni", 384 * k, 384 * k + 384), ALU.add)
+    cp(ap("tub", p=(0, 8)), ap("tui", p=(0, 8)))
+    mm(grp(ps(7, 0, 48), [(ap("G8", 16 - a, 144 - a, 1, (0, 8)), ap("tub", a, 768, 16, (0, 8))) for a in range(16)]))
+    ts(ap("Pt"), ps(7, 0, 48), 1024.0, ALU.mult)
+    tt(ap("Pc"), ap("Pt"), ap("PC"), ALU.add)
+
+    def least(src, dst):
+        tt(ap("mn"), src(0), src(1), ALU.min)
+        tt(ap("mni"), ap("mn"), src(2), ALU.min)
+        ts(ap("mnj"), ap("mni"), 1023, ALU.bitwise_and)
+        cp(dst, ap("mnj"))
+
+    least(lambda l: ap("Pc", 16 * l, 16 * l + 16), ap("elf"))
+    for c in range(2):
+        mm(grp(ps(c, 0, 128), [(ap("gli", 128 * c, 128 * c + 128), I_)]))
+        act(ap("GT0", 128 * c, 128 * c + 128), ps(c, 0, 128), AF.Identity, 0.0, -1.0)
+    send([ap("GT0")], [(k, ap("GT%d" % k), "ag%d" % k) for k in range(1, N)], "lg", 4000)
+
+    def counters(V, go):
+        for l in range(3):
+            tt(ap("Pt", 16 * l, 16 * l + 16), ap(V, PM + 16 * l, PM + 16 * l + 16), go, ALU.mult)
+        tt(ap("Pc"), ap("Pt"), ap(V, PB, PB + 48), ALU.add)
+
+    for t in range(RO):
+        V, GT, SY, LY = "V%d" % t, "GT%d" % t, "SY%d" % t, "LY%d" % t
+        now[0] = t
+        h8 = lambda name, c: ap(name, 8 * c, 8 * c + 8)
+        h128 = lambda name, c: ap(name, 128 * c, 128 * c + 128)
+        for l in range(3):
+            a3 = lambda name: ap(name, 256 * l, 256 * l + 256)
+            if OPT["kr"][l] == "A":
+                act(a3("KT"), a3(V), AF.Identity, RC)
+                act(a3("KR"), a3("KT"), AF.Identity, -RC)
+            else:
+                ts(a3("KR"), a3(V), RC, ALU.add, RC, ALU.subtract)
+            tr(a3("KT"), a3("KR"))
+            scan(a3("KM"), ap("dmax"), a3("KT"), ALU.add, ALU.max)
+        for c in range(2):
+            if t > 0:
+                tt(h8("elt", c), ap("LY%d" % (t - 1), 128 + 8 * c, 136 + 8 * c), ap(V, ED + 8 * c, ED + 8 * c + 8), ALU.mult)
+                tt(h8("elf", c), h8("elt", c), ap(V, EB + 8 * c, EB + 8 * c + 8), ALU.add)
+            cp(h8("elu", c), h8("elf", c))
+            cp(h128("Ve", c), ind(ap(V, 0, 768), h8("elu", c)), OPT["ve"][c])
+            if OPT["en"][c] == "A":
+                cp(h128("E", c), ind(ap("KR"), h8("elu", c)), "A")
+            else:
+                ts(h128("E", c), h128("Ve", c), RC, ALU.add, RC, ALU.subtract)
+            tt(h128("Ne", c), h128("Ve", c), h128("E", c), ALU.subtract)
+            ts(h128("q16", c), h128("Ne", c), 2047.5, ALU.add)
+        if t > 0:
+            counters(V, ap("LY%d" % (t - 1), 128, 144))
+        tt(ap("jv"), ap("elf"), ap("iL"), ALU.subtract)
+        for l in range(3):
+            ts(ap("m1", 16 * l, 16 * l + 16), ap("jv"), 256.0 * l, ALU.is_equal, 1024.0, ALU.mult)
+        tt(ap(V, PB, PB + 48), ap("Pc"), ap("m1"), ALU.add)
+        act(ap(V, PM, PM + 48), ap("m1"), AF.Identity, 0.0, -3.0)
+        act(pen(1), ap("m1"), AF.Identity, BIG, -BIG / 1024)
+        act(pen(0, None, 1), ap("m1", 32, 48), AF.Identity, BIG, -BIG / 1024)
+        if t < RO - 1:
+            least(lambda l: ap(V, PB + 16 * l, PB + 16 * l + 16), ap(V, EB, EB + 16))
+            tt(ap(V, ED, ED + 16), ap("elf"), ap(V, EB, EB + 16), ALU.subtract)
+        for k in range(8):
+            o = 512 * k
+            cp(ap("s", o, o + 512), ind(ap("S", 0, 4096), ap("q16", o // 16, o // 16 + 32)), OPT["s"][k])
+        for c in range(2):
+            mb = 5 + c
+            o = 2048 * c
+            for hf in range(2):
+                oo = o + 1024 * hf
+                mm(grp(ps(mb, 64 * hf, 64 * hf + 64), [(sl("Fmk", k), ap("s", oo + k, oo + 1024, 16)) for k in range(16)]))
+            tt(h128("Z", c), h128("E", c), ps(mb, 0, 128), ALU.max)
+            tr(h128("ZT", c), h128("Z", c))
+            scan(h128("ZM", c), ap("dmin"), h128("ZT", c), ALU.add, ALU.min)
+            ts(h8("k0i", c), ap("ZM", 128 * c + 15, 128 * c + 128, 16), 1.0 / 256, ALU.mult, 15.0, ALU.add)
+            ts(h8("k0j", c), h8("k0i", c), 15, ALU.bitwise_and)
+            cp(h8("k0b", c), h8("k0j", c))
+            swap(mb, 128, 4, lambda h: ap("k0b", 8 * c + h, 8 * c + 8, 2), False, lambda cc: ap("c16", cc, 8, 2))
+            cp(h8("lx", c), ps(mb, 128, 136))
+            cp(h128("x", c), ind(ap("s", o, o + 2048), h8("lx", c)), OPT["x"][c])
+            for hf in range(2):
+                oo = o + 1024 * hf
+                scan(ap("sm", oo, oo + 1024), ap("k16"), ap("s", oo, oo + 1024), ALU.mult, ALU.max)
+            uv = ps(7, 0, 8)
+            mm(grp(uv, [(ap("sm", o + 15, o + 2048, 16), ap("Fone", 16, 144, 16)), (h128("x", c), ap("Fcf", 16, 144, 16))]))
+            mm(grp(ps(mb, 0, 128), [(ap("Bcf"), h128("x", c))]))
+            cp(h8("opi", c), uv)
+            act(h128("ub", c), ps(mb, 0, 128), AF.Identity, 32.0)
+            ts(h8("opj", c), h8("opi", c), 511, ALU.bitwise_and)
+            turn(h8("opj", c), h128("gm", c), ps(7, 8, 16))
+            cp(h8("lo", c), ps(7, 8, 16))
+            tt(h128("pn", c), ind(ap("OT"), h8("lo", c)), h128("ub", c), ALU.mult)
+            ts(h128("pn2", c), h128("pn", c), 5, ALU.arith_shift_right, 4095, ALU.bitwise_and)
+            ts(h128("n16", c), h128("pn2", c), ap("ncol", 0, 1), ALU.add)
+            if "A" in OPT["e"][4 * c:4 * c + 4]:
+                mm(grp(ps(mb, 128, 256), [(h128("x", c), ap("Inz"))]))
+                cp(h128("xT", c), ps(mb, 128, 256), "A")
+            if "V" in OPT["e"][4 * c:4 * c + 4]:
+                act(ap("xs", o, o + 2048, 16), h128("x", c), AF.Identity, 0.0, col(NZ))
+            mm(grp(ps(mb, 0, 128), [(ap("Inz"), h128("x", c)), (h128(GT, c), I_)]))
+            hs = lambda l, c=c: ap("HS", 256 * l + 128 * c, 256 * l + 128 * c + 128)
+            act(hs(0), ps(mb, 0, 128), AF.Abs)
+            act(hs(2), ps(mb, 0, 128), AF.Abs, 0.0, ap("rmf", 0, 1))
+            ts(hs(1), hs(0), 6.0, ALU.is_gt, 16.0, ALU.mult)
+        act(ap("xm"), ap("x"), AF.Identity, col(R15), col(NZ))
+
+        def distances_of_x():
+            mm(grp(ps(4, 0, 48), [(sl("F4", a), ap("HS", a, 768, 16)) for a in range(16)]))
+            tt(ap("hx3"), ps(4, 0, 48), pen(1), ALU.add)
+            tt(ap("hx2"), ap("hx3", 0, 16), ap("hx3", 16, 32), ALU.min)
+            tt(ap("hx1"), ap("hx2"), ap("hx3", 32, 48), ALU.min)
+
+        def queues():
+            late = []
+            for c in range(2):
+                tt(ind(ap(V, 0, 768), h8("elu", c)), h128("Z", c), h128("Ne", c), ALU.add)
+            for l in range(3):
+                a3 = lambda name: ap(name, 256 * l, 256 * l + 256)
+                nb = 6
+                o = 256 * (l % 2) if OPT["d"][l] == "A" else 0
+                it = grp(ps(nb, o, o + 256), [(ap("B4"), a3("HS"))])
+                it += [(ps(nb, o + 128 * c, o + 128 * c + 128), ap("C128", p=(0, 17 + 2 * t + c)), ap("CR", p=(0, 17 + 2 * t + c)), False) for c in range(2)]
+                if OPT["d"][l] == "A":
+                    late.append((l, o, it + [(ps(nb, o, o + 256), ap("NIf"), a3(V), False)]))
+                    continue
+                mm(it)
+                tt(a3("D"), ps(nb, 0, 256), a3(V), ALU.subtract)
+            scan(ap("KM", 768, 1024), ap("dmax"), ap("ZT"), ALU.add, ALU.max)
+            ts(ap("wi"), ap("KM", 15, 1024, 16), -1.0 / 256, ALU.mult, 32783.0, ALU.add)
+            ts(ap("wj"), ap("wi"), 15, ALU.bitwise_and)
+            cp(ap("wb"), ap("wj"))
+            swap(7, 0, 24, lambda h: ap("wb", h, 48, 2), False)
+            for l in range(3):
+                swap(7, 48 + 16 * l, 8, lambda h: ap("wb", 48 + h, 64, 2), False)
+            tt(ap("w1"), ps(7, 0, 48), ap("m1"), ALU.add)
+            tt(ap("w2"), ps(7, 48, 96), pen(1), ALU.add)
+            tt(ap("w1"), ap("w1"), ap("w2"), ALU.min)
+            cp(ap("lw"), ap("w1"))
+            for l in range(3):
+                if OPT["d"][l] == "V":
+                    tt(ap("D2", 256 * l, 256 * l + 256), ind(ap("Tm"), ap("lw", 16 * l, 16 * l + 16)), ap("D", 256 * l, 256 * l + 256), ALU.mult)
+            for l, o, it in late[:2]:
+                mm(it)
+            for k, (l, o, it) in enumerate(late):
+                cp(ap("D", 256 * l, 256 * l + 256), ind(ap("Tm"), ap("lw", 16 * l, 16 * l + 16)), "A")
+                if k == 2:
+                    mm(it)
+                tt(ap("D2", 256 * l, 256 * l + 256), ps(6, o, o + 256), ap("D", 256 * l, 256 * l + 256), ALU.mult)
+            if t < RO - 1:
+                send([ap(V), ap("D2")], [(1, ap("V%d" % (t + 1)), "av%d" % (t + 1))], "lv%d" % (t + 1), 7000)
+            else:
+                act(ap("VO"), ap(V, 0, 768), AF.Identity, -2048.5)
+                dma("S", "oq0", T.yq[:], T["VO"][:], [ap("VO")], [ap("qki")], 3500)
+                dma("G", "oq1", T.yq[:], T["D2"][:, 0:768], [ap("D2"), ap("qki")], [], 4500, accum_op=ALU.add)
+
+        def mark_lists():
+            swap(7, 0, 8, lambda h: ap("k0b", h, 16, 2), False)
+            cp(ap("lk"), ps(7, 0, 16))
+            tt(ap("MN"), ind(ap("Tm"), ap("lk")), ap("Ne"), ALU.mult)
+            it = []
+            for h in range(2):
+                it += grp(ps(7, 256 * h, 256 * h + 256), [(I_, ap("Tri")), (ap("H%d" % h), ap("MN"))])
+            mm(it)
+            tr(ap("XT"), ps(7))
+            ts(ap("o2"), ap("XT", 0, 512, 32), -16384.0, ALU.add)
+            for k in range(16):
+                if OPT["eq"][k] == "A":
+                    act(ap("EQ", 32 * k, 32 * k + 32), ps(7, 32 * k, 32 * k + 32), AF.Abs, ap("o2", k, k + 1), -1.0)
+                else:
+                    ts(ap("EQ", 32 * k, 32 * k + 32), ps(7, 32 * k, 32 * k + 32), ap("o2", k, k + 1), ALU.not_equal)
+            scan(ap("EM"), ap("d32"), ap("EQ"), ALU.add, ALU.min)
+            ts(ap("o1"), ap("EM", 31, 512, 32), -8192.0, ALU.mult, col(DC), ALU.add)
+            tt(ap("o3"), ap("o1"), ap("o2"), ALU.max)
+            swap(7, 0, 8, lambda h: ap("o3", 8 * h, 8 * h + 8), True)
+            ts(ap("lm"), ps(7, 0, 16), 2047.5, ALU.add)
+
+        def before_turned(c):
+            hb = 4 + c
+            if OPT["gj"][c] == "A":
+                for k in range(8):
+                    act(ap("gmj", 128 * c + 16 * k, 128 * c + 16 * k + 16), ap("Ma", 0, 16), AF.Identity, 0.0, ap("jv", 8 * c + k, 8 * c + k + 1))
+                mm(grp(ps(hb, 0, 8), [(h128("gmj", c), ap("Rb"))]))
+            else:
+                turn(h8("jv", c), h128("gmj", c), ps(hb, 0, 8))
+            for k, l in enumerate((2, 1, 0, 2, 1)):
+                act(ap("penT", 48 * c + 8 * k, 48 * c + 8 * k + 8), ps(hb, 0, 8), AF.Abs, -BIG * l, BIG / 256)
+            it = []
+            for k, l in enumerate((0, 2, 1)):
+                it += grp(ps(hb, 8 * k, 8 * k + 8), [(ap("HS", 256 * l + 128 * c, 256 * l + 128 * c + 128), ap("F4", 16, 144, 16))])
+            mm(it)
+            tt(ap("hx3", 24 * c, 24 * c + 24), ps(hb, 0, 24), ap("penT", 48 * c + 16, 48 * c + 40), ALU.add)
+            tt(h8("hx2", c), ap("hx3", 24 * c, 24 * c + 8), ap("hx3", 24 * c + 8, 24 * c + 16), ALU.min)
+            tt(h8("hx1", c), h8("hx2", c), ap("hx3", 24 * c + 16, 24 * c + 24), ALU.min)
+
+        def finish_turned(c, sign):
+            hb, o = 4 + c, 2048 * c
+            rows = (0, 3 if sign else 2)
+            mm(grp(ps(hb, 0, 384), [(ap("LT", p=rows), ap("RT", p=rows))]), last=False)
+            mm([(ps(hb, k, 256, 16), ap("df", o + k, o + 2048, 16), ap("WD"), False) for k in range(16)], last=False)
+            mm([(ps(hb, 256 + k, 384, 16), ap("tf", o + k, o + 2048, 16), ap("F8" if sign else "F4", 16, 144, 16), False) for k in range(16)])
+            o = 384 * c
+            scan(ap("RM", o, o + 384), ap("dres"), ps(hb, 0, 384), ALU.add, ALU.min)
+            r15 = ap("RM", o + 15, o + 384, 16)
+            tt(ap("TT", 48 * c + 1, 48 * c + 48, 2), r15, ap("penT", 48 * c, 48 * c + 24), ALU.add)
+            tt(ap("TT", 48 * c, 48 * c + 48, 2), r15, ap("penT", 48 * c + 16, 48 * c + 40), ALU.add)
+            h16 = lambda name: ap(name, 16 * c, 16 * c + 16)
+            tt(h16("T2"), ap("TT", 48 * c, 48 * c + 16), ap("TT", 48 * c + 16, 48 * c + 32), ALU.min)
+            tt(h16("ri"), h16("T2"), ap("TT", 48 * c + 32, 48 * c + 48), ALU.min)
+            ts(h16("rj"), h16("ri"), 4095, ALU.bitwise_and)
+            turn(h16("rj"), h128("gmb", c), ps(hb, 384, 392), "l8b")
+            tt(h8("goT", c), ap("ri", 16 * c, 16 * c + 16, 2), h8("hx1", c), ALU.is_lt)
+            turn(h8("goT", c), h128("gmg", c), ps(hb, 392, 400))
+            cp(h8("lb", c), ps(hb, 384, 392))
+            cp(ap(SY, 128 + 8 * c, 136 + 8 * c), ps(hb, 392, 400))
+            cp(ap(SY, 144 * c, 144 * c + 128), ind(ap("y", 2048 * c, 2048 * c + 2048), h8("lb", c)), OPT["yb"][c])
+            send([ap(SY, 136 * c, 136 * c + 136)], [(1, ap(LY, 136 * c, 136 * c + 136), "ay%d_%d" % (t, c))], "ly%d_%d" % (t, c), 2500)
+            turn(h16("rj"), h128("gma", c), ps(hb, 400, 408), "l8a")
+            cp(h8("la", c), ps(hb, 400, 408))
+
+        if OPT["h"] == "T":
+            before_turned(0)
+            before_turned(1)
+        else:
+            distances_of_x()
+        for c in range(2):
+            for q in range(4):
+                k = 4 * c + q
+                if k == OPT["qat"]:
+                    queues()
+                if k == OPT["mat"]:
+                    mark_lists()
+                o = 512 * k
+                eg = ind(ap("EF"), ap("n16", 32 * k, 32 * k + 32))
+                Rq = ap("R", 512 * q, 512 * q + 512)
+                if OPT["e"][k] == "V":
+                    scan(ap("xb", o, o + 512), ap("k16", 0, 512), ap("xs", o, o + 512), ALU.mult, ALU.add)
+                    tt(ap("e", o, o + 512), eg, ap("xb", o, o + 512), ALU.add)
+                    ts(ap("y", o, o + 512), ap("e", o, o + 512), 0.0, ALU.max, 63.0, ALU.min)
+                else:
+                    b = bank[0] % 4
+                    bank[0] += 1
+                    cp(ap("e", o, o + 512), eg, "A")
+                    mm(grp(ps(b), [(h128("xT", c), Rq), (I_, ap("e", o, o + 512))]))
+                    ts(ap("y", o, o + 512), ps(b), 0.0, ALU.max, 63.0, ALU.min)
+                b = bank[0] % 4
+                bank[0] += 1
+                mm(grp(ps(b), [(h128(GT, c), Rq), (I_, ap("y", o, o + 512))]))
+                if OPT["h"] == "T":
+                    act(ap("df", o, o + 512), ps(b), AF.Abs)
+                    sign = OPT["t"][2 * c] == "A"
+                    if sign:
+                        act(ap("tf", o, o + 512), ap("df", o, o + 512), AF.Sign, col(M65))
+                    else:
+                        ts(ap("tf", o, o + 512), ap("df", o, o + 512), 6.0, ALU.is_gt, 16.0, ALU.mult)
+                    if q == 3:
+                        finish_turned(c, sign)
+                    continue
+                act(ap4("d", 2 * k, 2 * k + 2), ps(b), AF.Abs)
+                sign = OPT["t"][k // 2] == "A"
+                if sign:
+                    act(ap4("tt", 2 * k, 2 * k + 2), ap4("d", 2 * k, 2 * k + 2), AF.Sign, col(M65))
+                else:
+                    ts(ap4("tt", 2 * k, 2 * k + 2), ap4("d", 2 * k, 2 * k + 2), 6.0, ALU.is_gt, 16.0, ALU.mult)
+                if q % 2 == 1:
+                    hf = q // 2
+                    b0 = 8 * c + 4 * hf
+                    for l, (w, src) in ((0, ("F4", "d")), (2, ("Frm", "d")), (1, ("F8" if sign else "F4", "tt"))):
+                        rows = (0, 4 if w == "F8" else 3)
+                        pr = [(ap("L3", p=rows), ap("R3", 64 * hf, 64 * hf + 64, 1, rows))]
+                        pr += [(sl(w, a), ap4(src, b0, b0 + 4, a)) for a in range(16)]
+                        mm(grp(ps(4 + c, 128 * l + 64 * hf, 128 * l + 64 * hf + 64), pr))
+            if OPT["h"] == "T":
+                continue
+            o = 384 * c
+            scan(ap("RM", o, o + 384), ap("dres"), ps(4 + c, 0, 384), ALU.add, ALU.min)
+            r15 = ap("RM", o + 15, o + 384, 16)
+            tt(ap("TT", 48 * c + 1, 48 * c + 48, 2), r15, pen(0, c), ALU.add)
+            tt(ap("TT", 48 * c, 48 * c + 48, 2), r15, pen(1, c), ALU.add)
+            h16 = lambda name: ap(name, 16 * c, 16 * c + 16)
+            tt(h16("T2"), ap("TT", 48 * c, 48 * c + 16), ap("TT", 48 * c + 16, 48 * c + 32), ALU.min)
+            tt(h16("ri"), h16("T2"), ap("TT", 48 * c + 32, 48 * c + 48), ALU.min)
+            ts(h16("rj"), h16("ri"), 4095, ALU.bitwise_and)
+            cp(h8("lb", c), ap("rj", 16 * c + 1, 16 * c + 16, 2))
+            yw = ap("y", 2048 * c, 2048 * c + 2048)
+            cp(ap(SY, 144 * c, 144 * c + 128), ind(yw, h8("lb", c)), OPT["yb"][c])
+            tt(ap(SY, 128 + 8 * c, 136 + 8 * c), ap("ri", 16 * c, 16 * c + 16, 2), h8("hx1", c), ALU.is_lt)
+            cp(h8("la", c), ap("rj", 16 * c, 16 * c + 16, 2))
+            send([ap(SY, 136 * c, 136 * c + 136)], [(1, ap(LY, 136 * c, 136 * c + 136), "ay%d_%d" % (t, c))], "ly%d_%d" % (t, c), 2500)
+        for k in range(8):
+            cp(ind(ap("S"), ap("lm", 2 * k, 2 * k + 2)), ap("xm", 32 * k, 32 * k + 32))
+        for c in range(2):
+            o = 256 * t + 128 * c
+            cp(ap("S", o, o + 128), ind(ap("y", 2048 * c, 2048 * c + 2048), h8("la", c)), OPT["ya"][c])
+        if t < RO - 1:
+            for c in range(2):
+                o = 256 * (RO + t) + 128 * c
+                cp(ap("S", o, o + 128), ap(LY, 144 * c, 144 * c + 128), OPT["ly"])
+            add("V", [lambda SY=SY: g.vector.tensor_reduce(T["gs"][:, 0:1], T[SY][:, 128:144], AxisListType.X, ALU.add)], 64.0,
+                [ap(SY, 128, 144)], [ap("gs", 0, 1)])
+            cp(ap("gsb", 0, 1), ap("gs", 0, 1), "A")
+            mm(grp(ps(4, 0, 1), [(ap("B1"), ap("gsb", 0, 1))]))
+            cp(ap("Ai", 0, 1), ps(4, 0, 1))
+            ts(ap("Aj", 0, 1), ap("Ai", 0, 1), 63, ALU.bitwise_and)
+            ts(ap("ncol", 0, 1), ap("Aj", 0, 1), col(K37), ALU.add)
+        else:
+            dma("S", "om", T.ym[:], T["S"][15:128:16, 2048:4096], [ap("S", 2048, 4096)], [], 2500)
+            dma("S", "os0", T.ys[:, 0:1792], T["S"][:, 0:1792], [ap("S", 0, 1792)], [], 4000)
+            for c in range(2):
+                dma("SA"[c], "os%d" % (c + 1), T.ys[:, 1792 + 128 * c:1920 + 128 * c], T[LY][:, 144 * c:144 * c + 128], [ap(LY, 136 * c, 136 * c + 136)], [], 2200)
+            counters(V, ap(SY, 128, 144))
+            tt(ap("Pt"), ap("Pc"), ap("PC"), ALU.subtract)
+            ts(ap("Pb"), ap("Pt"), 1.0 / 1024, ALU.mult)
+            for hf in range(2):
+                mm([(ps(5 + hf, a, 384, 16, (0, 8)), ap("W", 16 + a, 144, 16), ap("Pb", 24 * hf, 24 * hf + 24), True) for a in range(16)])
+                cp(ap("yo", 384 * hf, 384 * hf + 384, 1, (0, 8)), ps(5 + hf, 0, 384, 1, (0, 8)), "VA"[hf])
+            dma("S", "op", T.yp[:], T["yo"][0:8, :], [ap("yo")], [], 2200)
+    return ops, Q
+
+
+def place(ops, edges, key):
+    n = len(ops)
+    succ = [[] for _ in range(n)]
+    left = [len(edges[i]) for i in range(n)]
+    for i in range(n):
+        for j, w in edges[i]:
+            succ[j].append(i)
+    start = [0.0] * n
+    busy = {e: [] for e in "VAPGS"}
+    pool = sorted((key[i], i) for i in range(n) if left[i] == 0)
+    while pool:
+        i = pool.pop(0)[1]
+        t = max([start[j] + w for j, w in edges[i]] + [0.0])
+        e, c = ops[i]["eng"], ops[i]["cost"]
+        if e is not None:
+            b = busy[e]
+            lo, hi = 0, len(b)
+            while lo < hi:
+                mid = (lo + hi) // 2
+                if b[mid][1] <= t:
+                    lo = mid + 1
+                else:
+                    hi = mid
+            while lo < len(b) and b[lo][0] < t + c:
+                t = max(t, b[lo][1])
+                lo += 1
+            b.insert(lo, (t, t + c))
+        start[i] = t
+        new = False
+        for k in succ[i]:
+            left[k] -= 1
+            if left[k] == 0:
+                pool.append((key[k], k))
+                new = True
+        if new:
+            pool.sort()
+    return start
+
+
+def schedule(ops, seed=0):
+    n = len(ops)
+    fw = [[] for _ in range(n)]
+    bw = [[] for _ in range(n)]
+    for i, o in enumerate(ops):
+        for j, need in o["deps"].items():
+            p = ops[j]
+            gap = p["lat"] + (SLAT if p["eng"] == o["eng"] else XLAT) if need or o["kind"] == "r" else 0.0
+            fw[i].append((j, p["cost"] + gap))
+            bw[j].append((i, o["cost"] + gap))
+    tail = [o["lat"] for o in ops]
+    twin = {o["cls"]: i for i, o in enumerate(ops)}
+    z = seed * 7919 + 13
+    best = None
+    for attempt in range(OPT["tries"]):
+        if best is None:
+            key = [float(i) for i in range(n)]
+        else:
+            z = (z * 1103515245 + 12345) % 2147483648
+            w0 = best[0] * (z / 2147483648.0) - 0.5 * OPT["window"]
+            z = (z * 1103515245 + 12345) % 2147483648
+            amp = OPT["noise"] * (z / 2147483648.0) ** 2
+            key = list(best[1])
+            if attempt % 8 == 0:
+                a, b = (z >> 8) % RO, (z >> 12) % RO
+                pairs = [(i, twin[(a,) + ops[i]["cls"][1:]]) for i in range(n) if ops[i]["cls"][0] == b and (a,) + ops[i]["cls"][1:] in twin]
+                shift = sorted(key[i] - key[j] for i, j in pairs)[len(pairs) // 2]
+                for i, j in pairs:
+                    key[i] = best[1][j] + shift
+                amp = 0.0
+            for i in range(n):
+                if amp and w0 <= key[i] < w0 + OPT["window"]:
+                    z = (z * 1103515245 + 12345) % 2147483648
+                    key[i] += amp * (z / 2147483648.0 - 0.5)
+        for rnd in range(2):
+            st = place(ops, fw, key)
+            end = max(st[i] + ops[i]["cost"] + tail[i] for i in range(n))
+            if best is None or end <= best[0]:
+                best = (end, st)
+            if rnd == 0:
+                back = place(ops, bw, [-(st[i] + ops[i]["cost"] + tail[i]) for i in range(n)])
+                key = [-(back[i] + ops[i]["cost"]) for i in range(n)]
+    st = best[1]
+    order = {e: [i for s, i in sorted((st[i], i) for i in range(n) if ops[i]["eng"] == e)] for e in "VAPGS"}
+    return order, st, [st[i] + ops[i]["cost"] + tail[i] for i in range(n)]
+
+
+KEPT = {}
+
+
+def rank_program(g, core, T, topo):
+    if T.rank_of(core) is None:
+        return
+    ops, Q = build(g, core, T, topo)
+    if "order" not in KEPT:
+        KEPT["order"] = schedule(ops, OPT["seed"])[0]
+    order = KEPT["order"]
+    tick = {}
+    total = {}
+    for e in "VAPG":
+        k = 0
+        for i in order[e]:
+            if ops[i]["kind"] == "c":
+                k += 1
+                tick[i] = ("c" + e, k)
+        total["c" + e] = k
+    for i, o in enumerate(ops):
+        if o["kind"] != "c":
+            tick[i] = (o["sem"], o["cnt"])
+            total[o["sem"]] = o["cnt"]
+    for e in "SPAVG":
+        seen = {}
+        for i in order[e]:
+            o = ops[i]
+            need = {}
+            for j, w in o["deps"].items():
+                if w:
+                    s, v = tick[j]
+                    need[s] = max(need.get(s, 0), v)
+            for s, v in need.items():
+                if seen.get(s, 0) < v:
+                    Q[e].wait_ge(T.sem[s], v)
+                    seen[s] = v
+            r = None
+            for f in o["fns"]:
+                r = f()
+            if o["kind"] == "c":
+                r.then_inc(T.sem["c" + e], 1)
+            elif o["kind"] == "d":
+                r.then_inc(T.sem[o["sem"]], 16)
+        if e == "G":
+            for s, v in total.items():
+                if seen.get(s, 0) < v:
+                    g.wait_ge(T.sem[s], v)

@@ -60,9 +60,9 @@ SEMAPHORES = (["cV", "cA", "cP", "cG"] + DMAS + ["lg", "ag1", "ag2", "ag3"]
               + ["%s%d" % (k, t) for k in ("lv", "av") for t in range(1, RO)]
               + ["%s%d_%d" % (k, t, c) for k in ("ly", "ay") for t in range(RO) for c in range(2)])
 
-CY, PCY, GC, SC = 1.0, 0.5, 1.5, 3.5
-XLAT, SLAT = 120.0, 70.0
-OPT = {"s": "AAVAAAAA", "eq": "A" * 16, "e": "AAAAAAAA", "ly": "V", "ve": "AA", "x": "AA", "ya": "AA", "t": "VVAA", "kr": "AAA", "en": "AV", "h": "T", "d": "VVV", "gj": "VV", "qat": 4, "mat": 7, "yb": "AA",
+CY, PCY, GC, SC = 0.95, 0.5, 1.5, 3.5
+XLAT, SLAT = 260.0, 140.0
+OPT = {"s": "AAVAAAAA", "eq": "A" * 16, "e": "AAAAAAAV", "ly": "V", "ve": "AA", "x": "VV", "ya": "AA", "t": "VVAA", "kr": "AAA", "en": "AV", "h": "T", "d": "VVV", "gj": "VV", "qat": 4, "mat": 7, "yb": "AV",
        "tries": 2500, "seed": 0, "noise": 8000.0, "window": 15000.0}
 
 
@@ -759,7 +759,7 @@ def rank_program(g, core, T, topo):
         return
     ops, Q = build(g, core, T, topo)
     if "order" not in KEPT:
-        KEPT["order"] = schedule(ops, OPT["seed"])[0]
+        KEPT["order"], KEPT["start"] = schedule(ops, OPT["seed"])[:2]
     order = KEPT["order"]
     tick = {}
     total = {}
@@ -774,19 +774,26 @@ def rank_program(g, core, T, topo):
         if o["kind"] != "c":
             tick[i] = (o["sem"], o["cnt"])
             total[o["sem"]] = o["cnt"]
+    start = KEPT["start"]
+    state = {e: {} for e in "SPAVG"}
+    known, waits = {}, {}
+    for s0, i in sorted((start[i], i) for i in range(len(ops))):
+        o = ops[i]
+        seen = state.get(o["eng"], {})
+        waits[i] = []
+        for s1, j in sorted(((start[j], j) for j, w in o["deps"].items() if w), reverse=True):
+            s, v = tick[j]
+            if seen.get(s, 0) < v:
+                waits[i].append((s, v))
+                for s2, v2 in list(known[j].items()) + [(s, v)]:
+                    seen[s2] = max(seen.get(s2, 0), v2)
+        known[i] = dict(seen) if o["eng"] is not None else {}
     for e in "SPAVG":
-        seen = {}
+        seen = state[e]
         for i in order[e]:
             o = ops[i]
-            need = {}
-            for j, w in o["deps"].items():
-                if w:
-                    s, v = tick[j]
-                    need[s] = max(need.get(s, 0), v)
-            for s, v in need.items():
-                if seen.get(s, 0) < v:
-                    Q[e].wait_ge(T.sem[s], v)
-                    seen[s] = v
+            for s, v in waits[i]:
+                Q[e].wait_ge(T.sem[s], v)
             r = None
             for f in o["fns"]:
                 r = f()

@@ -1,69 +1,78 @@
 from concourse.bass import DstId, RemoteDMATransfer
-from concourse.mybir import AluOpType, AxisListType, ActivationFunctionType
+from concourse.mybir import AluOpType, ActivationFunctionType
 
 N, RO = 4, 4
 ALU = AluOpType
 AF = ActivationFunctionType
 F32, BF, I32, U16 = "float32", "bfloat16", "int32", "uint16"
-VW = 896
-PB, PM, EB, ED = 768, 816, 864, 880
+VW = 464
+PB, PM, EB, ED = 384, 416, 448, 456
 RC = 1.5 * 2.0 ** 35
 BIG = 2.0 ** 23
+B = 2.0 ** 17
 
-SB = {
-    "S": (4128, BF), "EF": (4736, BF), "OT": (512, BF), "qni": (768, I32), "qki": (768, I32), "tui": (768, I32),
-    "tub": (768, BF), "gli": (256, BF), "rmb": (8, BF), "rmf": (4, F32),
-    "s": (4096, BF), "sm": (4096, BF), "e": (4096, BF), "y": (4096, BF), "xs": (4096, BF), "xb": (4096, BF),
-    "D2": (VW, F32), "D": (768, F32), "KR": (768, F32), "KT": (768, F32), "KM": (1024, F32), "VO": (768, F32),
-    "Ve": (256, F32), "E": (256, F32), "Ne": (256, F32), "Z": (256, F32), "ZT": (256, F32), "ZM": (256, F32),
-    "q16": (256, U16), "n16": (256, U16), "pn": (256, I32), "pn2": (256, I32), "ub": (256, F32),
-    "x": (256, BF), "xm": (256, BF), "xT": (256, BF), "HS": (768, BF), "MN": (256, F32),
-    "XT": (512, F32), "EQ": (512, BF), "EM": (512, BF), "RM": (768, F32),
-    "elf": (16, F32), "elt": (16, F32), "elu": (16, U16), "jv": (16, F32), "m1": (48, F32),
-    "Pc": (48, F32), "Pt": (48, F32), "mn": (16, F32), "mni": (16, I32), "mnj": (16, I32),
-    "k0i": (16, I32), "k0j": (16, I32), "k0b": (16, BF), "lx": (16, U16), "lk": (16, U16),
-    "opi": (16, I32), "opj": (16, I32), "lo": (16, U16), "wi": (64, I32), "wj": (64, I32), "wb": (64, BF), "w1": (48, F32), "w2": (48, F32), "lw": (48, U16),
-    "TT": (96, F32), "T2": (32, F32), "ri": (32, I32), "rj": (32, I32), "la": (16, U16), "lb": (16, U16),
-    "hx3": (48, F32), "hx2": (16, F32), "hx1": (16, F32), "o1": (16, F32), "o2": (16, F32), "o3": (16, F32), "lm": (16, U16),
-    "gs": (4, F32), "gsb": (8, BF), "Ai": (4, I32), "Aj": (4, I32), "ncol": (4, F32), "Pb": (48, BF), "yo": (768, F32),
-    "pi": (4, I32), "ci": (32, I32), "cf": (32, F32), "J160": (160, BF), "Jg": (128, BF), "J32": (128, BF), "Jc": (256, BF),
-    "Jb": (128, F32), "Jl": (48, F32), "KI2": (128, BF), "c16": (8, BF), "iL": (16, F32), "PC": (48, F32),
-    "NIf": (128, F32), "l8a": (8, U16), "l8b": (8, U16), "LT": (128, BF), "RT": (384, BF), "WD": (16, BF), "penT": (96, F32), "goT": (16, F32),
-    "gmj": (256, F32), "gmb": (256, F32), "gmg": (256, F32), "gma": (256, F32), "df": (4096, BF), "tf": (4096, BF),
-    "l8": (8, U16), "Ma": (128, F32), "Rb": (8, F32), "gm": (256, F32), "L3": (128, BF), "R3": (128, BF), "R3a": (128, BF), "CR": (128, BF), "C128": (128, BF),
-    "W": (160, BF), "W0": (160, BF), "W1": (160, BF), "W0f": (160, F32), "W1f": (160, F32), "Inz": (128, BF),
-    "Fone": (160, BF), "Fcf": (160, BF), "F4": (160, BF), "F8": (160, BF), "Frm": (160, BF), "Fmk": (160, BF), "G8": (160, BF),
-    "B4": (128, BF), "Bcf": (128, BF), "B1": (128, BF), "H0": (128, F32), "H1": (128, F32), "Tri": (256, BF), "Tm": (16, F32),
-    "R": (2048, BF), "k16": (1024, BF), "d32": (512, BF), "dmin": (128, BF), "dmax": (256, BF), "dres": (384, BF),
+TWICE = {
+    "s": (2048, BF), "sm": (2048, BF), "e": (2048, BF), "y": (2048, BF), "df": (2048, BF), "tf": (2048, BF),
+    "qni": (384, I32), "qki": (384, I32), "VO": (384, F32), "D2": (VW, F32), "KM": (384, F32), "RM": (384, F32),
+    "Vi": (128, I32), "Ni": (128, I32), "Ki": (128, I32), "Ve": (128, F32), "Ne": (128, F32), "Z": (128, F32), "ZT": (128, F32), "ZM": (128, F32),
+    "q16": (128, U16), "n16": (128, U16), "pn": (128, I32), "pn2": (128, I32), "ub": (128, F32),
+    "x": (128, BF), "xT": (128, BF), "xd": (256, BF), "HS": (256, BF), "MN": (128, F32), "ya": (128, BF),
+    "XT": (256, F32), "EQ": (256, BF), "EM": (256, BF), "RW": (80, BF), "RWT": (128, BF), "RWN": (128, BF),
+    "elf": (8, F32), "elt": (8, F32), "elu": (8, U16), "m1": (32, BF), "Pc": (32, F32), "Pt": (32, F32), "mn": (8, F32), "mn2": (8, F32),
+    "k0t": (8, F32), "k0b": (16, BF), "lx": (8, U16), "lk": (8, U16), "opi": (8, I32), "opj": (8, I32), "lo": (8, U16), "wt": (24, F32),
+    "sa": (24, F32), "sb": (24, F32), "la": (8, U16), "lb": (8, U16), "o1": (8, F32), "lm": (16, U16),
+    "gs": (8, F32), "gsb": (16, BF), "ncol": (8, F32), "Pb": (32, BF), "rmf": (8, F32), "r32": (8, F32),
+    "gmj": (128, BF), "gmb": (128, F32), "gma": (128, F32), "gm": (128, F32),
+    "xs": (512, BF), "xb": (512, BF), "bt": (8, F32), "br": (16, BF), "gmc": (128, BF),
+    "Gt": (160, BF), "Dup": (128, BF), "Brm": (128, BF), "WD": (32, BF), "WK": (32, BF), "WX0": (384, BF), "LT": (128, BF),
 }
+SB = {
+    "tui": (128, I32), "tub": (128, BF), "gli": (256, BF), "rmb": (8, BF),
+    "pi": (4, I32), "ci": (32, I32), "cf": (48, F32), "J160": (160, BF), "Jg": (128, BF), "Jh": (128, BF), "J32": (128, BF), "Jc": (256, BF), "J64": (192, BF),
+    "J8": (8, F32), "Jl": (32, F32), "KI": (128, BF), "JR": (512, BF), "Jx": (24, BF), "Jq": (384, BF), "QW": (384, BF), "JM": (384, BF),
+    "c16": (8, BF), "c16s": (8, BF), "PC": (32, F32), "l3": (4, U16), "CK": (16, F32), "KS": (128, BF),
+    "l8": (8, U16), "l8s": (8, U16), "Ma": (128, F32), "Rb": (8, F32), "Rbn": (8, F32), "Rbb": (8, BF), "Rbs": (8, F32), "Rj": (48, BF), "Cj": (48, BF),
+    "CR": (128, BF), "CR0": (128, BF), "ONE": (128, BF), "ONR": (128, BF), "NEG": (128, BF), "RCt": (384, BF), "CS": (32, BF),
+    "W": (160, BF), "W0": (160, BF), "W1": (160, BF), "DW0": (160, F32), "DW1": (160, F32), "Inz": (128, BF), "If": (128, F32), "I4": (128, BF),
+    "Fone": (160, BF), "Fcf": (160, BF), "Fmk": (160, BF),
+    "B4": (128, BF), "Bcf": (128, BF), "B1": (128, F32), "B64": (128, F32), "B64n": (128, F32),
+    "H0": (128, F32), "H1": (128, F32), "Tm": (16, F32), "WX1": (384, BF), "WT": (24, BF), "W2": (24, BF),
+    "R": (512, BF), "k16": (512, BF), "dgt": (256, BF), "dmin": (128, BF), "dcap": (128, BF), "dmax": (384, BF), "dres": (384, BF),
+}
+for _k, (_w, _d) in TWICE.items():
+    SB[_k] = (2 * _w, _d)
 SCRATCH, PLACE, _fill = {}, {}, {}
 for _k, (_w, _d) in SB.items():
-    if _w <= 160 and _k not in ("rmb", "gs"):
+    if _w <= 256 and _k not in ("rmb", "gs", "tui", "gli"):
         PLACE[_k] = ("pool_" + _d, _fill.get(_d, 0), _w)
         _fill[_d] = _fill.get(_d, 0) + (_w + 15) // 16 * 16
     else:
         SCRATCH[_k] = ("sbuf", [128, _w], _d)
 for _d, _w in _fill.items():
     SCRATCH["pool_" + _d] = ("sbuf", [128, _w], _d)
-SCRATCH["pen"] = ("sbuf", [128, 4, 16], F32)
-SCRATCH["d"] = ("sbuf", [128, 16, 16, 16], BF)
-SCRATCH["tt"] = ("sbuf", [128, 16, 16, 16], BF)
+for _c in range(2):
+    SCRATCH["S%d" % _c] = ("sbuf", [128, 4128], BF)
+    SCRATCH["EF%d" % _c] = ("sbuf", [128, 4736], BF)
+    SCRATCH["OT%d" % _c] = ("sbuf", [128, 512], BF)
+    SCRATCH["o3%d" % _c] = ("sbuf", [128, 2, 8], F32)
+    SCRATCH["yo%d" % _c] = ("sbuf", [128, 3, 256], F32)
 for _t in range(RO):
-    SCRATCH["V%d" % _t] = ("sbuf", [128, VW], F32)
+    SCRATCH["V%d" % _t] = ("sbuf", [128, 2 * VW], F32)
     SCRATCH["GT%d" % _t] = ("sbuf", [128, 256], BF)
-    SCRATCH["SY%d" % _t] = ("sbuf", [128, 272], BF)
-    SCRATCH["LY%d" % _t] = ("sbuf", [128, 272], BF)
+    SCRATCH["SY%d" % _t] = ("sbuf", [128, 288], BF)
+    SCRATCH["LY%d" % _t] = ("sbuf", [128, 288], BF)
 for _b in range(8):
     SCRATCH["ps%d" % _b] = ("psum", [128, 512], F32)
-DMAS = ["dS0", "dS1", "dE0", "dE1", "dE2", "dOT", "dqn", "dqk", "dtu", "dgl", "drm", "oq0", "oq1", "op", "os0", "os1", "os2", "om"]
-SEMAPHORES = (["cV", "cA", "cP", "cG"] + DMAS + ["lg", "ag1", "ag2", "ag3"]
-              + ["%s%d" % (k, t) for k in ("lv", "av") for t in range(1, RO)]
+SEMAPHORES = (["cV", "cA", "cP", "cG", "dtu", "dgl", "drm", "lg", "ag1", "ag2", "ag3"]
+              + [k + str(c) for k in ("dSa", "dSb", "dEa", "dEb", "dOT", "dqn", "dqk", "oq", "op", "osa", "osb", "om") for c in range(2)]
+              + ["%s%d_%d" % (k, t, c) for k in ("lv", "av") for t in range(1, RO) for c in range(2)]
               + ["%s%d_%d" % (k, t, c) for k in ("ly", "ay") for t in range(RO) for c in range(2)])
 
 CY, PCY, GC, SC = 0.95, 0.5, 1.5, 3.5
 XLAT, SLAT = 260.0, 140.0
-OPT = {"s": "AAVAAAAA", "eq": "A" * 16, "e": "AAAAAAAV", "ly": "V", "ve": "AA", "x": "VV", "ya": "AA", "t": "VVAA", "kr": "AAA", "en": "AV", "h": "T", "d": "VVV", "gj": "VV", "qat": 4, "mat": 7, "yb": "AV",
-       "tries": 2500, "seed": 0, "noise": 8000.0, "window": 15000.0}
+OPT = {"s": "AAAVAAAV", "e": "AAAXAAAX", "t": "AAAAAAAA", "x": "AA", "uv": "TT", "qat": 2, "mat": 0, "sq": "A", "z": "V", "gj": "AA",
+       "ya": "AA", "yb": "AA", "sa": "AA", "sb": "AA", "b": "P", "cuts": (0, 128),
+       "tries": 9000, "seed": 0, "noise": 5000.0, "window": 10000.0, "slack": 800.0}
 
 
 def build(g, core, T, topo):
@@ -86,15 +95,14 @@ def build(g, core, T, topo):
         steps[(name, lo, hi, len(range(lo, hi, step)))] = step
         return (name, lo, hi, r, len(range(lo, hi, step)), SCRATCH[name][2])
 
-    def ap4(name, b0, b1, a=None):
-        t = T[name]
-        r = t[:, b0:b1, :, :] if a is None else t[:, b0:b1, a, :]
-        return (name, 256 * b0, 256 * b1, r, (b1 - b0) * (256 if a is None else 16), BF)
+    def of(c):
+        def u(name, lo=0, hi=None, step=1, p=None):
+            w = TWICE[name][0] if name in TWICE else T[name].shape[1] // 2
+            return ap(name, c * w + lo, c * w + (w if hi is None else hi), step, p)
+        return u
 
-    def pen(l0, c=None, n=3):
-        t = T["pen"]
-        r = t[:, l0:l0 + n, :] if c is None else t[:, l0:l0 + n, 8 * c:8 * c + 8]
-        return ("pen", 16 * l0, 16 * (l0 + n), r, n * (16 if c is None else 8), F32)
+    def view(name, r, n):
+        return (name, 0, 1, r, n, SCRATCH[name][2])
 
     def ind(win, off):
         return (win[0], win[1], win[2], win[3].indirect(off[3]), 16 * off[4], win[5], off)
@@ -117,7 +125,7 @@ def build(g, core, T, topo):
         ops.append({"eng": eng, "fns": fns, "cost": cost, "deps": deps, "kind": kind, "sem": sem, "cnt": cnt, "lat": lat,
                     "tag": wr[0][:2] if wr else ("", 0)})
         nm = wr[0][0] if wr else ""
-        nm = (eng, kind, nm[:2] if nm[:2] in ("SY", "LY", "ps") else "V" if nm[:1] == "V" and nm[1:].isdigit() else nm)
+        nm = (eng, kind, nm[:2] if nm[:2] in ("SY", "LY") else "V" if nm[:1] == "V" and nm[1:].isdigit() else nm)
         seen[(now[0], nm)] = seen.get((now[0], nm), 0) + 1
         ops[i]["cls"] = (now[0], nm, seen[(now[0], nm)])
         for isw, a in [(False, a) for a in rd] + [(True, a) for a in wr]:
@@ -179,12 +187,18 @@ def build(g, core, T, topo):
     def tr(out, a):
         return add("V", [lambda: g.vector.transpose(out[3], a[3])], vcost(out, [a]), [a], [out])
 
-    def act(out, a, fn, bias=0.0, scale=1.0):
+    def act(out, a, fn, bias=0.0, scale=1.0, acc=None):
         c = 65 + out[4] * GC * CY if len(a) > 6 else max(64, out[4]) * CY
+        if acc is not None:
+            f = lambda: g.scalar.activation(out[3], a[3], fn, bias=val(bias), scale=val(scale), accum_out=acc[3])
+            return add("A", [f], c + 20, [a, bias, scale], [out, acc])
         return add("A", [lambda: g.scalar.activation(out[3], a[3], fn, bias=val(bias), scale=val(scale))], c, [a, bias, scale], [out])
 
-    def mm(items, last=True):
-        fns, cost, rd, wr = [], 0.0, [], []
+    def mul(out, a, c):
+        return act(out, a, AF.Identity, 0.0, c)
+
+    def mm(items, last=True, also=()):
+        fns, cost, rd, wr = [], 0.0, [], list(also)
         for k, (o, l, r, st) in enumerate(items):
             nxt = items[k + 1][3] if k + 1 < len(items) else last
             fns.append(lambda o=o, l=l, r=r, st=st, sp=nxt: g.tensor.matmul(o[3], l[3], r[3], st, sp))
@@ -196,15 +210,24 @@ def build(g, core, T, topo):
     def grp(o, pairs, first=True):
         return [(o, l, r, first and k == 0) for k, (l, r) in enumerate(pairs)]
 
+    alone = ("alone", 0, 1, None, 1, F32)
+
     def iota(out, pat, base, cm):
         if out[5] == I32:
             f = lambda: g.iota(out[3], pat, base, cm)
         else:
             f = lambda: g.iota(out[3], pat, base, cm, allow_small_or_imprecise_dtypes=True)
-        return add("G", [f], 130 + 2 * out[4] * CY, [], [out])
+        return add("G", [f], 130 + 2 * out[4] * CY, [alone], [out])
 
-    def dma(eng, sem, out, in_, reads, writes, lat, after=(), **kw):
-        return add(eng, [lambda: Q[eng].dma_start(out, in_, **kw)], 60.0, reads, writes, "d", sem, 16, lat, after)
+    def select(out, a, pat, base, cm):
+        f = lambda: g.affine_select(out[3], a[3], pat, ALU.is_equal, 0.0, base, cm)
+        return add("G", [f], 170 + 2 * out[4] * CY, [a], [out, alone])
+
+    last_dma = {}
+
+    def dma(eng, sem, pairs, reads, writes, lat):
+        fns = [lambda o=o, a=a: Q[eng].dma_start(o, a) for o, a in pairs]
+        last_dma[eng] = add(eng, fns, 60.0 * len(pairs), reads, writes, "d", sem, 16 * len(pairs), lat, [last_dma[eng]] if eng in last_dma and now[0] < 0 else [])
 
     def send(srcs, dsts, lsem, lat):
         trs = []
@@ -221,486 +244,462 @@ def build(g, core, T, topo):
             add(None, [], 0.0, [], [land], "r", asem, per, 0.0, [i])
 
     ps = lambda b, lo=0, hi=512, step=1, p=None: ap("ps%d" % b, lo, hi, step, p)
-    col = lambda k: ap("cf", k, k + 1)
+    col = lambda k, p=None: ap("cf", k, k + 1, 1, p)
     sl = lambda name, s: ap(name, 16 - s, 144 - s)
+    row = lambda name, lo=0, hi=None, n=1: ap(name, lo, hi, 1, (0, n))
+    half = lambda r: slice(64 * r, 64 * r + 64)
 
-    dma("S", "dtu", T["tui"][0:8, :], T.tu[:], [], [ap("tui")], 2200)
-    dma("A", "dqk", T["qki"][:], T.qk[:], [], [ap("qki")], 2500)
-    dma("S", "dqn", T["qni"][:], T.qn[:], [], [ap("qni")], 2500)
-    dma("A", "dS0", T["S"][:, 0:2048], T.st0[:, 0:2048], [], [ap("S", 0, 2048)], 5500)
-    dma("S", "dS1", T["S"][:, 2048:4096], T.st0[:, 2048:4096], [], [ap("S", 2048, 4096)], 5500)
-    dma("S", "dgl", T["gli"][:], T.gl[:], [], [ap("gli")], 5500)
-    dma("A", "drm", T["rmb"][:, 0:1], T.rm[:], [], [ap("rmb")], 5500)
-    dma("S", "dOT", T["OT"][:], T.ot[:], [], [ap("OT")], 6000)
-    dma("S", "dE0", T["EF"][:, 0:2048], T.ef[:, 0:2048], [], [ap("EF", 0, 2048)], 9000)
-    dma("S", "dE1", T["EF"][:, 2048:4096], T.ef[:, 2048:4096], [], [ap("EF", 2048, 4096)], 9000)
-    dma("S", "dE2", T["EF"][:, 4096:4736], T.ef[:, 0:640], [], [ap("EF", 4096, 4736)], 9500)
+    dma("S", "dtu", [(T["tui"][32 * l:32 * l + 16, :], T.tu[:, 256 * l:256 * l + 256]) for l in range(3)], [], [ap("tui")], 2200)
+    for c in range(2):
+        u = of(c)
+        for eng, nm, src in (("A", "qk", T.qk), ("S", "qn", T.qn)):
+            dma(eng, "d%s%d" % (nm, c), [(u(nm + "i", 128 * l, 128 * l + 128, 1, (64 * r, 64 * r + 64))[3], src[half(c), 256 * l + 128 * r:256 * l + 128 * r + 128])
+                                         for r in range(2) for l in range(3)], [], [u(nm + "i")], 2500 + 4500 * c)
+        for r in range(2):
+            dma("AS"[r], "dS%s%d" % ("ab"[r], c), [(T["S%d" % c][half(r), 0:4096], T.st0[half(c), :])], [], [ap("S%d" % c, 2048 * r, 2048 * r + 2048)], 5500 + 4000 * c)
+        if c == 0:
+            dma("S", "dgl", [(T["gli"][:], T.gl[:])], [], [ap("gli")], 5500)
+            dma("A", "drm", [(T["rmb"][:, 0:1], T.rm[:])], [], [ap("rmb")], 5500)
+    for c in range(2):
+        dma("S", "dOT%d" % c, [(T["OT%d" % c][half(r), :], T.ot[half(c), :]) for r in range(2)], [], [ap("OT%d" % c)], 9000 + 4000 * c)
+        for r in range(2):
+            dma("S", "dE%s%d" % ("ab"[r], c), [(T["EF%d" % c][half(r), 0:4096], T.ef[half(c), :]), (T["EF%d" % c][half(r), 4096:4736], T.ef[half(c), 0:640])],
+                [], [ap("EF%d" % c, 2048 * r, 2048 * r + 2048)], 12500 + 4000 * c)
 
-    P_, K_, G16, P32, A32, NZ, CFC, NZ4, MK, HH0, HH1, R15, K16, K37, DC, P16, RM4, E0, N0, E1, N1, E1X, E2, E3X, M65, E2X = range(26)
+    (P_, K_, G16, P32, A32, NZ, CFC, MK, HH0, HH1, R15, K16, K37, DC, E0, N0, E1, N1, N32, G1, G2, SQ, SQN, M65, CA, CB, K128,
+     P64, G64, RR0, RR1, K8, TA, TB) = range(34)
     iota(ap("pi", 0, 1), [[0, 1]], 0, 1)
     iota(ap("J160"), [[1, 160]], -16, 0)
-    iota(ap("Jl"), [[256, 3], [16, 16]], 0, 0)
-    iota(ap("Jb"), [[256, 8], [0, 16]], 0, 0)
+    iota(ap("Jl"), [[128, 4], [16, 8]], 0, 0)
+    iota(ap("J8"), [[1, 8]], 0, 0)
     iota(ap("Jg"), [[16, 8], [0, 16]], 0, 0)
-    iota(ap("KI2"), [[0, 8], [1, 16]], 0, 0)
+    iota(ap("KI"), [[0, 8], [1, 16]], 0, 0)
+    iota(ap("J64"), [[0, 3], [1, 64]], 0, 0)
+    iota(ap("Jh"), [[0, 2], [16, 4], [0, 16]], 0, 0)
     iota(ap("J32"), [[32, 4], [0, 32]], 0, 0)
     iota(ap("Jc"), [[0, 8], [1, 32]], 0, 0)
+    iota(ap("JR"), [[1, 32], [0, 16]], 0, 0)
+    iota(ap("Jx"), [[16, 8], [1, 3]], 0, 0)
+    iota(ap("Jq"), [[0, 24], [2, 16]], -30, 0)
     cp(col(P_), ap("pi", 0, 1))
-    ts(ap("ci", 0, 1), ap("pi", 0, 1), 15, ALU.bitwise_and)
-    ts(ap("ci", 4, 5), ap("pi", 0, 1), 31, ALU.bitwise_and)
-    cp(col(K_), ap("ci", 0, 1))
-    cp(col(P32), ap("ci", 4, 5))
+    for k, (m, cl) in enumerate(((15, K_), (31, P32), (63, P64), (7, K8), (1, TA), (6, TB), (8, CA))):
+        ts(ap("ci", k, k + 1), ap("pi", 0, 1), m, ALU.bitwise_and)
+        cp(col(cl), ap("ci", k, k + 1))
+    J = ap("J160")
+    mul(col(TB), col(TB), 8.0)
+    act(col(TA), col(TA), AF.Identity, col(TB), 64.0)
+    for c in range(2):
+        act(col(TB), col(CA), AF.Abs, -128.0 * 8 * c, 128.0)
+        tt(col(TB), col(TB), col(TA), ALU.add)
+        ts(of(c)("Gt"), J, col(TB), ALU.is_equal)
     ts(col(G16), col(P_), col(K_), ALU.subtract)
     ts(col(A32), col(P_), col(P32), ALU.subtract)
+    ts(col(G64), col(P64), col(K_), ALU.subtract)
     ts(col(NZ), col(K_), 15.0, ALU.is_lt)
     ts(col(CFC), col(K_), 2.0, ALU.mult, 1.0, ALU.add)
     ts(col(CFC), col(CFC), col(NZ), ALU.mult)
-    ts(col(NZ4), col(K_), 15.0, ALU.is_lt, 4096.0, ALU.mult)
     ts(col(MK), col(K_), 15.0, ALU.is_equal, 2.0 ** 22, ALU.mult)
     ts(col(HH0), col(P32), 16.0, ALU.is_lt)
-    ts(col(HH1), col(P32), 16.0, ALU.is_ge)
-    ts(col(R15), col(K_), 15.0, ALU.is_equal)
-    ts(col(K16), col(K_), 16.0, ALU.mult)
-    ts(col(K37), col(K_), 37.0, ALU.mult)
-    ts(col(DC), col(P32), 2048.5, ALU.add)
-    ts(col(P16), col(P_), 16.0, ALU.mult)
+    ts(col(RR0), col(P_), 64.0, ALU.is_lt)
     ts(col(E0), col(P_), 0.0, ALU.is_equal)
-    ts(col(N0), col(P_), 0.0, ALU.not_equal)
     ts(col(E1), col(P_), 1.0, ALU.is_equal)
-    ts(col(N1), col(P_), 1.0, ALU.not_equal)
-    ts(col(E1X), col(P_), 1.0, ALU.is_equal, 16.0, ALU.mult)
-    ts(col(E2), col(P_), 2.0, ALU.is_equal)
-    cp(ap("rmf", 0, 1), ap("rmb", 0, 1))
-    ts(col(RM4), ap("rmf", 0, 1), 4096.0, ALU.mult)
-    J = ap("J160")
-    ts(ap("G8"), J, col(P16), ALU.is_equal)
-    for nm, c in (("Fmk", MK), ("Fone", NZ), ("Fcf", CFC), ("F4", NZ4), ("Frm", RM4)):
+    for a, b in ((HH1, HH0), (RR1, RR0), (R15, NZ), (N1, E1)):
+        act(col(a), col(b), AF.Identity, 1.0, -1.0)
+    act(col(N0), col(E0), AF.Identity, 128.0, -128.0)
+    mul(col(K16), col(K_), 16.0)
+    mul(col(K37), col(K_), 37.0)
+    mul(col(N32), col(NZ), -32.0)
+    act(col(DC), col(P32), AF.Identity, 4096.0)
+    act(col(G1), col(G16), AF.Identity, 1.0)
+    act(col(G2), col(G16), AF.Identity, 2.0)
+    for p, v in (((0, 32), 2.0 ** 16), ((32, 64), 2.0 ** -26), ((64, 96), BIG)):
+        ms(col(SQ, p), v)
+    ms(col(M65), -6.5)
+    for nm, c in (("Fmk", MK), ("Fone", NZ), ("Fcf", CFC)):
         ts(ap(nm), J, col(G16), ALU.is_equal, col(c), ALU.mult)
     ts(ap("W"), J, col(P_), ALU.is_equal)
-    for sfx in ("", "f"):
-        ts(ap("W0" + sfx), J, col(P_), ALU.is_equal, col(HH0), ALU.mult)
-        ts(ap("W1" + sfx), J, col(P_), ALU.is_equal, col(HH1), ALU.mult)
-    ts(ap("Inz"), ap("J160", 16, 144), col(P_), ALU.is_equal, col(NZ), ALU.mult)
-    ts(ap("B4"), ap("Jg"), col(G16), ALU.is_equal, col(NZ4), ALU.mult)
-    ts(ap("Bcf"), ap("Jg"), col(G16), ALU.is_equal, col(CFC), ALU.mult)
+    I_ = sl("W", 0)
+    for k in range(2):
+        mul(ap("W%d" % k), ap("W"), col((HH0, HH1)[k]))
+        ts(of(k)("Dup"), ap("J64", 0, 128), col(P64), ALU.is_equal, col((RR0, RR1)[k]), ALU.mult)
+    mul(ap("Inz"), I_, col(NZ))
+    mul(ap("If"), I_, 1.0)
+    mul(ap("I4"), I_, 4.0)
     ts(ap("B1"), ap("Jg"), col(G16), ALU.is_equal)
+    ts(ap("B64"), ap("Jh"), col(G64), ALU.is_equal)
+    mul(ap("B64n"), ap("B64"), -1.0)
+    mul(ap("Bcf"), ap("B1"), col(CFC))
+    mul(ap("B4"), ap("B1"), col(N32))
+    mul(ap("B4"), ap("B4"), 128.0)
     ts(ap("H0"), ap("J32"), col(A32), ALU.is_equal, col(HH0), ALU.mult)
     ts(ap("H1"), ap("J32"), col(A32), ALU.is_equal, col(HH1), ALU.mult)
-    ts(ap("Tri"), ap("Jc"), col(P32), ALU.is_ge, 16384.0, ALU.mult)
+    ts(ap("dgt"), ap("Jc"), col(P32), ALU.is_gt)
     ts(ap("Tm"), ap("J160", 16, 32), col(K_), ALU.is_equal)
-    ts(ap("R3a"), ap("KI2"), col(E0), ALU.mult, col(E1), ALU.add)
-    if OPT["h"] != "T":
-        ts(col(E3X), col(P_), 3.0, ALU.is_equal, 120.0 * 4096, ALU.mult)
-        ts(ap("L3"), ap("KI2"), col(E1X), ALU.mult, col(N1), ALU.add)
-        ts(ap("R3"), ap("Jb"), col(E2), ALU.mult, col(E3X), ALU.add)
-        tt(ap("R3"), ap("R3"), ap("R3a"), ALU.add)
-    if "A" in OPT["t"]:
-        ts(ap("F8"), ap("F4"), 8.0, ALU.mult)
-        ms(col(M65), -6.5)
-    if "A" in OPT["d"]:
-        ts(ap("NIf"), ap("J160", 16, 144), col(P_), ALU.is_equal, -1.0, ALU.mult)
-    ts(ap("CR"), ap("J160", 16, 144), 0.5, ALU.add, 1.0 / 128, ALU.mult)
+    ts(ap("CR0"), ap("J160", 16, 144), col(E0), ALU.mult, col(N0), ALU.add)
+    act(ap("CR"), ap("J160", 16, 144), AF.Identity, 0.5)
     ts(ap("CR"), ap("CR"), col(E0), ALU.mult, col(N0), ALU.add)
-    ms(ap("C128"), 128.0)
-    ts(ap("c16"), ap("Jb", 0, 128, 16), col(K16), ALU.add)
-    ts(ap("iL"), ap("Jl", 0, 16), col(K_), ALU.add)
-    ts(ap("PC"), ap("Jl"), col(K_), ALU.add, 16384.0, ALU.add)
-    I_ = sl("W", 0)
-    for k in range(16):
-        cp(ap("R", k, 2048, 16), I_)
-    for nm, per, v0, v in (("k16", 16, 0.0, 1.0), ("d32", 32, 2 * BIG, 0.0), ("dmin", 16, 2 * BIG, -256.0), ("dmax", 16, -2 * BIG, 256.0), ("dres", 16, 2 * BIG, 0.0)):
+    ms(ap("ONE"), 1.0)
+    ms(ap("NEG"), -1.0)
+    ms(ap("ONR", 64, 128), -1.0)
+    mul(ap("ONR", 0, 64), ap("NEG", 0, 64), col(N1))
+    ms(ap("RCt"), 2.0 ** 35)
+    ms(ap("CS", 0, 8), 1.5 * 2.0 ** 28)
+    ms(ap("CS", 8, 9), 1.5 * 2.0 ** 29)
+    ms(ap("CS", 9, 10), 31.5)
+    ts(ap("c16"), ap("J8"), 256.0, ALU.mult, col(K16), ALU.add)
+    mul(ap("c16s"), ap("c16"), 128.0)
+    ts(ap("PC"), ap("Jl"), col(K_), ALU.add, 1.0 / 1024, ALU.mult)
+    ts(ap("R"), ap("JR"), col(P32), ALU.is_equal)
+    inps = OPT["z"] == "P"
+    K0 = 0.0 if inps else 15.0
+    if inps:
+        mul(ap("KS"), ap("KI"), 128.0)
+        mul(col(K128), col(K_), 128.0)
+    for nm, per, v0, v in (("k16", 16, 0.0, 1.0), ("dcap", 16, 2.0 ** 22, -BIG) if inps else ("dmin", 16, 2 * BIG, -128.0),
+                           ("dmax", 16, -2 * BIG, 128.0), ("dres", 16, 2 * BIG, 0.0)):
         ms(ap(nm), v)
         ms(ap(nm, 0, None, per), v0)
-    ms(ap("D2", 768, VW), 0.0)
-    bank = [0]
-    for c in range(2):
-        if "V" in OPT["e"][4 * c:4 * c + 4]:
-            ms(ap("xs", 2048 * c, 2048 * c + 2048), 0.0)
-    cp(ap("ncol", 0, 1), col(K37))
+    ms(ap("RW"), 0.0)
+    ms(ap("RW", 64, 160, 80), 1.0)
+    select(ap("QW", p=(0, 32)), ap("Jq", p=(0, 32)), [[-1, 24], [0, 16]], 0, 1)
+    select(ap("QW", p=(32, 64)), ap("RCt", p=(32, 64)), [[-1, 24], [0, 16]], 0, 1)
+    act(ap("QW", p=(64, 96)), ap("Jq", p=(64, 96)), AF.Square, 0.0, 0.5)
+    cp(ap("l8"), ap("J8"))
+    ts(ap("l8s"), ap("J8"), 3.0, ALU.mult, 2.0, ALU.add)
+    ts(ap("Ma"), ap("KI", 0, 128), col(K_), ALU.is_equal)
+    ts(ap("Rb"), ap("Jg", 0, 128, 16), col(G16), ALU.is_equal)
+    mul(ap("Rbn"), ap("Rb"), -1.0)
+    mul(ap("Rbb"), ap("Rb"), 1.0)
+    mul(ap("Rbs"), ap("Rb"), 1.0 / B)
+    for k in range(2):
+        cp(ap("l3", k, k + 1), col(K8))
+    for k in range(3):
+        mul(ap("JM", 128 * k, 128 * k + 128), ap("Ma"), 128.0 * k)
+    ts(ap("WT"), ap("Jx"), col(G1), ALU.is_equal, col(N32), ALU.mult)
+    ts(ap("CK"), ap("KI", 0, 16), col(R15), ALU.mult, col(NZ), ALU.add)
+    for k in range(16):
+        cp(ap("WX1", k, 384, 16), ap("WT"), "A")
+    mul(ap("WT"), ap("WT"), -8.0)
+    STEP = (((2 * BIG, 0.0), (-B, 2 * B), (-3 * B, 2 * B)), ((2 * BIG, 0.0), (4 * B, -4 * B), (-B, 2 * B)))
+    for w in range(2):
+        for l in range(3):
+            mul(ap("Rj", 24 * w + l, 24 * w + 24, 3), ap("Rb"), STEP[w][l][1] / 128)
+            mul(col(CA), col(E0), STEP[w][l][0])
+            act(col(CB), col(E1), AF.Identity, col(CA), (0.0, -3840.0, 3840.0)[l])
+            act(ap("Cj", 24 * w + l, 24 * w + 24, 3), ap("ONE", 0, 8), AF.Identity, 0.0, col(CB))
+    ms(ap("LT"), 1.0)
+    for k in range(8):
+        if OPT["t"][k] == "V":
+            mul(ap("LT", 32 * k, 32 * k + 32), ap("ONE", 0, 32), col(E0))
+    for k in range(2):
+        ts(ap("DW%d" % k, 0, 16), ap("J64", 48, 64), col(P64), ALU.is_equal, col((HH0, HH1)[k]), ALU.mult)
+        ts(ap("DW%d" % k, 16, 160), ap("J64", 0, 144), col(P64), ALU.is_equal, col((HH0, HH1)[k]), ALU.mult)
 
-    def swap(bank, lo, n, src, f32, extra=None):
+    def swap(bank, lo, n, src, pat, extra=None):
         it = []
         for c in range(2):
-            pr = [(sl("W%d%s" % (c, "f" if f32 else ""), 16 * (h - c)), src(h)) for h in range(2)]
+            pr = [(sl("%s%d" % (pat, c), 16 * (h - c)), src(h)) for h in range(2)]
             if extra is not None:
                 pr.append((I_, extra(c)))
             it += grp(ps(bank, lo + c, lo + 2 * n, 2), pr)
         mm(it)
 
-    def turn(src, tmp, out, lst="l8"):
+    def spread(tmp, src, lst="l8"):
         tt(tmp, ind(src, ap(lst)), ap("Ma"), ALU.mult)
-        mm(grp(out, [(tmp, ap("Rb"))]))
 
-    ts(ap("l8"), ap("Jb", 0, 128, 16), 1.0 / 256, ALU.mult)
-    if OPT["h"] == "T":
-        ts(ap("l8a"), ap("Jb", 0, 128, 16), 1.0 / 128, ALU.mult)
-        ts(ap("l8b"), ap("Jb", 0, 128, 16), 1.0 / 128, ALU.mult, 1.0, ALU.add)
-        ts(ap("LT"), ap("J160", 16, 144), col(E1X), ALU.mult, col(N1), ALU.add)
-        cp(ap("RT", 0, 128), ap("R3a"))
-        cp(ap("RT", 128, 256), ap("R3a"))
-        ts(col(E2X), col(E2), 120.0 * 4096, ALU.mult)
-        ts(ap("RT", 256, 384), ap("R3a"), col(E2X), ALU.add)
-        cp(ap("WD", 0, 8), ap("F4", 16, 144, 16))
-        cp(ap("WD", 8, 16), ap("Frm", 16, 144, 16))
-    ts(ap("Ma"), ap("KI2"), col(K_), ALU.is_equal)
-    ts(ap("Rb"), ap("Jg", 0, 128, 16), col(G16), ALU.is_equal)
+    def child_list(tmp, out):
+        mm(grp(out, [(tmp, ap("Rbn")), (row("ONE"), row("CS", 0, 8)), (row("NEG"), row("CS", 0, 8)), (tmp, ap("Rb")), (I_, ap("c16"))]))
 
-    for k in range(2):
-        ts(ps(2 + k, 0, 384), ap("qki", 384 * k, 384 * k + 384), 4096.0, ALU.mult, 2048.5, ALU.add)
-        tt(ap("V0", 384 * k, 384 * k + 384), ps(2 + k, 0, 384), ap("qni", 384 * k, 384 * k + 384), ALU.add)
-    cp(ap("tub", p=(0, 8)), ap("tui", p=(0, 8)))
-    mm(grp(ps(7, 0, 48), [(ap("G8", 16 - a, 144 - a, 1, (0, 8)), ap("tub", a, 768, 16, (0, 8))) for a in range(16)]))
-    ts(ap("Pt"), ps(7, 0, 48), 1024.0, ALU.mult)
-    tt(ap("Pc"), ap("Pt"), ap("PC"), ALU.add)
+    def both(bank, src, out, eng):
+        mm([(ps(bank, 128 * r, 128 * r + 128), of(r)("Dup"), src, True) for r in range(2)])
+        cp(out, ps(bank, 0, 256), eng)
 
-    def least(src, dst):
-        tt(ap("mn"), src(0), src(1), ALU.min)
-        tt(ap("mni"), ap("mn"), src(2), ALU.min)
-        ts(ap("mnj"), ap("mni"), 1023, ALU.bitwise_and)
-        cp(dst, ap("mnj"))
+    def least(u, src, dst):
+        tt(u("mn"), src(0), src(1), ALU.min)
+        tt(u("mn2"), u("mn"), src(2), ALU.min)
+        ts(u("mn"), u("mn2"), 1.5 * BIG, ALU.add, 1.5 * BIG, ALU.subtract)
+        tt(dst, u("mn2"), u("mn"), ALU.subtract)
 
-    least(lambda l: ap("Pc", 16 * l, 16 * l + 16), ap("elf"))
+    def counters(u, V, go):
+        tt(u("Pt"), ind(go, ap("l3", 0, 2)), u(V, PM, PM + 32), ALU.mult)
+        tt(u("Pc"), u("Pt"), u(V, PB, PB + 32), ALU.add)
+
+    for l in range(3):
+        cp(ap("tub", p=(32 * l, 32 * l + 16)), ap("tui", p=(32 * l, 32 * l + 16)))
     for c in range(2):
-        mm(grp(ps(c, 0, 128), [(ap("gli", 128 * c, 128 * c + 128), I_)]))
-        act(ap("GT0", 128 * c, 128 * c + 128), ps(c, 0, 128), AF.Identity, 0.0, -1.0)
+        u = of(c)
+        b0 = 4 * c
+        for l in range(3):
+            p = (32 * l, 32 * l + 16)
+            mm(grp(ps(b0, 8 * l, 8 * l + 8), [(u("Gt", 16 - a, 144 - a, 1, p), ap("tub", a, 128, 16, p)) for a in range(16)]), also=[ps(b0, 0, 24)])
+        ms(u("Pc", 24, 32), 0.0)
+        tt(u("Pc", 0, 24), ps(b0, 0, 24), ap("PC", 0, 24), ALU.add)
+        least(u, lambda l: u("Pc", 8 * l, 8 * l + 8), u("elf"))
+        ts(ps(b0 + 1, 0, 384), u("qki"), 4096.0, ALU.mult, 2048.5, ALU.add)
+        tt(u("V0", 0, 384), ps(b0 + 1, 0, 384), u("qni"), ALU.add)
+        mm([(ps(b0 + 2, 64 * r, 64 * r + 64), ap("gli", 128 * r, 128 * r + 128), ap("W", 16 + 64 * c, 80 + 64 * c), True) for r in range(2)])
+        mul(u("GT0"), ps(b0 + 2, 0, 128), -1.0)
+        mm([(ps(b0 + 3, 0, 1), u("Dup"), ap("rmb", 0, 1), True)])
+        cp(u("rmf", 0, 1), ps(b0 + 3, 0, 1), "A")
+        mul(u("r32", 0, 1), u("rmf", 0, 1), -32.0)
+        mul(u("Brm"), ap("B4"), u("rmf", 0, 1))
+        ts(u("WD", 0, 24), ap("Jx"), col(G16), ALU.is_equal, col(N32), ALU.mult)
+        ts(ap("W2"), ap("Jx"), col(G2), ALU.is_equal, u("r32", 0, 1), ALU.mult)
+        tt(u("WD", 0, 24), u("WD", 0, 24), ap("W2"), ALU.add)
+        for l in range(3):
+            mul(u("WK", l, 24, 3), ap("Rb"), col(R15))
+        tt(u("WK", 0, 24), u("WK", 0, 24), u("WD", 0, 24), ALU.add)
+        for k in range(16):
+            mul(u("WX0", k, 384, 16), u("WK", 0, 24), ap("CK", k, k + 1))
+        mul(u("WD", 0, 24), u("WD", 0, 24), -1.0)
+        if "X" in OPT["e"][4 * c:4 * c + 4]:
+            ms(u("xs"), 0.0)
+        ms(u("D2", 384, VW), 0.0)
+        ms(view("o3%d" % c, T["o3%d" % c][:, :, :], 16), 0.0)
+        cp(u("ncol", 0, 1), col(K37), "A")
     send([ap("GT0")], [(k, ap("GT%d" % k), "ag%d" % k) for k in range(1, N)], "lg", 4000)
 
-    def counters(V, go):
-        for l in range(3):
-            tt(ap("Pt", 16 * l, 16 * l + 16), ap(V, PM + 16 * l, PM + 16 * l + 16), go, ALU.mult)
-        tt(ap("Pc"), ap("Pt"), ap(V, PB, PB + 48), ALU.add)
-
-    for t in range(RO):
-        V, GT, SY, LY = "V%d" % t, "GT%d" % t, "SY%d" % t, "LY%d" % t
-        now[0] = t
-        h8 = lambda name, c: ap(name, 8 * c, 8 * c + 8)
-        h128 = lambda name, c: ap(name, 128 * c, 128 * c + 128)
-        for l in range(3):
-            a3 = lambda name: ap(name, 256 * l, 256 * l + 256)
-            if OPT["kr"][l] == "A":
-                act(a3("KT"), a3(V), AF.Identity, RC)
-                act(a3("KR"), a3("KT"), AF.Identity, -RC)
-            else:
-                ts(a3("KR"), a3(V), RC, ALU.add, RC, ALU.subtract)
-            tr(a3("KT"), a3("KR"))
-            scan(a3("KM"), ap("dmax"), a3("KT"), ALU.add, ALU.max)
-        for c in range(2):
-            if t > 0:
-                tt(h8("elt", c), ap("LY%d" % (t - 1), 128 + 8 * c, 136 + 8 * c), ap(V, ED + 8 * c, ED + 8 * c + 8), ALU.mult)
-                tt(h8("elf", c), h8("elt", c), ap(V, EB + 8 * c, EB + 8 * c + 8), ALU.add)
-            cp(h8("elu", c), h8("elf", c))
-            cp(h128("Ve", c), ind(ap(V, 0, 768), h8("elu", c)), OPT["ve"][c])
-            if OPT["en"][c] == "A":
-                cp(h128("E", c), ind(ap("KR"), h8("elu", c)), "A")
-            else:
-                ts(h128("E", c), h128("Ve", c), RC, ALU.add, RC, ALU.subtract)
-            tt(h128("Ne", c), h128("Ve", c), h128("E", c), ALU.subtract)
-            ts(h128("q16", c), h128("Ne", c), 2047.5, ALU.add)
+    def step(t, c):
+        V, GT, SY, LY, S, O3 = "V%d" % t, "GT%d" % t, "SY%d" % t, "LY%d" % t, "S%d" % c, "o3%d" % c
+        end = t == RO - 1
+        u = of(c)
+        ba, bf = 4 * c, 4 * c + 1
+        k0, k1 = ba, bf
         if t > 0:
-            counters(V, ap("LY%d" % (t - 1), 128, 144))
-        tt(ap("jv"), ap("elf"), ap("iL"), ALU.subtract)
+            go = u("LY%d" % (t - 1), 128, 136)
+            tt(u("elt"), go, u(V, ED, ED + 8), ALU.mult)
+            tt(u("elf"), u("elt"), u(V, EB, EB + 8), ALU.add)
+        ts(u("elu"), u("elf"), 1024.0, ALU.mult)
+        ts(u("Vi"), ind(u(V, 0, 384), u("elu")), 2047.5, ALU.add)
+        ts(u("Ni"), u("Vi"), 4095, ALU.bitwise_and)
+        cp(u("q16"), u("Ni"))
+        if inps:
+            cp(u("Ve"), ind(u(V, 0, 384), u("elu")), "A")
+        else:
+            ts(u("Ki"), u("Vi"), 0x7FF000, ALU.bitwise_and)
+        ts(u("Ne"), u("Ni"), -2047.5, ALU.add)
+        if t > 0:
+            counters(u, V, go)
+        tt(u("m1"), ind(u("elf"), ap("l3", 0, 2)), ap("PC"), ALU.is_equal)
+        tt(u(V, PB, PB + 32), u("Pc"), u("m1"), ALU.add)
+        mul(u(V, PM, PM + 32), u("m1"), -3.0)
+        if not end:
+            least(u, lambda l: u(V, PB + 8 * l, PB + 8 * l + 8), u(V, EB, EB + 8))
+            tt(u(V, ED, ED + 8), u("elf"), u(V, EB, EB + 8), ALU.subtract)
+        for k in range(4):
+            cp(u("s", 512 * k, 512 * k + 512), ind(ap(S, 0, 4096), u("q16", 32 * k, 32 * k + 32)), OPT["s"][4 * c + k])
+        cp(u("gmj"), ind(ap("JM"), u("elu")), OPT["gj"][c])
+        mm(grp(ps(bf, 384, 432), [(u("gmj"), ap("Rj")), (u("LT", p=(0, 2)), row("Cj", n=2))]))
+        if inps:
+            mm(grp(ps(k0, 0, 128), [(ap("If"), u("Ve")), (row("ONE"), row("RCt", 0, 128)), (row("NEG"), row("RCt", 0, 128)), (row("KS"), row("ONE"))]), last=False)
+        for hf in range(2):
+            o = 1024 * hf
+            mm(grp(ps(k0, 64 * hf, 64 * hf + 64), [(sl("Fmk", k), u("s", o + k, o + 1024, 16)) for k in range(16)], not inps), last=hf == 1 or not inps)
+        if inps:
+            tr(u("ZT"), ps(k0, 0, 128))
+            scan(u("ZM"), ap("dcap"), u("ZT"), ALU.max, ALU.min)
+            ts(u("Z"), ps(k0, 0, 128), col(K128), ALU.subtract, 2.0 ** 22, ALU.min)
+        else:
+            tt(u("Z"), u("Ki"), ps(k0, 0, 128), ALU.max)
+            tr(u("ZT"), u("Z"))
+            scan(u("ZM"), ap("dmin"), u("ZT"), ALU.add, ALU.min)
+        z15 = u("ZM", 15, 128, 16)
+        ts(u("k0t"), z15, RC, ALU.add, RC, ALU.subtract)
+        tt(u("k0b", 0, 8), z15, u("k0t"), ALU.subtract)
+        swap(k0, 128, 4, lambda h: u("k0b", h, 8, 2), "W", lambda cc: ap("c16s", cc, 8, 2))
+        ts(u("lx"), ps(k0, 128, 136), 1.0 / 128, ALU.mult, K0, ALU.add)
+        if OPT["x"][c] == "A":
+            act(u("x"), ind(u("s"), u("lx")), AF.Identity, col(R15), col(NZ))
+        else:
+            ts(u("x"), ind(u("s"), u("lx")), col(NZ), ALU.mult, col(R15), ALU.add)
+        for o in range(0, 2048, 512):
+            scan(u("sm", o, o + 512), ap("k16"), u("s", o, o + 512), ALU.mult, ALU.max)
+        uv = ps(k1, 0, 8)
+        if OPT["uv"][c] == "D":
+            mm(grp(uv, [(sl("Fone", a), u("sm", 15 + 16 * a, 2048, 256)) for a in range(16)]), last=False)
+            mm(grp(uv, [(sl("Fcf", a), u("x", a, 128, 16)) for a in range(16)], False))
+        else:
+            mm(grp(uv, [(u("sm", 15, 2048, 16), ap("Fone", 16, 144, 16)), (u("x"), ap("Fcf", 16, 144, 16))]))
+        cp(u("opi"), uv)
+        mm(grp(ps(ba, 0, 128), [(ap("Bcf"), u("x"))]))
+        mm(grp(ps(ba, 128, 256), [(u("x"), ap("Inz"))]) + grp(ps(ba, 256, 384), [(ap("Inz"), u("x")), (u(GT), I_)]))
+        act(u("ub"), ps(ba, 0, 128), AF.Identity, 32.0)
+        ts(u("opj"), u("opi"), 511, ALU.bitwise_and)
+        if OPT["uv"][c] == "D":
+            cp(u("lo"), u("opj"))
+        else:
+            spread(u("gm"), u("opj"))
+            mm(grp(ps(k1, 8, 16), [(u("gm"), ap("Rb"))]))
+            cp(u("lo"), ps(k1, 8, 16))
+        tt(u("pn"), ind(ap("OT%d" % c), u("lo")), u("ub"), ALU.mult)
+        ts(u("pn2"), u("pn"), 5, ALU.arith_shift_right, 4095, ALU.bitwise_and)
+        ts(u("n16"), u("pn2"), u("ncol", 0, 1), ALU.add)
+        cp(u("xT"), ps(ba, 128, 256), "A")
+        act(u("HS", 0, 128), ps(ba, 256, 384), AF.Abs, col(R15))
+        ts(u("HS", 128, 256), u("HS", 0, 128), 6.0, ALU.is_gt, 16.0, ALU.mult)
+        tt(ind(u(V, 0, 384), u("elu")), u("Z"), u("Ne"), ALU.add)
         for l in range(3):
-            ts(ap("m1", 16 * l, 16 * l + 16), ap("jv"), 256.0 * l, ALU.is_equal, 1024.0, ALU.mult)
-        tt(ap(V, PB, PB + 48), ap("Pc"), ap("m1"), ALU.add)
-        act(ap(V, PM, PM + 48), ap("m1"), AF.Identity, 0.0, -3.0)
-        act(pen(1), ap("m1"), AF.Identity, BIG, -BIG / 1024)
-        act(pen(0, None, 1), ap("m1", 32, 48), AF.Identity, BIG, -BIG / 1024)
-        if t < RO - 1:
-            least(lambda l: ap(V, PB + 16 * l, PB + 16 * l + 16), ap(V, EB, EB + 16))
-            tt(ap(V, ED, ED + 16), ap("elf"), ap(V, EB, EB + 16), ALU.subtract)
-        for k in range(8):
-            o = 512 * k
-            cp(ap("s", o, o + 512), ind(ap("S", 0, 4096), ap("q16", o // 16, o // 16 + 32)), OPT["s"][k])
-        for c in range(2):
-            mb = 5 + c
-            o = 2048 * c
-            for hf in range(2):
-                oo = o + 1024 * hf
-                mm(grp(ps(mb, 64 * hf, 64 * hf + 64), [(sl("Fmk", k), ap("s", oo + k, oo + 1024, 16)) for k in range(16)]))
-            tt(h128("Z", c), h128("E", c), ps(mb, 0, 128), ALU.max)
-            tr(h128("ZT", c), h128("Z", c))
-            scan(h128("ZM", c), ap("dmin"), h128("ZT", c), ALU.add, ALU.min)
-            ts(h8("k0i", c), ap("ZM", 128 * c + 15, 128 * c + 128, 16), 1.0 / 256, ALU.mult, 15.0, ALU.add)
-            ts(h8("k0j", c), h8("k0i", c), 15, ALU.bitwise_and)
-            cp(h8("k0b", c), h8("k0j", c))
-            swap(mb, 128, 4, lambda h: ap("k0b", 8 * c + h, 8 * c + 8, 2), False, lambda cc: ap("c16", cc, 8, 2))
-            cp(h8("lx", c), ps(mb, 128, 136))
-            cp(h128("x", c), ind(ap("s", o, o + 2048), h8("lx", c)), OPT["x"][c])
-            for hf in range(2):
-                oo = o + 1024 * hf
-                scan(ap("sm", oo, oo + 1024), ap("k16"), ap("s", oo, oo + 1024), ALU.mult, ALU.max)
-            uv = ps(7, 0, 8)
-            mm(grp(uv, [(ap("sm", o + 15, o + 2048, 16), ap("Fone", 16, 144, 16)), (h128("x", c), ap("Fcf", 16, 144, 16))]))
-            mm(grp(ps(mb, 0, 128), [(ap("Bcf"), h128("x", c))]))
-            cp(h8("opi", c), uv)
-            act(h128("ub", c), ps(mb, 0, 128), AF.Identity, 32.0)
-            ts(h8("opj", c), h8("opi", c), 511, ALU.bitwise_and)
-            turn(h8("opj", c), h128("gm", c), ps(7, 8, 16))
-            cp(h8("lo", c), ps(7, 8, 16))
-            tt(h128("pn", c), ind(ap("OT"), h8("lo", c)), h128("ub", c), ALU.mult)
-            ts(h128("pn2", c), h128("pn", c), 5, ALU.arith_shift_right, 4095, ALU.bitwise_and)
-            ts(h128("n16", c), h128("pn2", c), ap("ncol", 0, 1), ALU.add)
-            if "A" in OPT["e"][4 * c:4 * c + 4]:
-                mm(grp(ps(mb, 128, 256), [(h128("x", c), ap("Inz"))]))
-                cp(h128("xT", c), ps(mb, 128, 256), "A")
-            if "V" in OPT["e"][4 * c:4 * c + 4]:
-                act(ap("xs", o, o + 2048, 16), h128("x", c), AF.Identity, 0.0, col(NZ))
-            mm(grp(ps(mb, 0, 128), [(ap("Inz"), h128("x", c)), (h128(GT, c), I_)]))
-            hs = lambda l, c=c: ap("HS", 256 * l + 128 * c, 256 * l + 128 * c + 128)
-            act(hs(0), ps(mb, 0, 128), AF.Abs)
-            act(hs(2), ps(mb, 0, 128), AF.Abs, 0.0, ap("rmf", 0, 1))
-            ts(hs(1), hs(0), 6.0, ALU.is_gt, 16.0, ALU.mult)
-        act(ap("xm"), ap("x"), AF.Identity, col(R15), col(NZ))
-
-        def distances_of_x():
-            mm(grp(ps(4, 0, 48), [(sl("F4", a), ap("HS", a, 768, 16)) for a in range(16)]))
-            tt(ap("hx3"), ps(4, 0, 48), pen(1), ALU.add)
-            tt(ap("hx2"), ap("hx3", 0, 16), ap("hx3", 16, 32), ALU.min)
-            tt(ap("hx1"), ap("hx2"), ap("hx3", 32, 48), ALU.min)
+            mm(grp(ps(bf, 128 * l, 128 * l + 128), [(u(V, 128 * l, 128 * l + 128), ap("If")), (row("ONE"), row("RCt", 0, 128)), (row("NEG"), row("RCt", 0, 128))]))
+        scan(u("KM"), ap("dmax"), ps(bf, 0, 384), ALU.add, ALU.max)
+        if end:
+            act(u("VO"), u(V, 0, 384), AF.Identity, -2048.5)
 
         def queues():
-            late = []
-            for c in range(2):
-                tt(ind(ap(V, 0, 768), h8("elu", c)), h128("Z", c), h128("Ne", c), ALU.add)
-            for l in range(3):
-                a3 = lambda name: ap(name, 256 * l, 256 * l + 256)
-                nb = 6
-                o = 256 * (l % 2) if OPT["d"][l] == "A" else 0
-                it = grp(ps(nb, o, o + 256), [(ap("B4"), a3("HS"))])
-                it += [(ps(nb, o + 128 * c, o + 128 * c + 128), ap("C128", p=(0, 17 + 2 * t + c)), ap("CR", p=(0, 17 + 2 * t + c)), False) for c in range(2)]
-                if OPT["d"][l] == "A":
-                    late.append((l, o, it + [(ps(nb, o, o + 256), ap("NIf"), a3(V), False)]))
-                    continue
-                mm(it)
-                tt(a3("D"), ps(nb, 0, 256), a3(V), ALU.subtract)
-            scan(ap("KM", 768, 1024), ap("dmax"), ap("ZT"), ALU.add, ALU.max)
-            ts(ap("wi"), ap("KM", 15, 1024, 16), -1.0 / 256, ALU.mult, 32783.0, ALU.add)
-            ts(ap("wj"), ap("wi"), 15, ALU.bitwise_and)
-            cp(ap("wb"), ap("wj"))
-            swap(7, 0, 24, lambda h: ap("wb", h, 48, 2), False)
-            for l in range(3):
-                swap(7, 48 + 16 * l, 8, lambda h: ap("wb", 48 + h, 64, 2), False)
-            tt(ap("w1"), ps(7, 0, 48), ap("m1"), ALU.add)
-            tt(ap("w2"), ps(7, 48, 96), pen(1), ALU.add)
-            tt(ap("w1"), ap("w1"), ap("w2"), ALU.min)
-            cp(ap("lw"), ap("w1"))
-            for l in range(3):
-                if OPT["d"][l] == "V":
-                    tt(ap("D2", 256 * l, 256 * l + 256), ind(ap("Tm"), ap("lw", 16 * l, 16 * l + 16)), ap("D", 256 * l, 256 * l + 256), ALU.mult)
-            for l, o, it in late[:2]:
-                mm(it)
-            for k, (l, o, it) in enumerate(late):
-                cp(ap("D", 256 * l, 256 * l + 256), ind(ap("Tm"), ap("lw", 16 * l, 16 * l + 16)), "A")
-                if k == 2:
-                    mm(it)
-                tt(ap("D2", 256 * l, 256 * l + 256), ps(6, o, o + 256), ap("D", 256 * l, 256 * l + 256), ALU.mult)
-            if t < RO - 1:
-                send([ap(V), ap("D2")], [(1, ap("V%d" % (t + 1)), "av%d" % (t + 1))], "lv%d" % (t + 1), 7000)
+            k15 = u("KM", 15, 384, 16)
+            ts(u("wt"), k15, RC, ALU.add, RC, ALU.subtract)
+            tt(u("RW", 0, 24), k15, u("wt"), ALU.subtract)
+            if OPT["sq"] == "A":
+                act(u("RW", 32, 56), u("RW", 0, 24), AF.Square)
             else:
-                act(ap("VO"), ap(V, 0, 768), AF.Identity, -2048.5)
-                dma("S", "oq0", T.yq[:], T["VO"][:], [ap("VO")], [ap("qki")], 3500)
-                dma("G", "oq1", T.yq[:], T["D2"][:, 0:768], [ap("D2"), ap("qki")], [], 4500, accum_op=ALU.add)
-
-        def mark_lists():
-            swap(7, 0, 8, lambda h: ap("k0b", h, 16, 2), False)
-            cp(ap("lk"), ps(7, 0, 16))
-            tt(ap("MN"), ind(ap("Tm"), ap("lk")), ap("Ne"), ALU.mult)
+                tt(u("RW", 32, 56), u("RW", 0, 24), u("RW", 0, 24), ALU.mult)
+            p65 = (0, 65)
+            qw = lambda l: ap("QW", 128 * l, 128 * l + 128, 1, p65)
+            mm([(ps(ba, 384, 512, 1, p65), u("RW", 0, 65), I_, True)])
+            mul(u("RWT", p=p65), ps(ba, 384, 512, 1, p65), col(SQ, p65))
+            M = u("VO") if end else u(V, 0, 384)
+            n = (2 if end else 18) + 2 * t
             it = []
-            for h in range(2):
-                it += grp(ps(7, 256 * h, 256 * h + 256), [(I_, ap("Tri")), (ap("H%d" % h), ap("MN"))])
+            for l in range(3):
+                it += grp(ps(ba, 128 * l, 128 * l + 128), [(qw(l), u("RWT", p=p65)), (u("Brm") if l == 2 else ap("B4"), u("HS", 128 * (l % 2), 128 * (l % 2) + 128)),
+                                                           (row("ONR", n=n), row("CR0" if end else "CR", n=n))])
             mm(it)
-            tr(ap("XT"), ps(7))
-            ts(ap("o2"), ap("XT", 0, 512, 32), -16384.0, ALU.add)
-            for k in range(16):
-                if OPT["eq"][k] == "A":
-                    act(ap("EQ", 32 * k, 32 * k + 32), ps(7, 32 * k, 32 * k + 32), AF.Abs, ap("o2", k, k + 1), -1.0)
-                else:
-                    ts(ap("EQ", 32 * k, 32 * k + 32), ps(7, 32 * k, 32 * k + 32), ap("o2", k, k + 1), ALU.not_equal)
-            scan(ap("EM"), ap("d32"), ap("EQ"), ALU.add, ALU.min)
-            ts(ap("o1"), ap("EM", 31, 512, 32), -8192.0, ALU.mult, col(DC), ALU.add)
-            tt(ap("o3"), ap("o1"), ap("o2"), ALU.max)
-            swap(7, 0, 8, lambda h: ap("o3", 8 * h, 8 * h + 8), True)
-            ts(ap("lm"), ps(7, 0, 16), 2047.5, ALU.add)
-
-        def before_turned(c):
-            hb = 4 + c
-            if OPT["gj"][c] == "A":
-                for k in range(8):
-                    act(ap("gmj", 128 * c + 16 * k, 128 * c + 16 * k + 16), ap("Ma", 0, 16), AF.Identity, 0.0, ap("jv", 8 * c + k, 8 * c + k + 1))
-                mm(grp(ps(hb, 0, 8), [(h128("gmj", c), ap("Rb"))]))
+            tt(M, M, ps(ba, 0, 384), ALU.min)
+            if end:
+                act(M, M, AF.Abs)
+                dma("S", "oq%d" % c, [(T.yq[half(c), 256 * l + 128 * r:256 * l + 128 * r + 128], u("VO", 128 * l, 128 * l + 128, 1, (64 * r, 64 * r + 64))[3])
+                                      for r in range(2) for l in range(3)], [M], [], 3000)
             else:
-                turn(h8("jv", c), h128("gmj", c), ps(hb, 0, 8))
-            for k, l in enumerate((2, 1, 0, 2, 1)):
-                act(ap("penT", 48 * c + 8 * k, 48 * c + 8 * k + 8), ps(hb, 0, 8), AF.Abs, -BIG * l, BIG / 256)
-            it = []
-            for k, l in enumerate((0, 2, 1)):
-                it += grp(ps(hb, 8 * k, 8 * k + 8), [(ap("HS", 256 * l + 128 * c, 256 * l + 128 * c + 128), ap("F4", 16, 144, 16))])
-            mm(it)
-            tt(ap("hx3", 24 * c, 24 * c + 24), ps(hb, 0, 24), ap("penT", 48 * c + 16, 48 * c + 40), ALU.add)
-            tt(h8("hx2", c), ap("hx3", 24 * c, 24 * c + 8), ap("hx3", 24 * c + 8, 24 * c + 16), ALU.min)
-            tt(h8("hx1", c), h8("hx2", c), ap("hx3", 24 * c + 16, 24 * c + 24), ALU.min)
+                act(u("D2", 0, 384), ps(ba, 0, 384), AF.Relu, 0.0, -2.0)
+                send([u(V), u("D2")], [(1, u("V%d" % (t + 1)), "av%d_%d" % (t + 1, c))], "lv%d_%d" % (t + 1, c), 4500)
 
-        def finish_turned(c, sign):
-            hb, o = 4 + c, 2048 * c
-            rows = (0, 3 if sign else 2)
-            mm(grp(ps(hb, 0, 384), [(ap("LT", p=rows), ap("RT", p=rows))]), last=False)
-            mm([(ps(hb, k, 256, 16), ap("df", o + k, o + 2048, 16), ap("WD"), False) for k in range(16)], last=False)
-            mm([(ps(hb, 256 + k, 384, 16), ap("tf", o + k, o + 2048, 16), ap("F8" if sign else "F4", 16, 144, 16), False) for k in range(16)])
-            o = 384 * c
-            scan(ap("RM", o, o + 384), ap("dres"), ps(hb, 0, 384), ALU.add, ALU.min)
-            r15 = ap("RM", o + 15, o + 384, 16)
-            tt(ap("TT", 48 * c + 1, 48 * c + 48, 2), r15, ap("penT", 48 * c, 48 * c + 24), ALU.add)
-            tt(ap("TT", 48 * c, 48 * c + 48, 2), r15, ap("penT", 48 * c + 16, 48 * c + 40), ALU.add)
-            h16 = lambda name: ap(name, 16 * c, 16 * c + 16)
-            tt(h16("T2"), ap("TT", 48 * c, 48 * c + 16), ap("TT", 48 * c + 16, 48 * c + 32), ALU.min)
-            tt(h16("ri"), h16("T2"), ap("TT", 48 * c + 32, 48 * c + 48), ALU.min)
-            ts(h16("rj"), h16("ri"), 4095, ALU.bitwise_and)
-            turn(h16("rj"), h128("gmb", c), ps(hb, 384, 392), "l8b")
-            tt(h8("goT", c), ap("ri", 16 * c, 16 * c + 16, 2), h8("hx1", c), ALU.is_lt)
-            turn(h8("goT", c), h128("gmg", c), ps(hb, 392, 400))
-            cp(h8("lb", c), ps(hb, 384, 392))
-            cp(ap(SY, 128 + 8 * c, 136 + 8 * c), ps(hb, 392, 400))
-            cp(ap(SY, 144 * c, 144 * c + 128), ind(ap("y", 2048 * c, 2048 * c + 2048), h8("lb", c)), OPT["yb"][c])
-            send([ap(SY, 136 * c, 136 * c + 136)], [(1, ap(LY, 136 * c, 136 * c + 136), "ay%d_%d" % (t, c))], "ly%d_%d" % (t, c), 2500)
-            turn(h16("rj"), h128("gma", c), ps(hb, 400, 408), "l8a")
-            cp(h8("la", c), ps(hb, 400, 408))
+        def marks():
+            swap(ba, 0, 4, lambda h: u("k0b", h, 8, 2), "W")
+            ts(u("lk"), ps(ba, 0, 8), 1.0 / 128, ALU.mult, K0, ALU.add)
+            both(ba, u("x"), u("xd"), "A")
+            tt(u("MN"), ind(ap("Tm"), u("lk")), u("Ni"), ALU.mult)
+            mm([(ps(ba, 128 * h, 128 * h + 128), ap("H%d" % h), u("MN"), True) for h in range(2)])
+            tr(u("XT"), ps(ba, 0, 256))
+            tt(u("EQ"), ps(ba, 0, 256), u("XT"), ALU.is_equal)
+            scan(u("EM"), ap("dgt"), u("EQ"), ALU.mult, ALU.add)
+            ts(u("o1"), u("EM", 31, 256, 32), 1.5, ALU.is_ge, col(DC), ALU.mult)
+            for r in range(2):
+                p = (64 * r, 64 * r + 64)
+                tt(view(O3, T[O3][half(r), :, 4 * r:4 * r + 4], 8), u("o1", p=p), u("XT", 0, 256, 32, p), ALU.max)
+            swap(ba, 0, 8, lambda h: view(O3, T[O3][:, h, :], 8), "DW")
+            cp(u("lm"), ps(ba, 0, 16))
+            for k in range(8):
+                cp(ind(ap(S), u("lm", 2 * k, 2 * k + 2)), u("xd", 32 * k, 32 * k + 32))
 
-        if OPT["h"] == "T":
-            before_turned(0)
-            before_turned(1)
+        mm(grp(ps(bf, 0, 384), [(u("HS", 0, 128), u("WX0")), (u("HS", 128, 256), ap("WX1"))]), last=False)
+        for q in range(5):
+            if q == OPT["qat"]:
+                queues()
+            if q == OPT["mat"]:
+                marks()
+            if q == 4:
+                break
+            ch = lambda name: u(name, 512 * q, 512 * q + 512)
+            p32 = (32 * q, 32 * q + 32)
+            eg = ind(ap("EF%d" % c), u("n16", 32 * q, 32 * q + 32))
+            if OPT["e"][4 * c + q] == "X":
+                mul(u("xs", 0, 512, 16), u("x", 32 * q, 32 * q + 32), col(NZ))
+                scan(u("xb"), ap("k16"), u("xs"), ALU.mult, ALU.add)
+                tt(ch("e"), eg, u("xb"), ALU.add)
+                ts(ch("y"), ch("e"), 0.0, ALU.max, 63.0, ALU.min)
+            else:
+                cp(ch("e"), eg, OPT["e"][4 * c + q])
+                mm(grp(ps(2 + q % 2), [(u("xT", p=p32), ap("R", p=p32)), (I_, ch("e"))]))
+                ts(ch("y"), ps(2 + q % 2), 0.0, ALU.max, 63.0, ALU.min)
+            mm(grp(ps(6 + q % 2), [(u(GT, p=p32), ap("R", p=p32)), (I_, ch("y"))]))
+            act(ch("df"), ps(6 + q % 2), AF.Abs)
+            if OPT["t"][4 * c + q] == "A":
+                act(ch("tf"), ch("df"), AF.Sign, col(M65))
+            else:
+                ts(ch("tf"), ch("df"), 6.0, ALU.is_gt, 2.0, ALU.mult)
+        cuts = OPT["cuts"]
+        for a, b in zip(cuts, cuts[1:]):
+            mm([(ps(bf, k, 384, 16, (a, b)), u("df", 16 * a + k, 16 * b, 16), u("WD", 0, 24), False) for k in range(16)], last=False)
+            mm([(ps(bf, k, 384, 16, (a, b)), u("tf", 16 * a + k, 16 * b, 16), ap("WT"), False) for k in range(16)], last=b == 128)
+        scan(u("RM"), ap("dres"), ps(bf, 0, 384), ALU.add, ALU.min)
+        r15 = u("RM", 15, 384, 16)
+        scan(u("sb"), ps(bf, 408, 432), r15, ALU.add, ALU.min)
+        scan(u("sa"), ps(bf, 384, 408), r15, ALU.add, ALU.min)
+        if OPT["b"] == "P":
+            spread(u("gmb"), u("sb"), "l8s")
+            spread(u("gma"), u("sa"), "l8s")
+            child_list(u("gmb"), ps(bf, 432, 440))
         else:
-            distances_of_x()
-        for c in range(2):
-            for q in range(4):
-                k = 4 * c + q
-                if k == OPT["qat"]:
-                    queues()
-                if k == OPT["mat"]:
-                    mark_lists()
-                o = 512 * k
-                eg = ind(ap("EF"), ap("n16", 32 * k, 32 * k + 32))
-                Rq = ap("R", 512 * q, 512 * q + 512)
-                if OPT["e"][k] == "V":
-                    scan(ap("xb", o, o + 512), ap("k16", 0, 512), ap("xs", o, o + 512), ALU.mult, ALU.add)
-                    tt(ap("e", o, o + 512), eg, ap("xb", o, o + 512), ALU.add)
-                    ts(ap("y", o, o + 512), ap("e", o, o + 512), 0.0, ALU.max, 63.0, ALU.min)
-                else:
-                    b = bank[0] % 4
-                    bank[0] += 1
-                    cp(ap("e", o, o + 512), eg, "A")
-                    mm(grp(ps(b), [(h128("xT", c), Rq), (I_, ap("e", o, o + 512))]))
-                    ts(ap("y", o, o + 512), ps(b), 0.0, ALU.max, 63.0, ALU.min)
-                b = bank[0] % 4
-                bank[0] += 1
-                mm(grp(ps(b), [(h128(GT, c), Rq), (I_, ap("y", o, o + 512))]))
-                if OPT["h"] == "T":
-                    act(ap("df", o, o + 512), ps(b), AF.Abs)
-                    sign = OPT["t"][2 * c] == "A"
-                    if sign:
-                        act(ap("tf", o, o + 512), ap("df", o, o + 512), AF.Sign, col(M65))
-                    else:
-                        ts(ap("tf", o, o + 512), ap("df", o, o + 512), 6.0, ALU.is_gt, 16.0, ALU.mult)
-                    if q == 3:
-                        finish_turned(c, sign)
-                    continue
-                act(ap4("d", 2 * k, 2 * k + 2), ps(b), AF.Abs)
-                sign = OPT["t"][k // 2] == "A"
-                if sign:
-                    act(ap4("tt", 2 * k, 2 * k + 2), ap4("d", 2 * k, 2 * k + 2), AF.Sign, col(M65))
-                else:
-                    ts(ap4("tt", 2 * k, 2 * k + 2), ap4("d", 2 * k, 2 * k + 2), 6.0, ALU.is_gt, 16.0, ALU.mult)
-                if q % 2 == 1:
-                    hf = q // 2
-                    b0 = 8 * c + 4 * hf
-                    for l, (w, src) in ((0, ("F4", "d")), (2, ("Frm", "d")), (1, ("F8" if sign else "F4", "tt"))):
-                        rows = (0, 4 if w == "F8" else 3)
-                        pr = [(ap("L3", p=rows), ap("R3", 64 * hf, 64 * hf + 64, 1, rows))]
-                        pr += [(sl(w, a), ap4(src, b0, b0 + 4, a)) for a in range(16)]
-                        mm(grp(ps(4 + c, 128 * l + 64 * hf, 128 * l + 64 * hf + 64), pr))
-            if OPT["h"] == "T":
-                continue
-            o = 384 * c
-            scan(ap("RM", o, o + 384), ap("dres"), ps(4 + c, 0, 384), ALU.add, ALU.min)
-            r15 = ap("RM", o + 15, o + 384, 16)
-            tt(ap("TT", 48 * c + 1, 48 * c + 48, 2), r15, pen(0, c), ALU.add)
-            tt(ap("TT", 48 * c, 48 * c + 48, 2), r15, pen(1, c), ALU.add)
-            h16 = lambda name: ap(name, 16 * c, 16 * c + 16)
-            tt(h16("T2"), ap("TT", 48 * c, 48 * c + 16), ap("TT", 48 * c + 16, 48 * c + 32), ALU.min)
-            tt(h16("ri"), h16("T2"), ap("TT", 48 * c + 32, 48 * c + 48), ALU.min)
-            ts(h16("rj"), h16("ri"), 4095, ALU.bitwise_and)
-            cp(h8("lb", c), ap("rj", 16 * c + 1, 16 * c + 16, 2))
-            yw = ap("y", 2048 * c, 2048 * c + 2048)
-            cp(ap(SY, 144 * c, 144 * c + 128), ind(yw, h8("lb", c)), OPT["yb"][c])
-            tt(ap(SY, 128 + 8 * c, 136 + 8 * c), ap("ri", 16 * c, 16 * c + 16, 2), h8("hx1", c), ALU.is_lt)
-            cp(h8("la", c), ap("rj", 16 * c, 16 * c + 16, 2))
-            send([ap(SY, 136 * c, 136 * c + 136)], [(1, ap(LY, 136 * c, 136 * c + 136), "ay%d_%d" % (t, c))], "ly%d_%d" % (t, c), 2500)
-        for k in range(8):
-            cp(ind(ap("S"), ap("lm", 2 * k, 2 * k + 2)), ap("xm", 32 * k, 32 * k + 32))
-        for c in range(2):
-            o = 256 * t + 128 * c
-            cp(ap("S", o, o + 128), ind(ap("y", 2048 * c, 2048 * c + 2048), h8("la", c)), OPT["ya"][c])
-        if t < RO - 1:
-            for c in range(2):
-                o = 256 * (RO + t) + 128 * c
-                cp(ap("S", o, o + 128), ap(LY, 144 * c, 144 * c + 128), OPT["ly"])
-            add("V", [lambda SY=SY: g.vector.tensor_reduce(T["gs"][:, 0:1], T[SY][:, 128:144], AxisListType.X, ALU.add)], 64.0,
-                [ap(SY, 128, 144)], [ap("gs", 0, 1)])
-            cp(ap("gsb", 0, 1), ap("gs", 0, 1), "A")
-            mm(grp(ps(4, 0, 1), [(ap("B1"), ap("gsb", 0, 1))]))
-            cp(ap("Ai", 0, 1), ps(4, 0, 1))
-            ts(ap("Aj", 0, 1), ap("Ai", 0, 1), 63, ALU.bitwise_and)
-            ts(ap("ncol", 0, 1), ap("Aj", 0, 1), col(K37), ALU.add)
+            ts(u("bt"), u("sb", 2, 24, 3), 1.5 * 2.0 ** 28, ALU.add, 1.5 * 2.0 ** 28, ALU.subtract)
+            tt(u("br", 0, 8), u("sb", 2, 24, 3), u("bt"), ALU.subtract)
+            spread(u("gmc"), u("br", 0, 8))
+            spread(u("gma"), u("sa"), "l8s")
+            mm(grp(ps(bf, 432, 440), [(I_, ap("c16")), (u("gmc"), ap("Rbb"))]))
+        mm(grp(ps(ba, 440, 448), [(ap("I4"), u("m1", 0, 8)), (I_, u("m1", 8, 16)), (u("gma"), ap("Rbs"))]))
+        cp(u("lb"), ps(bf, 432, 440))
+        ts(u(SY, 128, 136), ps(ba, 440, 448), 0.0, ALU.is_lt)
+        cp(u(SY, 0, 128), ind(u("y"), u("lb")), OPT["yb"][c])
+        send([u(SY, 0, 136)], [(1, u(LY, 0, 136), "ay%d_%d" % (t, c))], "ly%d_%d" % (t, c), 2500)
+        child_list(u("gma"), ps(k0, 0, 8))
+        cp(u("la"), ps(k0, 0, 8))
+        cp(u("ya"), ind(u("y"), u("la")), OPT["ya"][c])
+        both(k0, u("ya"), ap(S, 256 * t, 256 * t + 256), OPT["sa"][c])
+        if not end:
+            act(u("gsb", 0, 8), u(SY, 128, 136), AF.Identity, acc=u("gs", 0, 1))
+            gs = u("gs", 0, 1)
+            mm(grp(ps(ba, 0, 1), [(row("ONE"), row("CS", 9, 10)), (ap("B64n"), gs), (row("ONE"), row("CS", 8, 9)), (row("NEG"), row("CS", 8, 9)), (ap("B64"), gs)]))
+            act(u("ncol", 0, 1), ps(ba, 0, 1), AF.Identity, col(K37))
         else:
-            dma("S", "om", T.ym[:], T["S"][15:128:16, 2048:4096], [ap("S", 2048, 4096)], [], 2500)
-            dma("S", "os0", T.ys[:, 0:1792], T["S"][:, 0:1792], [ap("S", 0, 1792)], [], 4000)
-            for c in range(2):
-                dma("SA"[c], "os%d" % (c + 1), T.ys[:, 1792 + 128 * c:1920 + 128 * c], T[LY][:, 144 * c:144 * c + 128], [ap(LY, 136 * c, 136 * c + 136)], [], 2200)
-            counters(V, ap(SY, 128, 144))
-            tt(ap("Pt"), ap("Pc"), ap("PC"), ALU.subtract)
-            ts(ap("Pb"), ap("Pt"), 1.0 / 1024, ALU.mult)
-            for hf in range(2):
-                mm([(ps(5 + hf, a, 384, 16, (0, 8)), ap("W", 16 + a, 144, 16), ap("Pb", 24 * hf, 24 * hf + 24), True) for a in range(16)])
-                cp(ap("yo", 384 * hf, 384 * hf + 384, 1, (0, 8)), ps(5 + hf, 0, 384, 1, (0, 8)), "VA"[hf])
-            dma("S", "op", T.yp[:], T["yo"][0:8, :], [ap("yo")], [], 2200)
+            dma("S", "om%d" % c, [(T.ym[4 * c:4 * c + 4, :], T[S][15:64:16, 2048:4096])], [ap(S, 2048, 4096)], [], 2500)
+            dma("S", "osa%d" % c, [(T.ys[half(c), 0:1792], T[S][0:64, 0:1792])], [ap(S, 0, 1792)], [], 3500)
+            counters(u, V, u(SY, 128, 136))
+            tt(u("Pb"), u("Pc"), ap("PC"), ALU.subtract)
+            YO = "yo%d" % c
+            for r in range(2):
+                b = (ba, bf)[r]
+                mm([(ps(b, a, 384, 16, (0, 4)), ap("W", 16 + 64 * r + a, 80 + 64 * r, 16), u("Pb", 0, 24), True) for a in range(16)])
+                cp((YO, r, r + 1) + view(YO, T[YO][0:4, :, 128 * r:128 * r + 128], 384)[3:], ps(b, 0, 384, 1, (0, 4)), "VA"[r])
+            dma("S", "op%d" % c, [(T.yp[4 * c:4 * c + 4, :], T[YO][0:4, :, :])], [(YO, 0, 2) + view(YO, None, 768)[3:]], [], 2200)
+        if not end:
+            both(k1, u(LY, 0, 128), ap(S, 256 * (RO + t), 256 * (RO + t) + 256), OPT["sb"][c])
+        else:
+            dma("SA"[c], "osb%d" % c, [(T.ys[half(c), 1792 + 128 * r:1920 + 128 * r], u(LY, 0, 128, 1, (64 * r, 64 * r + 64))[3]) for r in range(2)], [u(LY, 0, 136)], [], 2200)
+
+    for t in range(RO):
+        now[0] = t
+        for c in range(2):
+            first = len(ops)
+            step(t, c)
+            for o in ops[first:]:
+                o["turn"] = 2 * t + c
     return ops, Q
 
 
-def place(ops, edges, key):
-    n = len(ops)
-    succ = [[] for _ in range(n)]
-    left = [len(edges[i]) for i in range(n)]
-    for i in range(n):
+def place(eng, cost, edges, key, seq, first):
+    key = list(key)
+    for i in seq:
         for j, w in edges[i]:
-            succ[j].append(i)
-    start = [0.0] * n
-    busy = {e: [] for e in "VAPGS"}
-    pool = sorted((key[i], i) for i in range(n) if left[i] == 0)
-    while pool:
-        i = pool.pop(0)[1]
-        t = max([start[j] + w for j, w in edges[i]] + [0.0])
-        e, c = ops[i]["eng"], ops[i]["cost"]
-        if e is not None:
-            b = busy[e]
-            lo, hi = 0, len(b)
-            while lo < hi:
-                mid = (lo + hi) // 2
-                if b[mid][1] <= t:
-                    lo = mid + 1
-                else:
-                    hi = mid
-            while lo < len(b) and b[lo][0] < t + c:
-                t = max(t, b[lo][1])
+            if key[j] >= key[i]:
+                key[i] = key[j] + 0.001
+    start = list(first)
+    busy = {e: ([], []) for e in "VAPGS"}
+    for i in sorted(seq, key=lambda i: key[i]):
+        t = start[i]
+        for j, w in edges[i]:
+            if start[j] + w > t:
+                t = start[j] + w
+        if eng[i] is not None:
+            c = cost[i]
+            s, f = busy[eng[i]]
+            m = lo = len(s)
+            while lo and f[lo - 1] > t:
+                lo -= 1
+            while lo < m and s[lo] < t + c:
+                if f[lo] > t:
+                    t = f[lo]
                 lo += 1
-            b.insert(lo, (t, t + c))
+            s.insert(lo, t)
+            f.insert(lo, t + c)
         start[i] = t
-        new = False
-        for k in succ[i]:
-            left[k] -= 1
-            if left[k] == 0:
-                pool.append((key[k], k))
-                new = True
-        if new:
-            pool.sort()
     return start
 
 
@@ -715,37 +714,42 @@ def schedule(ops, seed=0):
             fw[i].append((j, p["cost"] + gap))
             bw[j].append((i, o["cost"] + gap))
     tail = [o["lat"] for o in ops]
+    eng = [o["eng"] for o in ops]
+    cost = [o["cost"] for o in ops]
+    up = list(range(n))
     twin = {o["cls"]: i for i, o in enumerate(ops)}
-    z = seed * 7919 + 13
-    best = None
+    z = [seed * 7919 + 13]
+
+    def draw():
+        z[0] = (z[0] * 1103515245 + 12345) % 2147483648
+        return z[0] / 2147483648.0
+
+    def passes(key):
+        st = place(eng, cost, fw, key, up, [0.0] * n)
+        back = place(eng, cost, bw, [-(st[i] + cost[i] + tail[i]) for i in up], up[::-1], tail)
+        s2 = place(eng, cost, fw, [-(back[i] + cost[i]) for i in up], up, [0.0] * n)
+        return min((max(s[i] + cost[i] + tail[i] for i in up), s) for s in (st, s2))
+
+    best = cur = passes([float(i) for i in up])
     for attempt in range(OPT["tries"]):
-        if best is None:
-            key = [float(i) for i in range(n)]
+        key = list(cur[1])
+        if attempt % 10 == 0:
+            a, b = int(draw() * RO), int(draw() * RO)
+            pairs = [(i, twin[(a,) + ops[i]["cls"][1:]]) for i in up if ops[i]["cls"][0] == b and (a,) + ops[i]["cls"][1:] in twin]
+            shift = sorted(key[i] - key[j] for i, j in pairs)[len(pairs) // 2]
+            for i, j in pairs:
+                key[i] = cur[1][j] + shift
         else:
-            z = (z * 1103515245 + 12345) % 2147483648
-            w0 = best[0] * (z / 2147483648.0) - 0.5 * OPT["window"]
-            z = (z * 1103515245 + 12345) % 2147483648
-            amp = OPT["noise"] * (z / 2147483648.0) ** 2
-            key = list(best[1])
-            if attempt % 8 == 0:
-                a, b = (z >> 8) % RO, (z >> 12) % RO
-                pairs = [(i, twin[(a,) + ops[i]["cls"][1:]]) for i in range(n) if ops[i]["cls"][0] == b and (a,) + ops[i]["cls"][1:] in twin]
-                shift = sorted(key[i] - key[j] for i, j in pairs)[len(pairs) // 2]
-                for i, j in pairs:
-                    key[i] = best[1][j] + shift
-                amp = 0.0
-            for i in range(n):
-                if amp and w0 <= key[i] < w0 + OPT["window"]:
-                    z = (z * 1103515245 + 12345) % 2147483648
-                    key[i] += amp * (z / 2147483648.0 - 0.5)
-        for rnd in range(2):
-            st = place(ops, fw, key)
-            end = max(st[i] + ops[i]["cost"] + tail[i] for i in range(n))
-            if best is None or end <= best[0]:
-                best = (end, st)
-            if rnd == 0:
-                back = place(ops, bw, [-(st[i] + ops[i]["cost"] + tail[i]) for i in range(n)])
-                key = [-(back[i] + ops[i]["cost"]) for i in range(n)]
+            w0 = cur[0] * draw() - 0.5 * OPT["window"]
+            amp = OPT["noise"] * draw() ** 2
+            for i in up:
+                if w0 <= key[i] < w0 + OPT["window"]:
+                    key[i] += amp * (draw() - 0.5)
+        new = passes(key)
+        if new[0] <= cur[0] + OPT["slack"] * (1 - attempt / OPT["tries"]) * draw():
+            cur = new
+        if new[0] < best[0]:
+            best = new
     st = best[1]
     order = {e: [i for s, i in sorted((st[i], i) for i in range(n) if ops[i]["eng"] == e)] for e in "VAPGS"}
     return order, st, [st[i] + ops[i]["cost"] + tail[i] for i in range(n)]
@@ -797,10 +801,10 @@ def rank_program(g, core, T, topo):
             r = None
             for f in o["fns"]:
                 r = f()
+                if o["kind"] == "d":
+                    r.then_inc(T.sem[o["sem"]], 16)
             if o["kind"] == "c":
                 r.then_inc(T.sem["c" + e], 1)
-            elif o["kind"] == "d":
-                r.then_inc(T.sem[o["sem"]], 16)
         if e == "G":
             for s, v in total.items():
                 if seen.get(s, 0) < v:

from concourse.bass import DstId, RemoteDMATransfer
from concourse.mybir import AluOpType, ActivationFunctionType

N, RO = 4, 4
ALU = AluOpType
AF = ActivationFunctionType
F32, BF, I32, U16 = "float32", "bfloat16", "int32", "uint16"
VW = 464
PB, PM, EB, ED = 384, 416, 448, 456
RC = 1.5 * 2.0 ** 35
BIG = 2.0 ** 23
B = 2.0 ** 17

TWICE = {
    "s": (2048, BF), "sm": (2048, BF), "e": (2048, BF), "y": (2048, BF), "df": (2048, BF), "tf": (2048, BF),
    "qni": (384, I32), "qki": (384, I32), "VO": (384, F32), "D2": (VW, F32), "KM": (384, F32), "RM": (384, F32),
    "Vi": (128, I32), "Ni": (128, I32), "Ki": (128, I32), "Ve": (128, F32), "Ne": (128, F32), "Z": (128, F32), "ZT": (128, F32), "ZM": (128, F32),
    "q16": (128, U16), "n16": (128, U16), "pn": (128, I32), "pn2": (128, I32), "ub": (128, F32),
    "x": (128, BF), "xT": (128, BF), "xd": (256, BF), "HS": (256, BF), "MN": (128, F32), "ya": (128, BF),
    "XT": (256, F32), "EQ": (256, BF), "EM": (256, BF), "RW": (80, BF), "RWT": (128, BF), "RWN": (128, BF),
    "elf": (8, F32), "elt": (8, F32), "elu": (8, U16), "m1": (32, BF), "Pc": (32, F32), "Pt": (32, F32), "mn": (8, F32), "mn2": (8, F32),
    "k0t": (8, F32), "k0b": (16, BF), "lx": (8, U16), "lk": (8, U16), "opi": (8, I32), "opj": (8, I32), "lo": (8, U16), "wt": (24, F32),
    "sa": (24, F32), "sb": (24, F32), "la": (8, U16), "lb": (8, U16), "o1": (8, F32), "lm": (16, U16),
    "gs": (8, F32), "gsb": (16, BF), "ncol": (8, F32), "Pb": (32, BF), "rmf": (8, F32), "r32": (8, F32),
    "gmj": (128, BF), "gmb": (128, F32), "gma": (128, F32), "gm": (128, F32),
    "xs": (512, BF), "xb": (512, BF), "bt": (8, F32), "br": (16, BF), "gmc": (128, BF),
    "Gt": (160, BF), "Dup": (128, BF), "Brm": (128, BF), "WD": (32, BF), "WK": (32, BF), "WX0": (384, BF), "LT": (128, BF),
}
SB = {
    "tui": (128, I32), "tub": (128, BF), "gli": (256, BF), "rmb": (8, BF),
    "pi": (4, I32), "ci": (32, I32), "cf": (48, F32), "J160": (160, BF), "Jg": (128, BF), "Jh": (128, BF), "J32": (128, BF), "Jc": (256, BF), "J64": (192, BF),
    "J8": (8, F32), "Jl": (32, F32), "KI": (128, BF), "JR": (512, BF), "Jx": (24, BF), "Jq": (384, BF), "QW": (384, BF), "JM": (384, BF),
    "c16": (8, BF), "c16s": (8, BF), "PC": (32, F32), "l3": (4, U16), "CK": (16, F32), "KS": (128, BF),
    "l8": (8, U16), "l8s": (8, U16), "Ma": (128, F32), "Rb": (8, F32), "Rbn": (8, F32), "Rbb": (8, BF), "Rbs": (8, F32), "Rj": (48, BF), "Cj": (48, BF),
    "CR": (128, BF), "CR0": (128, BF), "ONE": (128, BF), "ONR": (128, BF), "NEG": (128, BF), "RCt": (384, BF), "CS": (32, BF),
    "W": (160, BF), "W0": (160, BF), "W1": (160, BF), "DW0": (160, F32), "DW1": (160, F32), "Inz": (128, BF), "If": (128, F32), "I4": (128, BF),
    "Fone": (160, BF), "Fcf": (160, BF), "Fmk": (160, BF),
    "B4": (128, BF), "Bcf": (128, BF), "B1": (128, F32), "B64": (128, F32), "B64n": (128, F32),
    "H0": (128, F32), "H1": (128, F32), "Tm": (16, F32), "WX1": (384, BF), "WT": (24, BF), "W2": (24, BF),
    "R": (512, BF), "k16": (512, BF), "dgt": (256, BF), "dmin": (128, BF), "dcap": (128, BF), "dmax": (384, BF), "dres": (384, BF),
}
for _k, (_w, _d) in TWICE.items():
    SB[_k] = (2 * _w, _d)
SCRATCH, PLACE, _fill = {}, {}, {}
for _k, (_w, _d) in SB.items():
    if _w <= 256 and _k not in ("rmb", "gs", "tui", "gli"):
        PLACE[_k] = ("pool_" + _d, _fill.get(_d, 0), _w)
        _fill[_d] = _fill.get(_d, 0) + (_w + 15) // 16 * 16
    else:
        SCRATCH[_k] = ("sbuf", [128, _w], _d)
for _d, _w in _fill.items():
    SCRATCH["pool_" + _d] = ("sbuf", [128, _w], _d)
for _c in range(2):
    SCRATCH["S%d" % _c] = ("sbuf", [128, 4128], BF)
    SCRATCH["EF%d" % _c] = ("sbuf", [128, 4736], BF)
    SCRATCH["OT%d" % _c] = ("sbuf", [128, 512], BF)
    SCRATCH["o3%d" % _c] = ("sbuf", [128, 2, 8], F32)
    SCRATCH["yo%d" % _c] = ("sbuf", [128, 3, 256], F32)
for _t in range(RO):
    SCRATCH["V%d" % _t] = ("sbuf", [128, 2 * VW], F32)
    SCRATCH["GT%d" % _t] = ("sbuf", [128, 256], BF)
    SCRATCH["SY%d" % _t] = ("sbuf", [128, 288], BF)
    SCRATCH["LY%d" % _t] = ("sbuf", [128, 288], BF)
for _b in range(8):
    SCRATCH["ps%d" % _b] = ("psum", [128, 512], F32)
SEMAPHORES = (["cV", "cA", "cP", "cG", "dtu", "dgl", "drm", "lg", "ag1", "ag2", "ag3"]
              + [k + str(c) for k in ("dSa", "dSb", "dEa", "dEb", "dOT", "dqn", "dqk", "oq", "op", "osa", "osb", "om") for c in range(2)]
              + ["%s%d_%d" % (k, t, c) for k in ("lv", "av") for t in range(1, RO) for c in range(2)]
              + ["%s%d_%d" % (k, t, c) for k in ("ly", "ay") for t in range(RO) for c in range(2)])

CY, PCY, GC, SC = 0.95, 0.5, 1.5, 3.5
XLAT, SLAT = 260.0, 140.0
OPT = {"s": "AAAVAAAV", "e": "AAAXAAAX", "t": "AAAAAAAA", "x": "AA", "uv": "TT", "qat": 2, "mat": 0, "sq": "A", "z": "V", "gj": "AA",
       "ya": "AA", "yb": "AA", "sa": "AA", "sb": "AA", "b": "P", "cuts": (0, 128),
       "tries": 9000, "seed": 0, "noise": 5000.0, "window": 10000.0, "slack": 800.0}


def build(g, core, T, topo):
    rank = T.rank_of(core)
    ops = []
    hist = {}
    steps = {}
    seen = {}
    now = [-1]
    Q = {"V": g.vector, "A": g.scalar, "P": g.tensor, "G": g, "S": g.sync}

    def ap(name, lo=0, hi=None, step=1, p=None):
        if name in PLACE:
            name, at, w = PLACE[name]
            lo, hi = at + lo, at + (w if hi is None else hi)
        t = T[name]
        if hi is None:
            hi = t.shape[1]
        r = t[:, lo:hi:step] if p is None else t[p[0]:p[1], lo:hi:step]
        steps[(name, lo, hi, len(range(lo, hi, step)))] = step
        return (name, lo, hi, r, len(range(lo, hi, step)), SCRATCH[name][2])

    def of(c):
        def u(name, lo=0, hi=None, step=1, p=None):
            w = TWICE[name][0] if name in TWICE else T[name].shape[1] // 2
            return ap(name, c * w + lo, c * w + (w if hi is None else hi), step, p)
        return u

    def view(name, r, n):
        return (name, 0, 1, r, n, SCRATCH[name][2])

    def ind(win, off):
        return (win[0], win[1], win[2], win[3].indirect(off[3]), 16 * off[4], win[5], off)

    def val(s):
        return s[3] if isinstance(s, tuple) else s

    def stp(a):
        return steps.get((a[0], a[1], a[2], a[4]), 1) if len(a) == 6 else 1

    def add(eng, fns, cost, reads, writes, kind="c", sem=None, cnt=0, lat=0.0, after=(), goes_on=False):
        i = len(ops)
        rd, wr = [], []
        for lst, a in [(rd, a) for a in reads] + [(wr, a) for a in writes]:
            if isinstance(a, tuple):
                lst.append(a)
                if len(a) > 6:
                    rd.append(a[6])
        deps = {j: False for j in after}
        ops.append({"eng": eng, "fns": fns, "cost": cost, "deps": deps, "kind": kind, "sem": sem, "cnt": cnt, "lat": lat,
                    "tag": wr[0][:2] if wr else ("", 0)})
        nm = wr[0][0] if wr else ""
        nm = (eng, kind, nm[:2] if nm[:2] in ("SY", "LY") else "V" if nm[:1] == "V" and nm[1:].isdigit() else nm)
        seen[(now[0], nm)] = seen.get((now[0], nm), 0) + 1
        ops[i]["cls"] = (now[0], nm, seen[(now[0], nm)])
        for isw, a in [(False, a) for a in rd] + [(True, a) for a in wr]:
            psum = a[0].startswith("ps")
            st = stp(a)
            for (lo, hi, j, w, s2) in hist.get(a[0], []):
                o = ops[j]
                same = o["eng"] == eng and o["kind"] == "c" and kind == "c"
                over = lo < a[2] and a[1] < hi and not (st == s2 and st > 1 and (lo - a[1]) % st)
                if psum:
                    need = (not same) or (over and (w or isw) and not goes_on)
                    deps[j] = deps.get(j, False) or need
                elif over and (w or isw):
                    deps[j] = True
        for isw, a in [(False, a) for a in rd] + [(True, a) for a in wr]:
            h = hist.setdefault(a[0], [])
            if a[0].startswith("ps"):
                if any(ops[r[2]]["eng"] != eng for r in h):
                    h[:] = [r for r in h if r[2] == i]
            elif isw and stp(a) == 1:
                h[:] = [r for r in h if not (a[1] <= r[0] and r[1] <= a[2])]
            h.append((a[1], a[2], i, isw, stp(a)))
        deps.pop(i, None)
        return i

    def vcost(out, ins, two=False):
        n = out[4]
        if len(out) > 6:
            return 50 + n * SC * CY
        if len(ins[0]) > 6:
            return 50 + n * GC * CY
        if two:
            f = 1.0 if any(a[0].startswith("ps") for a in ins) else 2.0
        else:
            f = 0.5 if all(a[5] in (BF, U16) for a in [out] + ins) else 1.0
        return max(64, n * f) * CY

    def ts(out, in0, s1, op0, s2=None, op1=None):
        if op1 is None:
            f = lambda: g.vector.tensor_scalar(out[3], in0[3], val(s1), None, op0)
        else:
            f = lambda: g.vector.tensor_scalar(out[3], in0[3], val(s1), val(s2), op0, op1)
        return add("V", [f], vcost(out, [in0]), [in0, s1, s2], [out])

    def tt(out, a, b, op):
        return add("V", [lambda: g.vector.tensor_tensor(out[3], a[3], b[3], op)], vcost(out, [a, b], True), [a, b], [out])

    def cp(out, a, eng="V"):
        if eng == "A":
            return act(out, a, AF.Identity)
        return add("V", [lambda: g.vector.tensor_copy(out[3], a[3])], vcost(out, [a]), [a], [out])

    def ms(out, c):
        return add("V", [lambda: g.vector.memset(out[3], c)], vcost(out, [out]), [], [out])

    def scan(out, d0, d1, op0, op1):
        return add("V", [lambda: g.vector.tensor_tensor_scan(out[3], d0[3], d1[3], 0.0, op0, op1)], vcost(out, [d0, d1]), [d0, d1], [out])

    def tr(out, a):
        return add("V", [lambda: g.vector.transpose(out[3], a[3])], vcost(out, [a]), [a], [out])

    def act(out, a, fn, bias=0.0, scale=1.0, acc=None):
        c = 65 + out[4] * GC * CY if len(a) > 6 else max(64, out[4]) * CY
        if acc is not None:
            f = lambda: g.scalar.activation(out[3], a[3], fn, bias=val(bias), scale=val(scale), accum_out=acc[3])
            return add("A", [f], c + 20, [a, bias, scale], [out, acc])
        return add("A", [lambda: g.scalar.activation(out[3], a[3], fn, bias=val(bias), scale=val(scale))], c, [a, bias, scale], [out])

    def mul(out, a, c):
        return act(out, a, AF.Identity, 0.0, c)

    def mm(items, last=True, also=()):
        fns, cost, rd, wr = [], 0.0, [], list(also)
        for k, (o, l, r, st) in enumerate(items):
            nxt = items[k + 1][3] if k + 1 < len(items) else last
            fns.append(lambda o=o, l=l, r=r, st=st, sp=nxt: g.tensor.matmul(o[3], l[3], r[3], st, sp))
            cost += max(min(64, l[4]), r[4]) * (4 if r[5] == F32 else 1) * PCY
            rd += [l, r]
            wr.append(o)
        return add("P", fns, cost, rd, wr, goes_on=not items[0][3])

    def grp(o, pairs, first=True):
        return [(o, l, r, first and k == 0) for k, (l, r) in enumerate(pairs)]

    alone = ("alone", 0, 1, None, 1, F32)

    def iota(out, pat, base, cm):
        if out[5] == I32:
            f = lambda: g.iota(out[3], pat, base, cm)
        else:
            f = lambda: g.iota(out[3], pat, base, cm, allow_small_or_imprecise_dtypes=True)
        return add("G", [f], 130 + 2 * out[4] * CY, [alone], [out])

    def select(out, a, pat, base, cm):
        f = lambda: g.affine_select(out[3], a[3], pat, ALU.is_equal, 0.0, base, cm)
        return add("G", [f], 170 + 2 * out[4] * CY, [a], [out, alone])

    last_dma = {}

    def dma(eng, sem, pairs, reads, writes, lat):
        fns = [lambda o=o, a=a: Q[eng].dma_start(o, a) for o, a in pairs]
        last_dma[eng] = add(eng, fns, 60.0 * len(pairs), reads, writes, "d", sem, 16 * len(pairs), lat, [last_dma[eng]] if eng in last_dma and now[0] < 0 else [])

    def send(srcs, dsts, lsem, lat):
        trs = []
        for k, (dist, land, asem) in enumerate(dsts):
            dst = T.cores[(rank + dist) % N]
            en = topo.engines(core, dst)
            per = len(en) if len(dsts) == 1 else 2
            m = sum(1 << e for e in en[k * per:(k + 1) * per])
            rid, pid = topo.addr(dst)[0], topo.addr(dst)[1]
            kw = {"src": srcs[0][3]} if len(srcs) == 1 else {"srcs": [a[3] for a in srcs], "alu_op": 1}
            trs.append((RemoteDMATransfer(dst_ids=[DstId(rid=rid, pnc=pid)], dma_engine_mask=m, remote_sem=T.sem[asem], dst=land[3], **kw), per))
        i = add("G", [lambda: g.remote_dma_fused([a for a, b in trs], local_sem=T.sem[lsem])], 600.0, srcs, [], "s", lsem, sum(b for a, b in trs), lat)
        for (dist, land, asem), (a, per) in zip(dsts, trs):
            add(None, [], 0.0, [], [land], "r", asem, per, 0.0, [i])

    ps = lambda b, lo=0, hi=512, step=1, p=None: ap("ps%d" % b, lo, hi, step, p)
    col = lambda k, p=None: ap("cf", k, k + 1, 1, p)
    sl = lambda name, s: ap(name, 16 - s, 144 - s)
    row = lambda name, lo=0, hi=None, n=1: ap(name, lo, hi, 1, (0, n))
    half = lambda r: slice(64 * r, 64 * r + 64)

    dma("S", "dtu", [(T["tui"][32 * l:32 * l + 16, :], T.tu[:, 256 * l:256 * l + 256]) for l in range(3)], [], [ap("tui")], 2200)
    for c in range(2):
        u = of(c)
        for eng, nm, src in (("A", "qk", T.qk), ("S", "qn", T.qn)):
            dma(eng, "d%s%d" % (nm, c), [(u(nm + "i", 128 * l, 128 * l + 128, 1, (64 * r, 64 * r + 64))[3], src[half(c), 256 * l + 128 * r:256 * l + 128 * r + 128])
                                         for r in range(2) for l in range(3)], [], [u(nm + "i")], 2500 + 4500 * c)
        for r in range(2):
            dma("AS"[r], "dS%s%d" % ("ab"[r], c), [(T["S%d" % c][half(r), 0:4096], T.st0[half(c), :])], [], [ap("S%d" % c, 2048 * r, 2048 * r + 2048)], 5500 + 4000 * c)
        if c == 0:
            dma("S", "dgl", [(T["gli"][:], T.gl[:])], [], [ap("gli")], 5500)
            dma("A", "drm", [(T["rmb"][:, 0:1], T.rm[:])], [], [ap("rmb")], 5500)
    for c in range(2):
        dma("S", "dOT%d" % c, [(T["OT%d" % c][half(r), :], T.ot[half(c), :]) for r in range(2)], [], [ap("OT%d" % c)], 9000 + 4000 * c)
        for r in range(2):
            dma("S", "dE%s%d" % ("ab"[r], c), [(T["EF%d" % c][half(r), 0:4096], T.ef[half(c), :]), (T["EF%d" % c][half(r), 4096:4736], T.ef[half(c), 0:640])],
                [], [ap("EF%d" % c, 2048 * r, 2048 * r + 2048)], 12500 + 4000 * c)

    (P_, K_, G16, P32, A32, NZ, CFC, MK, HH0, HH1, R15, K16, K37, DC, E0, N0, E1, N1, N32, G1, G2, SQ, SQN, M65, CA, CB, K128,
     P64, G64, RR0, RR1, K8, TA, TB) = range(34)
    iota(ap("pi", 0, 1), [[0, 1]], 0, 1)
    iota(ap("J160"), [[1, 160]], -16, 0)
    iota(ap("Jl"), [[128, 4], [16, 8]], 0, 0)
    iota(ap("J8"), [[1, 8]], 0, 0)
    iota(ap("Jg"), [[16, 8], [0, 16]], 0, 0)
    iota(ap("KI"), [[0, 8], [1, 16]], 0, 0)
    iota(ap("J64"), [[0, 3], [1, 64]], 0, 0)
    iota(ap("Jh"), [[0, 2], [16, 4], [0, 16]], 0, 0)
    iota(ap("J32"), [[32, 4], [0, 32]], 0, 0)
    iota(ap("Jc"), [[0, 8], [1, 32]], 0, 0)
    iota(ap("JR"), [[1, 32], [0, 16]], 0, 0)
    iota(ap("Jx"), [[16, 8], [1, 3]], 0, 0)
    iota(ap("Jq"), [[0, 24], [2, 16]], -30, 0)
    cp(col(P_), ap("pi", 0, 1))
    for k, (m, cl) in enumerate(((15, K_), (31, P32), (63, P64), (7, K8), (1, TA), (6, TB), (8, CA))):
        ts(ap("ci", k, k + 1), ap("pi", 0, 1), m, ALU.bitwise_and)
        cp(col(cl), ap("ci", k, k + 1))
    J = ap("J160")
    mul(col(TB), col(TB), 8.0)
    act(col(TA), col(TA), AF.Identity, col(TB), 64.0)
    for c in range(2):
        act(col(TB), col(CA), AF.Abs, -128.0 * 8 * c, 128.0)
        tt(col(TB), col(TB), col(TA), ALU.add)
        ts(of(c)("Gt"), J, col(TB), ALU.is_equal)
    ts(col(G16), col(P_), col(K_), ALU.subtract)
    ts(col(A32), col(P_), col(P32), ALU.subtract)
    ts(col(G64), col(P64), col(K_), ALU.subtract)
    ts(col(NZ), col(K_), 15.0, ALU.is_lt)
    ts(col(CFC), col(K_), 2.0, ALU.mult, 1.0, ALU.add)
    ts(col(CFC), col(CFC), col(NZ), ALU.mult)
    ts(col(MK), col(K_), 15.0, ALU.is_equal, 2.0 ** 22, ALU.mult)
    ts(col(HH0), col(P32), 16.0, ALU.is_lt)
    ts(col(RR0), col(P_), 64.0, ALU.is_lt)
    ts(col(E0), col(P_), 0.0, ALU.is_equal)
    ts(col(E1), col(P_), 1.0, ALU.is_equal)
    for a, b in ((HH1, HH0), (RR1, RR0), (R15, NZ), (N1, E1)):
        act(col(a), col(b), AF.Identity, 1.0, -1.0)
    act(col(N0), col(E0), AF.Identity, 128.0, -128.0)
    mul(col(K16), col(K_), 16.0)
    mul(col(K37), col(K_), 37.0)
    mul(col(N32), col(NZ), -32.0)
    act(col(DC), col(P32), AF.Identity, 4096.0)
    act(col(G1), col(G16), AF.Identity, 1.0)
    act(col(G2), col(G16), AF.Identity, 2.0)
    for p, v in (((0, 32), 2.0 ** 16), ((32, 64), 2.0 ** -26), ((64, 96), BIG)):
        ms(col(SQ, p), v)
    ms(col(M65), -6.5)
    for nm, c in (("Fmk", MK), ("Fone", NZ), ("Fcf", CFC)):
        ts(ap(nm), J, col(G16), ALU.is_equal, col(c), ALU.mult)
    ts(ap("W"), J, col(P_), ALU.is_equal)
    I_ = sl("W", 0)
    for k in range(2):
        mul(ap("W%d" % k), ap("W"), col((HH0, HH1)[k]))
        ts(of(k)("Dup"), ap("J64", 0, 128), col(P64), ALU.is_equal, col((RR0, RR1)[k]), ALU.mult)
    mul(ap("Inz"), I_, col(NZ))
    mul(ap("If"), I_, 1.0)
    mul(ap("I4"), I_, 4.0)
    ts(ap("B1"), ap("Jg"), col(G16), ALU.is_equal)
    ts(ap("B64"), ap("Jh"), col(G64), ALU.is_equal)
    mul(ap("B64n"), ap("B64"), -1.0)
    mul(ap("Bcf"), ap("B1"), col(CFC))
    mul(ap("B4"), ap("B1"), col(N32))
    mul(ap("B4"), ap("B4"), 128.0)
    ts(ap("H0"), ap("J32"), col(A32), ALU.is_equal, col(HH0), ALU.mult)
    ts(ap("H1"), ap("J32"), col(A32), ALU.is_equal, col(HH1), ALU.mult)
    ts(ap("dgt"), ap("Jc"), col(P32), ALU.is_gt)
    ts(ap("Tm"), ap("J160", 16, 32), col(K_), ALU.is_equal)
    ts(ap("CR0"), ap("J160", 16, 144), col(E0), ALU.mult, col(N0), ALU.add)
    act(ap("CR"), ap("J160", 16, 144), AF.Identity, 0.5)
    ts(ap("CR"), ap("CR"), col(E0), ALU.mult, col(N0), ALU.add)
    ms(ap("ONE"), 1.0)
    ms(ap("NEG"), -1.0)
    ms(ap("ONR", 64, 128), -1.0)
    mul(ap("ONR", 0, 64), ap("NEG", 0, 64), col(N1))
    ms(ap("RCt"), 2.0 ** 35)
    ms(ap("CS", 0, 8), 1.5 * 2.0 ** 28)
    ms(ap("CS", 8, 9), 1.5 * 2.0 ** 29)
    ms(ap("CS", 9, 10), 31.5)
    ts(ap("c16"), ap("J8"), 256.0, ALU.mult, col(K16), ALU.add)
    mul(ap("c16s"), ap("c16"), 128.0)
    ts(ap("PC"), ap("Jl"), col(K_), ALU.add, 1.0 / 1024, ALU.mult)
    ts(ap("R"), ap("JR"), col(P32), ALU.is_equal)
    inps = OPT["z"] == "P"
    K0 = 0.0 if inps else 15.0
    if inps:
        mul(ap("KS"), ap("KI"), 128.0)
        mul(col(K128), col(K_), 128.0)
    for nm, per, v0, v in (("k16", 16, 0.0, 1.0), ("dcap", 16, 2.0 ** 22, -BIG) if inps else ("dmin", 16, 2 * BIG, -128.0),
                           ("dmax", 16, -2 * BIG, 128.0), ("dres", 16, 2 * BIG, 0.0)):
        ms(ap(nm), v)
        ms(ap(nm, 0, None, per), v0)
    ms(ap("RW"), 0.0)
    ms(ap("RW", 64, 160, 80), 1.0)
    select(ap("QW", p=(0, 32)), ap("Jq", p=(0, 32)), [[-1, 24], [0, 16]], 0, 1)
    select(ap("QW", p=(32, 64)), ap("RCt", p=(32, 64)), [[-1, 24], [0, 16]], 0, 1)
    act(ap("QW", p=(64, 96)), ap("Jq", p=(64, 96)), AF.Square, 0.0, 0.5)
    cp(ap("l8"), ap("J8"))
    ts(ap("l8s"), ap("J8"), 3.0, ALU.mult, 2.0, ALU.add)
    ts(ap("Ma"), ap("KI", 0, 128), col(K_), ALU.is_equal)
    ts(ap("Rb"), ap("Jg", 0, 128, 16), col(G16), ALU.is_equal)
    mul(ap("Rbn"), ap("Rb"), -1.0)
    mul(ap("Rbb"), ap("Rb"), 1.0)
    mul(ap("Rbs"), ap("Rb"), 1.0 / B)
    for k in range(2):
        cp(ap("l3", k, k + 1), col(K8))
    for k in range(3):
        mul(ap("JM", 128 * k, 128 * k + 128), ap("Ma"), 128.0 * k)
    ts(ap("WT"), ap("Jx"), col(G1), ALU.is_equal, col(N32), ALU.mult)
    ts(ap("CK"), ap("KI", 0, 16), col(R15), ALU.mult, col(NZ), ALU.add)
    for k in range(16):
        cp(ap("WX1", k, 384, 16), ap("WT"), "A")
    mul(ap("WT"), ap("WT"), -8.0)
    STEP = (((2 * BIG, 0.0), (-B, 2 * B), (-3 * B, 2 * B)), ((2 * BIG, 0.0), (4 * B, -4 * B), (-B, 2 * B)))
    for w in range(2):
        for l in range(3):
            mul(ap("Rj", 24 * w + l, 24 * w + 24, 3), ap("Rb"), STEP[w][l][1] / 128)
            mul(col(CA), col(E0), STEP[w][l][0])
            act(col(CB), col(E1), AF.Identity, col(CA), (0.0, -3840.0, 3840.0)[l])
            act(ap("Cj", 24 * w + l, 24 * w + 24, 3), ap("ONE", 0, 8), AF.Identity, 0.0, col(CB))
    ms(ap("LT"), 1.0)
    for k in range(8):
        if OPT["t"][k] == "V":
            mul(ap("LT", 32 * k, 32 * k + 32), ap("ONE", 0, 32), col(E0))
    for k in range(2):
        ts(ap("DW%d" % k, 0, 16), ap("J64", 48, 64), col(P64), ALU.is_equal, col((HH0, HH1)[k]), ALU.mult)
        ts(ap("DW%d" % k, 16, 160), ap("J64", 0, 144), col(P64), ALU.is_equal, col((HH0, HH1)[k]), ALU.mult)

    def swap(bank, lo, n, src, pat, extra=None):
        it = []
        for c in range(2):
            pr = [(sl("%s%d" % (pat, c), 16 * (h - c)), src(h)) for h in range(2)]
            if extra is not None:
                pr.append((I_, extra(c)))
            it += grp(ps(bank, lo + c, lo + 2 * n, 2), pr)
        mm(it)

    def spread(tmp, src, lst="l8"):
        tt(tmp, ind(src, ap(lst)), ap("Ma"), ALU.mult)

    def child_list(tmp, out):
        mm(grp(out, [(tmp, ap("Rbn")), (row("ONE"), row("CS", 0, 8)), (row("NEG"), row("CS", 0, 8)), (tmp, ap("Rb")), (I_, ap("c16"))]))

    def both(bank, src, out, eng):
        mm([(ps(bank, 128 * r, 128 * r + 128), of(r)("Dup"), src, True) for r in range(2)])
        cp(out, ps(bank, 0, 256), eng)

    def least(u, src, dst):
        tt(u("mn"), src(0), src(1), ALU.min)
        tt(u("mn2"), u("mn"), src(2), ALU.min)
        ts(u("mn"), u("mn2"), 1.5 * BIG, ALU.add, 1.5 * BIG, ALU.subtract)
        tt(dst, u("mn2"), u("mn"), ALU.subtract)

    def counters(u, V, go):
        tt(u("Pt"), ind(go, ap("l3", 0, 2)), u(V, PM, PM + 32), ALU.mult)
        tt(u("Pc"), u("Pt"), u(V, PB, PB + 32), ALU.add)

    for l in range(3):
        cp(ap("tub", p=(32 * l, 32 * l + 16)), ap("tui", p=(32 * l, 32 * l + 16)))
    for c in range(2):
        u = of(c)
        b0 = 4 * c
        for l in range(3):
            p = (32 * l, 32 * l + 16)
            mm(grp(ps(b0, 8 * l, 8 * l + 8), [(u("Gt", 16 - a, 144 - a, 1, p), ap("tub", a, 128, 16, p)) for a in range(16)]), also=[ps(b0, 0, 24)])
        ms(u("Pc", 24, 32), 0.0)
        tt(u("Pc", 0, 24), ps(b0, 0, 24), ap("PC", 0, 24), ALU.add)
        least(u, lambda l: u("Pc", 8 * l, 8 * l + 8), u("elf"))
        ts(ps(b0 + 1, 0, 384), u("qki"), 4096.0, ALU.mult, 2048.5, ALU.add)
        tt(u("V0", 0, 384), ps(b0 + 1, 0, 384), u("qni"), ALU.add)
        mm([(ps(b0 + 2, 64 * r, 64 * r + 64), ap("gli", 128 * r, 128 * r + 128), ap("W", 16 + 64 * c, 80 + 64 * c), True) for r in range(2)])
        mul(u("GT0"), ps(b0 + 2, 0, 128), -1.0)
        mm([(ps(b0 + 3, 0, 1), u("Dup"), ap("rmb", 0, 1), True)])
        cp(u("rmf", 0, 1), ps(b0 + 3, 0, 1), "A")
        mul(u("r32", 0, 1), u("rmf", 0, 1), -32.0)
        mul(u("Brm"), ap("B4"), u("rmf", 0, 1))
        ts(u("WD", 0, 24), ap("Jx"), col(G16), ALU.is_equal, col(N32), ALU.mult)
        ts(ap("W2"), ap("Jx"), col(G2), ALU.is_equal, u("r32", 0, 1), ALU.mult)
        tt(u("WD", 0, 24), u("WD", 0, 24), ap("W2"), ALU.add)
        for l in range(3):
            mul(u("WK", l, 24, 3), ap("Rb"), col(R15))
        tt(u("WK", 0, 24), u("WK", 0, 24), u("WD", 0, 24), ALU.add)
        for k in range(16):
            mul(u("WX0", k, 384, 16), u("WK", 0, 24), ap("CK", k, k + 1))
        mul(u("WD", 0, 24), u("WD", 0, 24), -1.0)
        if "X" in OPT["e"][4 * c:4 * c + 4]:
            ms(u("xs"), 0.0)
        ms(u("D2", 384, VW), 0.0)
        ms(view("o3%d" % c, T["o3%d" % c][:, :, :], 16), 0.0)
        cp(u("ncol", 0, 1), col(K37), "A")
    send([ap("GT0")], [(k, ap("GT%d" % k), "ag%d" % k) for k in range(1, N)], "lg", 4000)

    def step(t, c):
        V, GT, SY, LY, S, O3 = "V%d" % t, "GT%d" % t, "SY%d" % t, "LY%d" % t, "S%d" % c, "o3%d" % c
        end = t == RO - 1
        u = of(c)
        ba, bf = 4 * c, 4 * c + 1
        k0, k1 = ba, bf
        if t > 0:
            go = u("LY%d" % (t - 1), 128, 136)
            tt(u("elt"), go, u(V, ED, ED + 8), ALU.mult)
            tt(u("elf"), u("elt"), u(V, EB, EB + 8), ALU.add)
        ts(u("elu"), u("elf"), 1024.0, ALU.mult)
        ts(u("Vi"), ind(u(V, 0, 384), u("elu")), 2047.5, ALU.add)
        ts(u("Ni"), u("Vi"), 4095, ALU.bitwise_and)
        cp(u("q16"), u("Ni"))
        if inps:
            cp(u("Ve"), ind(u(V, 0, 384), u("elu")), "A")
        else:
            ts(u("Ki"), u("Vi"), 0x7FF000, ALU.bitwise_and)
        ts(u("Ne"), u("Ni"), -2047.5, ALU.add)
        if t > 0:
            counters(u, V, go)
        tt(u("m1"), ind(u("elf"), ap("l3", 0, 2)), ap("PC"), ALU.is_equal)
        tt(u(V, PB, PB + 32), u("Pc"), u("m1"), ALU.add)
        mul(u(V, PM, PM + 32), u("m1"), -3.0)
        if not end:
            least(u, lambda l: u(V, PB + 8 * l, PB + 8 * l + 8), u(V, EB, EB + 8))
            tt(u(V, ED, ED + 8), u("elf"), u(V, EB, EB + 8), ALU.subtract)
        for k in range(4):
            cp(u("s", 512 * k, 512 * k + 512), ind(ap(S, 0, 4096), u("q16", 32 * k, 32 * k + 32)), OPT["s"][4 * c + k])
        cp(u("gmj"), ind(ap("JM"), u("elu")), OPT["gj"][c])
        mm(grp(ps(bf, 384, 432), [(u("gmj"), ap("Rj")), (u("LT", p=(0, 2)), row("Cj", n=2))]))
        if inps:
            mm(grp(ps(k0, 0, 128), [(ap("If"), u("Ve")), (row("ONE"), row("RCt", 0, 128)), (row("NEG"), row("RCt", 0, 128)), (row("KS"), row("ONE"))]), last=False)
        for hf in range(2):
            o = 1024 * hf
            mm(grp(ps(k0, 64 * hf, 64 * hf + 64), [(sl("Fmk", k), u("s", o + k, o + 1024, 16)) for k in range(16)], not inps), last=hf == 1 or not inps)
        if inps:
            tr(u("ZT"), ps(k0, 0, 128))
            scan(u("ZM"), ap("dcap"), u("ZT"), ALU.max, ALU.min)
            ts(u("Z"), ps(k0, 0, 128), col(K128), ALU.subtract, 2.0 ** 22, ALU.min)
        else:
            tt(u("Z"), u("Ki"), ps(k0, 0, 128), ALU.max)
            tr(u("ZT"), u("Z"))
            scan(u("ZM"), ap("dmin"), u("ZT"), ALU.add, ALU.min)
        z15 = u("ZM", 15, 128, 16)
        ts(u("k0t"), z15, RC, ALU.add, RC, ALU.subtract)
        tt(u("k0b", 0, 8), z15, u("k0t"), ALU.subtract)
        swap(k0, 128, 4, lambda h: u("k0b", h, 8, 2), "W", lambda cc: ap("c16s", cc, 8, 2))
        ts(u("lx"), ps(k0, 128, 136), 1.0 / 128, ALU.mult, K0, ALU.add)
        if OPT["x"][c] == "A":
            act(u("x"), ind(u("s"), u("lx")), AF.Identity, col(R15), col(NZ))
        else:
            ts(u("x"), ind(u("s"), u("lx")), col(NZ), ALU.mult, col(R15), ALU.add)
        for o in range(0, 2048, 512):
            scan(u("sm", o, o + 512), ap("k16"), u("s", o, o + 512), ALU.mult, ALU.max)
        uv = ps(k1, 0, 8)
        if OPT["uv"][c] == "D":
            mm(grp(uv, [(sl("Fone", a), u("sm", 15 + 16 * a, 2048, 256)) for a in range(16)]), last=False)
            mm(grp(uv, [(sl("Fcf", a), u("x", a, 128, 16)) for a in range(16)], False))
        else:
            mm(grp(uv, [(u("sm", 15, 2048, 16), ap("Fone", 16, 144, 16)), (u("x"), ap("Fcf", 16, 144, 16))]))
        cp(u("opi"), uv)
        mm(grp(ps(ba, 0, 128), [(ap("Bcf"), u("x"))]))
        mm(grp(ps(ba, 128, 256), [(u("x"), ap("Inz"))]) + grp(ps(ba, 256, 384), [(ap("Inz"), u("x")), (u(GT), I_)]))
        act(u("ub"), ps(ba, 0, 128), AF.Identity, 32.0)
        ts(u("opj"), u("opi"), 511, ALU.bitwise_and)
        if OPT["uv"][c] == "D":
            cp(u("lo"), u("opj"))
        else:
            spread(u("gm"), u("opj"))
            mm(grp(ps(k1, 8, 16), [(u("gm"), ap("Rb"))]))
            cp(u("lo"), ps(k1, 8, 16))
        tt(u("pn"), ind(ap("OT%d" % c), u("lo")), u("ub"), ALU.mult)
        ts(u("pn2"), u("pn"), 5, ALU.arith_shift_right, 4095, ALU.bitwise_and)
        ts(u("n16"), u("pn2"), u("ncol", 0, 1), ALU.add)
        cp(u("xT"), ps(ba, 128, 256), "A")
        act(u("HS", 0, 128), ps(ba, 256, 384), AF.Abs, col(R15))
        ts(u("HS", 128, 256), u("HS", 0, 128), 6.0, ALU.is_gt, 16.0, ALU.mult)
        tt(ind(u(V, 0, 384), u("elu")), u("Z"), u("Ne"), ALU.add)
        for l in range(3):
            mm(grp(ps(bf, 128 * l, 128 * l + 128), [(u(V, 128 * l, 128 * l + 128), ap("If")), (row("ONE"), row("RCt", 0, 128)), (row("NEG"), row("RCt", 0, 128))]))
        scan(u("KM"), ap("dmax"), ps(bf, 0, 384), ALU.add, ALU.max)
        if end:
            act(u("VO"), u(V, 0, 384), AF.Identity, -2048.5)

        def queues():
            k15 = u("KM", 15, 384, 16)
            ts(u("wt"), k15, RC, ALU.add, RC, ALU.subtract)
            tt(u("RW", 0, 24), k15, u("wt"), ALU.subtract)
            if OPT["sq"] == "A":
                act(u("RW", 32, 56), u("RW", 0, 24), AF.Square)
            else:
                tt(u("RW", 32, 56), u("RW", 0, 24), u("RW", 0, 24), ALU.mult)
            p65 = (0, 65)
            qw = lambda l: ap("QW", 128 * l, 128 * l + 128, 1, p65)
            mm([(ps(ba, 384, 512, 1, p65), u("RW", 0, 65), I_, True)])
            mul(u("RWT", p=p65), ps(ba, 384, 512, 1, p65), col(SQ, p65))
            M = u("VO") if end else u(V, 0, 384)
            n = (2 if end else 18) + 2 * t
            it = []
            for l in range(3):
                it += grp(ps(ba, 128 * l, 128 * l + 128), [(qw(l), u("RWT", p=p65)), (u("Brm") if l == 2 else ap("B4"), u("HS", 128 * (l % 2), 128 * (l % 2) + 128)),
                                                           (row("ONR", n=n), row("CR0" if end else "CR", n=n))])
            mm(it)
            tt(M, M, ps(ba, 0, 384), ALU.min)
            if end:
                act(M, M, AF.Abs)
                dma("S", "oq%d" % c, [(T.yq[half(c), 256 * l + 128 * r:256 * l + 128 * r + 128], u("VO", 128 * l, 128 * l + 128, 1, (64 * r, 64 * r + 64))[3])
                                      for r in range(2) for l in range(3)], [M], [], 3000)
            else:
                act(u("D2", 0, 384), ps(ba, 0, 384), AF.Relu, 0.0, -2.0)
                send([u(V), u("D2")], [(1, u("V%d" % (t + 1)), "av%d_%d" % (t + 1, c))], "lv%d_%d" % (t + 1, c), 4500)

        def marks():
            swap(ba, 0, 4, lambda h: u("k0b", h, 8, 2), "W")
            ts(u("lk"), ps(ba, 0, 8), 1.0 / 128, ALU.mult, K0, ALU.add)
            both(ba, u("x"), u("xd"), "A")
            tt(u("MN"), ind(ap("Tm"), u("lk")), u("Ni"), ALU.mult)
            mm([(ps(ba, 128 * h, 128 * h + 128), ap("H%d" % h), u("MN"), True) for h in range(2)])
            tr(u("XT"), ps(ba, 0, 256))
            tt(u("EQ"), ps(ba, 0, 256), u("XT"), ALU.is_equal)
            scan(u("EM"), ap("dgt"), u("EQ"), ALU.mult, ALU.add)
            ts(u("o1"), u("EM", 31, 256, 32), 1.5, ALU.is_ge, col(DC), ALU.mult)
            for r in range(2):
                p = (64 * r, 64 * r + 64)
                tt(view(O3, T[O3][half(r), :, 4 * r:4 * r + 4], 8), u("o1", p=p), u("XT", 0, 256, 32, p), ALU.max)
            swap(ba, 0, 8, lambda h: view(O3, T[O3][:, h, :], 8), "DW")
            cp(u("lm"), ps(ba, 0, 16))
            for k in range(8):
                cp(ind(ap(S), u("lm", 2 * k, 2 * k + 2)), u("xd", 32 * k, 32 * k + 32))

        mm(grp(ps(bf, 0, 384), [(u("HS", 0, 128), u("WX0")), (u("HS", 128, 256), ap("WX1"))]), last=False)
        for q in range(5):
            if q == OPT["qat"]:
                queues()
            if q == OPT["mat"]:
                marks()
            if q == 4:
                break
            ch = lambda name: u(name, 512 * q, 512 * q + 512)
            p32 = (32 * q, 32 * q + 32)
            eg = ind(ap("EF%d" % c), u("n16", 32 * q, 32 * q + 32))
            if OPT["e"][4 * c + q] == "X":
                mul(u("xs", 0, 512, 16), u("x", 32 * q, 32 * q + 32), col(NZ))
                scan(u("xb"), ap("k16"), u("xs"), ALU.mult, ALU.add)
                tt(ch("e"), eg, u("xb"), ALU.add)
                ts(ch("y"), ch("e"), 0.0, ALU.max, 63.0, ALU.min)
            else:
                cp(ch("e"), eg, OPT["e"][4 * c + q])
                mm(grp(ps(2 + q % 2), [(u("xT", p=p32), ap("R", p=p32)), (I_, ch("e"))]))
                ts(ch("y"), ps(2 + q % 2), 0.0, ALU.max, 63.0, ALU.min)
            mm(grp(ps(6 + q % 2), [(u(GT, p=p32), ap("R", p=p32)), (I_, ch("y"))]))
            act(ch("df"), ps(6 + q % 2), AF.Abs)
            if OPT["t"][4 * c + q] == "A":
                act(ch("tf"), ch("df"), AF.Sign, col(M65))
            else:
                ts(ch("tf"), ch("df"), 6.0, ALU.is_gt, 2.0, ALU.mult)
        cuts = OPT["cuts"]
        for a, b in zip(cuts, cuts[1:]):
            mm([(ps(bf, k, 384, 16, (a, b)), u("df", 16 * a + k, 16 * b, 16), u("WD", 0, 24), False) for k in range(16)], last=False)
            mm([(ps(bf, k, 384, 16, (a, b)), u("tf", 16 * a + k, 16 * b, 16), ap("WT"), False) for k in range(16)], last=b == 128)
        scan(u("RM"), ap("dres"), ps(bf, 0, 384), ALU.add, ALU.min)
        r15 = u("RM", 15, 384, 16)
        scan(u("sb"), ps(bf, 408, 432), r15, ALU.add, ALU.min)
        scan(u("sa"), ps(bf, 384, 408), r15, ALU.add, ALU.min)
        if OPT["b"] == "P":
            spread(u("gmb"), u("sb"), "l8s")
            spread(u("gma"), u("sa"), "l8s")
            child_list(u("gmb"), ps(bf, 432, 440))
        else:
            ts(u("bt"), u("sb", 2, 24, 3), 1.5 * 2.0 ** 28, ALU.add, 1.5 * 2.0 ** 28, ALU.subtract)
            tt(u("br", 0, 8), u("sb", 2, 24, 3), u("bt"), ALU.subtract)
            spread(u("gmc"), u("br", 0, 8))
            spread(u("gma"), u("sa"), "l8s")
            mm(grp(ps(bf, 432, 440), [(I_, ap("c16")), (u("gmc"), ap("Rbb"))]))
        mm(grp(ps(ba, 440, 448), [(ap("I4"), u("m1", 0, 8)), (I_, u("m1", 8, 16)), (u("gma"), ap("Rbs"))]))
        cp(u("lb"), ps(bf, 432, 440))
        ts(u(SY, 128, 136), ps(ba, 440, 448), 0.0, ALU.is_lt)
        cp(u(SY, 0, 128), ind(u("y"), u("lb")), OPT["yb"][c])
        send([u(SY, 0, 136)], [(1, u(LY, 0, 136), "ay%d_%d" % (t, c))], "ly%d_%d" % (t, c), 2500)
        child_list(u("gma"), ps(k0, 0, 8))
        cp(u("la"), ps(k0, 0, 8))
        cp(u("ya"), ind(u("y"), u("la")), OPT["ya"][c])
        both(k0, u("ya"), ap(S, 256 * t, 256 * t + 256), OPT["sa"][c])
        if not end:
            act(u("gsb", 0, 8), u(SY, 128, 136), AF.Identity, acc=u("gs", 0, 1))
            gs = u("gs", 0, 1)
            mm(grp(ps(ba, 0, 1), [(row("ONE"), row("CS", 9, 10)), (ap("B64n"), gs), (row("ONE"), row("CS", 8, 9)), (row("NEG"), row("CS", 8, 9)), (ap("B64"), gs)]))
            act(u("ncol", 0, 1), ps(ba, 0, 1), AF.Identity, col(K37))
        else:
            dma("S", "om%d" % c, [(T.ym[4 * c:4 * c + 4, :], T[S][15:64:16, 2048:4096])], [ap(S, 2048, 4096)], [], 2500)
            dma("S", "osa%d" % c, [(T.ys[half(c), 0:1792], T[S][0:64, 0:1792])], [ap(S, 0, 1792)], [], 3500)
            counters(u, V, u(SY, 128, 136))
            tt(u("Pb"), u("Pc"), ap("PC"), ALU.subtract)
            YO = "yo%d" % c
            for r in range(2):
                b = (ba, bf)[r]
                mm([(ps(b, a, 384, 16, (0, 4)), ap("W", 16 + 64 * r + a, 80 + 64 * r, 16), u("Pb", 0, 24), True) for a in range(16)])
                cp((YO, r, r + 1) + view(YO, T[YO][0:4, :, 128 * r:128 * r + 128], 384)[3:], ps(b, 0, 384, 1, (0, 4)), "VA"[r])
            dma("S", "op%d" % c, [(T.yp[4 * c:4 * c + 4, :], T[YO][0:4, :, :])], [(YO, 0, 2) + view(YO, None, 768)[3:]], [], 2200)
        if not end:
            both(k1, u(LY, 0, 128), ap(S, 256 * (RO + t), 256 * (RO + t) + 256), OPT["sb"][c])
        else:
            dma("SA"[c], "osb%d" % c, [(T.ys[half(c), 1792 + 128 * r:1920 + 128 * r], u(LY, 0, 128, 1, (64 * r, 64 * r + 64))[3]) for r in range(2)], [u(LY, 0, 136)], [], 2200)

    for t in range(RO):
        now[0] = t
        for c in range(2):
            first = len(ops)
            step(t, c)
            for o in ops[first:]:
                o["turn"] = 2 * t + c
    return ops, Q


def place(eng, cost, edges, key, seq, first):
    key = list(key)
    for i in seq:
        for j, w in edges[i]:
            if key[j] >= key[i]:
                key[i] = key[j] + 0.001
    start = list(first)
    busy = {e: ([], []) for e in "VAPGS"}
    for i in sorted(seq, key=lambda i: key[i]):
        t = start[i]
        for j, w in edges[i]:
            if start[j] + w > t:
                t = start[j] + w
        if eng[i] is not None:
            c = cost[i]
            s, f = busy[eng[i]]
            m = lo = len(s)
            while lo and f[lo - 1] > t:
                lo -= 1
            while lo < m and s[lo] < t + c:
                if f[lo] > t:
                    t = f[lo]
                lo += 1
            s.insert(lo, t)
            f.insert(lo, t + c)
        start[i] = t
    return start


def schedule(ops, seed=0):
    n = len(ops)
    fw = [[] for _ in range(n)]
    bw = [[] for _ in range(n)]
    for i, o in enumerate(ops):
        for j, need in o["deps"].items():
            p = ops[j]
            gap = p["lat"] + (SLAT if p["eng"] == o["eng"] else XLAT) if need or o["kind"] == "r" else 0.0
            fw[i].append((j, p["cost"] + gap))
            bw[j].append((i, o["cost"] + gap))
    tail = [o["lat"] for o in ops]
    eng = [o["eng"] for o in ops]
    cost = [o["cost"] for o in ops]
    up = list(range(n))
    twin = {o["cls"]: i for i, o in enumerate(ops)}
    z = [seed * 7919 + 13]

    def draw():
        z[0] = (z[0] * 1103515245 + 12345) % 2147483648
        return z[0] / 2147483648.0

    def passes(key):
        st = place(eng, cost, fw, key, up, [0.0] * n)
        back = place(eng, cost, bw, [-(st[i] + cost[i] + tail[i]) for i in up], up[::-1], tail)
        s2 = place(eng, cost, fw, [-(back[i] + cost[i]) for i in up], up, [0.0] * n)
        return min((max(s[i] + cost[i] + tail[i] for i in up), s) for s in (st, s2))

    best = cur = passes([float(i) for i in up])
    for attempt in range(OPT["tries"]):
        key = list(cur[1])
        if attempt % 10 == 0:
            a, b = int(draw() * RO), int(draw() * RO)
            pairs = [(i, twin[(a,) + ops[i]["cls"][1:]]) for i in up if ops[i]["cls"][0] == b and (a,) + ops[i]["cls"][1:] in twin]
            shift = sorted(key[i] - key[j] for i, j in pairs)[len(pairs) // 2]
            for i, j in pairs:
                key[i] = cur[1][j] + shift
        else:
            w0 = cur[0] * draw() - 0.5 * OPT["window"]
            amp = OPT["noise"] * draw() ** 2
            for i in up:
                if w0 <= key[i] < w0 + OPT["window"]:
                    key[i] += amp * (draw() - 0.5)
        new = passes(key)
        if new[0] <= cur[0] + OPT["slack"] * (1 - attempt / OPT["tries"]) * draw():
            cur = new
        if new[0] < best[0]:
            best = new
    st = best[1]
    order = {e: [i for s, i in sorted((st[i], i) for i in range(n) if ops[i]["eng"] == e)] for e in "VAPGS"}
    return order, st, [st[i] + ops[i]["cost"] + tail[i] for i in range(n)]


KEPT = {}


def rank_program(g, core, T, topo):
    if T.rank_of(core) is None:
        return
    ops, Q = build(g, core, T, topo)
    if "order" not in KEPT:
        KEPT["order"], KEPT["start"] = schedule(ops, OPT["seed"])[:2]
    order = KEPT["order"]
    tick = {}
    total = {}
    for e in "VAPG":
        k = 0
        for i in order[e]:
            if ops[i]["kind"] == "c":
                k += 1
                tick[i] = ("c" + e, k)
        total["c" + e] = k
    for i, o in enumerate(ops):
        if o["kind"] != "c":
            tick[i] = (o["sem"], o["cnt"])
            total[o["sem"]] = o["cnt"]
    start = KEPT["start"]
    state = {e: {} for e in "SPAVG"}
    known, waits = {}, {}
    for s0, i in sorted((start[i], i) for i in range(len(ops))):
        o = ops[i]
        seen = state.get(o["eng"], {})
        waits[i] = []
        for s1, j in sorted(((start[j], j) for j, w in o["deps"].items() if w), reverse=True):
            s, v = tick[j]
            if seen.get(s, 0) < v:
                waits[i].append((s, v))
                for s2, v2 in list(known[j].items()) + [(s, v)]:
                    seen[s2] = max(seen.get(s2, 0), v2)
        known[i] = dict(seen) if o["eng"] is not None else {}
    for e in "SPAVG":
        seen = state[e]
        for i in order[e]:
            o = ops[i]
            for s, v in waits[i]:
                Q[e].wait_ge(T.sem[s], v)
            r = None
            for f in o["fns"]:
                r = f()
                if o["kind"] == "d":
                    r.then_inc(T.sem[o["sem"]], 16)
            if o["kind"] == "c":
                r.then_inc(T.sem["c" + e], 1)
        if e == "G":
            for s, v in total.items():
                if seen.get(s, 0) < v:
                    g.wait_ge(T.sem[s], v)
